import numpy as np, ml_dtypes
CORES = [66,74,82,90,194,202,210,218]
N = 8
BF = ml_dtypes.bfloat16
W, A, L, S, Q, C = 2048, 4, 3, 5, 96, 32
def place(x, wv, kv):
    u = np.sum(wv * x, axis=2) & (W - 1)
    return (((u * u) >> 5)[..., None] + kv[:, :, None, :] * u[..., None]) & (W - 1)
def search(X, q, wv, kv):
    n, m = q.shape[0], q.shape[3]
    pl = place(q, wv, kv); ok = np.ones(pl.shape, bool); line = [pl]; levels, dist = [], []
    for l in range(L):
        k = A ** (l + 1)
        occ = np.take_along_axis(X, pl.reshape(n, 8, 1, m * k), 3)
        d = np.sum(np.abs(occ.reshape(n, 8, 16, m, k) - q[..., None]), axis=2)
        if l == 0: hit = np.any(d == 0, axis=3)
        levels.append(pl); dist.append(np.where(ok, d, -1))
        if l < L - 1:
            good = ok & (occ[:, :, 0].reshape(n, 8, m, k) != 512)
            pl = place(occ, wv, kv).reshape(n, 8, m, k * A)
            line = [np.repeat(a, A, axis=3) for a in line]
            ok = np.repeat(good, A, axis=3)
            for a in line: ok = ok & (pl != a)
            line.append(pl)
    D = np.concatenate(dist, axis=3); v = D.shape[3] - 1 - np.argmax(D[..., ::-1], axis=3)
    path = np.full((n, 8, m, L), -1, np.int64); depth = np.zeros((n, 8, m), np.int64); base = 0
    for l in range(L):
        k = A ** (l + 1); here = (v >= base) & (v < base + k); j = np.clip(v - base, 0, k - 1)
        for h in range(l + 1):
            t = np.take_along_axis(levels[h], (j // A ** (l - h))[..., None], 3)[..., 0]
            path[..., h] = np.where(here, t, path[..., h])
        depth = np.where(here, l, depth); base += k
    return (q[:, :, 0] != 512) & ~hit, depth, path
def step(X, q, wv, kv):
    n, m = q.shape[0], q.shape[3]
    live, depth, path = search(X, q, wv, kv)
    meet = np.zeros((n, 8, m, m), bool)
    for a in range(L):
        for b in range(L):
            meet |= (path[..., a][..., :, None] == path[..., b][..., None, :]) & (path[..., a] >= 0)[..., None]
    go = live & ~np.any(meet & live[:, :, None, :] & np.tri(m, m, -1, dtype=bool), axis=3)
    old = [np.take_along_axis(X, np.maximum(path[..., l], 0)[:, :, None, :], 3) for l in range(L)]
    Y = X.copy(); val = q; vic = old[0]
    for l in range(L):
        r, g, i = np.nonzero(go & (depth >= l))
        Y[r, g, :, path[r, g, i, l]] = val[r, g, :, i]; val = old[l]
        vic = np.where((depth >= l)[:, :, None, :], old[l], vic)
    gone = go & (vic[:, :, 0] != 512); slot = np.add.accumulate(gone.astype(np.int64), axis=2) - 1
    out = np.full((n, 8, 16, C), 512, np.int32); r, g, i = np.nonzero(gone & (slot < C))
    out[r, g, :, slot[r, g, i]] = vic[r, g, :, i]
    return Y, out
def records(rng, k): return rng.integers(0, 256, (N, 8, 16, k)).astype(np.int32)
def hashes(rng): return rng.integers(1, 256, (N, 8, 16, 1)).astype(np.int32), 2 * rng.integers(0, 1024, (N, 8, A)) + 1
def fill(rng, rec, wv, kv, full, bare):
    pl = place(rec, wv, kv); k = rec.shape[3]; X = np.full((N, 8, 16, W), 512, np.int32)
    for r in range(N):
        for g in range(8):
            own = np.full(W, -1); free = np.arange(k)
            for a in range(A):
                p = pl[r, g, free, a]; e = own[p] < 0; own[p[e]] = free[e]; free = free[own[p] != free]
            if full[r, g]: own = np.where(own < 0, rng.integers(0, k, W), own)
            own = np.where(rng.random(W) < bare[r, g], -1, own)
            X[r, g] = np.where(own >= 0, rec[r, g][:, own], 512)
    return X
def ask(rng, X, fresh):
    c = rng.integers(0, W, (N, 8, 1, S * Q)); v = np.take_along_axis(X, c, 3).reshape(N, 8, 16, S, Q)
    q = np.where((rng.random((N, 8, 1, S, Q)) < 0.2) & (v[:, :, :1] != 512), v, fresh.reshape(N, 8, 16, S, Q))
    j = np.where(rng.random((N, 8, 1, S, Q)) < 0.06, rng.integers(0, Q, (N, 8, 1, S, Q)), np.arange(Q))
    return np.take_along_axis(q, j, 4)
def pack(X, q, wv, kv):
    return {"x0": X.reshape(N, 128, W).astype(np.float32).astype(BF), "qs": np.ascontiguousarray(q).reshape(N, 128, S * Q).astype(np.float32).astype(BF),
            "wt": wv.reshape(N, 128, 1).astype(np.float32).astype(BF), "kk": np.repeat(kv, 16, axis=1).astype(np.int32)}
def setup_inputs(rng):
    wv, kv = hashes(rng); full = rng.random((N, 8)) < 0.5; bare = rng.choice(np.array([0.0, 0.002, 0.005, 0.02, 0.1]), (N, 8))
    full[:, 0] = True; bare[:, 0] = 0.0; bare[:, 1] = 0.005; bare[:, 2] = 0.02
    X = fill(rng, records(rng, 2 * W), wv, kv, full, bare)
    return pack(X, ask(rng, X, records(rng, S * Q)), wv, kv)
def setup_inputs_room(rng):
    wv, kv = hashes(rng); X = fill(rng, records(rng, 2 * W), wv, kv, np.ones((N, 8), bool), np.zeros((N, 8)))
    q = ask(rng, X, records(rng, S * Q)); pool = records(rng, 2 * Q); live, depth, path = search(X, pool, wv, kv)
    home = np.any(place(X, wv, kv) == np.arange(W)[:, None], axis=3)
    for r in range(N):
        for g in range(8):
            n = int(rng.choice(np.array([0, 1, C - 1, C, C + 1, Q])))
            if r == 0: n = (C, C + 1, Q, C - 1, 1, 0, C, Q)[g]
            used, take = set(), []
            for i in rng.permutation(2 * Q):
                p = set(path[r, g, i].tolist()) - {-1}
                if len(take) < n and live[r, g, i] and not (p & used):
                    take.append(int(i)); used |= p
            stay = rng.choice(np.nonzero(home[r, g])[0], Q - len(take))
            q[r, g, :, 0] = np.concatenate([pool[r, g][:, np.array(take, np.int64)], X[r, g][:, stay]], axis=1)[:, rng.permutation(Q)]
    return pack(X, q, wv, kv)
def setup_inputs_alike(rng):
    wv, kv = hashes(rng); wv[:] = wv[:1].copy(); kv[:, 2] = kv[:, 2, :1]; kv[:, 3, 1:] = kv[:, 3, 1:2]; kv[:] = kv[:1].copy()
    rec = (255 * rng.integers(0, 2, (N, 8, 16, 2 * W))).astype(np.int32); fresh = (255 * rng.integers(0, 2, (N, 8, 16, S * Q))).astype(np.int32)
    few = rng.integers(0, 256, (16, 24)).astype(np.int32)
    for g in (1, 5):
        for r in range(N):
            rec[r, g] = few[:, rng.integers(0, 24, 2 * W)]
            fresh[r, g] = np.where(rng.random(S * Q) < 0.5, few[:, rng.integers(0, 24, S * Q)], rng.integers(0, 256, (16, S * Q)))
    rec[:, 6, :, ::4] = 0
    rec[:, 7] = rng.integers(0, 3, (N, 16, 2 * W))
    full = rng.random((N, 8)) < 0.7; full[:, 1] = True; bare = rng.choice(np.array([0.0, 0.005, 0.02]), (N, 8))
    X = fill(rng, rec, wv, kv, full, bare); q = ask(rng, X, fresh)
    q[:, 4, :, 1] = q[:, 4, :, 1, :1]; q[:, 6, :, 2, ::5] = 0; q[:, 6, :, 0, Q - 1] = 255
    return pack(X, q, wv, kv)
def setup_inputs_hollow(rng):
    wv, kv = hashes(rng); bare = rng.choice(np.array([0.3, 0.6, 0.9, 0.97, 1.0]), (N, 8)); bare[0, 0] = 1.0; bare[1, 1] = 0.6
    full = rng.random((N, 8)) < 0.5; bare[:, 6:] = 0.0; full[:, 7] = True
    X = fill(rng, records(rng, 2 * W), wv, kv, full, bare); q = ask(rng, X, records(rng, S * Q))
    q[:, :, :, 2] = q[:, :, :, 1][..., rng.permutation(Q)]
    return pack(X, q, wv, kv)
def setup_inputs_edges(rng):
    wv, kv = hashes(rng); wv[:, 0] = 255; kv[:, :2] = rng.choice(np.array([1, 2046, 2047]), (N, 2, A)); kv[:, :2, 0] = 2047
    wv[:, 6, 0] |= 1; kv[:, 6] = kv[:, 6, :1].copy()
    full = rng.random((N, 8)) < 0.5; full[:, 0] = True; full[:, 4] = False; full[::2, 5] = True; full[1::2, 5] = False; full[:, 6] = False
    bare = np.zeros((N, 8)); bare[:, 3] = 0.3; bare[:, 7] = 0.1
    rec, fresh = records(rng, 2 * W), records(rng, S * Q)
    for v in (rec, fresh):
        k = v.shape[3]; v[:, 0] = np.where(rng.random((N, 1, k)) < 0.5, rng.integers(200, 256, (N, 16, k)), v[:, 0])
        v[::2, 5] = v[::2, 5] >> 2
    X = fill(rng, rec, wv, kv, full, bare); q = ask(rng, X, fresh)
    q[:, 0, :, 0, 0] = 255
    q[:, 1:3, :, 0, :8] = records(rng, 8)[:, 1:3]
    t = q[:, :, :, 0, :8].copy(); pl = place(t, wv, kv)[..., 0]; i = rng.integers(0, 16, (N, 8, 1, 8))
    near = np.where(np.arange(16)[:, None] == i, t + np.where(t < 255, 1, -1), t)
    for r in range(N):
        for g in (1, 2):
            for j in range(7, -1, -1): X[r, g, :, pl[r, g, j]] = near[r, g, :, j]
    X[:, 3] = np.where(rng.random((N, 1, W)) < 0.02, 0, X[:, 3]); X[:, 3, :, 0] = 512
    q[:, 3, :, 0, 0] = 0; q[:, 3, :, 1, 0] = 255
    X[:, 7, :, 0] = records(rng, 1)[:, 7, :, 0]; q[:, 7, :, 0, 0] = 0; pe = place(X[..., :1], wv, kv)[:, 7, 0]
    for r in range(N): X[r, 7, :, pe[r]] = 512
    for r in range(N):
        g = 4 + r % 2; c = rng.choice(np.nonzero(X[r, g, 0] != 512)[0], Q); q[r, g, :, 0] = X[r, g][:, c]
    q[1::2, 4, :, 0, 0] = records(rng, 1)[1::2, 4, :, 0]; q[1::2, 4, :, 1] = q[1::2, 4, :, 0, :1]
    rr = np.arange(8) % N; m = 256; pool = rng.integers(128, 256, (1, 8, 16, m)).astype(np.int32)
    live, depth, path = search(X[rr, 5][None], pool, wv[rr, 5][None], kv[rr, 5][None])
    for r in range(1, N, 2):
        p = path[0, r]; same = np.sum((p[:, None, :, None] == p[None, :, None, :]) & (p >= 0)[:, None, :, None], axis=(2, 3))
        fit = (same == 1) & live[0, r][:, None] & (live[0, r] & (depth[0, r] == L - 1))[None, :]
        a, b = divmod(int(np.argmax(fit)), m); z = pool[0, r][:, b:b + 1]
        q[r, 5, :, 1] = z; q[r, 5, :, 1, 0] = pool[0, r, :, a]
        X[r - 1, 5] = np.where(rng.random(W) < 0.125, z, X[r - 1, 5])
    mine = place(rec, wv, kv)[:, 6, :, 0]
    for r in range(1, N, 2):
        e = r - 1; p = mine[e]; i = np.nonzero(np.any(X[e, 6][:, p] != rec[e, 6], axis=0))[0]
        i = i[np.unique(p[i], return_index=True)[1]]
        t = place(X[e, 6][:, p[i]][None, None], wv[r:r + 1, 6:7], kv[r:r + 1, 6:7])[0, 0, :, 0]
        j = rng.permutation(np.unique(t, return_index=True)[1]); last = j[X[r, 6, 0, t[j]] != 512][:1]
        j = j[j != last[0]][:Q - 1]; j = np.concatenate([j[:C - 1], last, j[C - 1:]])
        q[e, 6] = rec[e, 6][:, i[j]][:, None, :]
        z = X[r, 6, :, int(t[last[0]])].copy()
        X[r, 6, :, t[j[:C]]] = 512
        c = rng.choice(np.nonzero(X[r, 6, 0] != 512)[0], S * Q); q[r, 6] = X[r, 6][:, c].reshape(16, S, Q); q[r, 6, :, 1, 0] = z
    return pack(X, q, wv, kv)
def setup_inputs_spread(rng):
    def uneven(k):
        v = np.minimum((np.exp2(2 + 6 * rng.random((N, 8, 1, k))) * rng.random((N, 8, 16, k))).astype(np.int32), 255)
        return np.where(rng.random((N, 8, 16, k)) < 0.02, 255, v).astype(np.int32)
    wv = np.minimum(np.exp2(8 * rng.random((N, 8, 16, 1))).astype(np.int32), 255); kv = np.minimum(np.exp2(11 * rng.random((N, 8, A))).astype(np.int64), 2047)
    X = fill(rng, uneven(2 * W), wv, kv, rng.random((N, 8)) < 0.6, rng.choice(np.array([0.0, 0.003, 0.01]), (N, 8)))
    return pack(X, ask(rng, X, uneven(S * Q)), wv, kv)
def check_inputs(d):
    bad = []
    v = np.asarray(d["x0"]).astype(np.float32); e = v == 512
    if not np.all(e | ((v >= 0) & (v <= 255) & (np.floor(v) == v))): bad.append("range of x0")
    e = e.reshape(N, 8, 16, W)
    if np.any(np.any(e, axis=2) != np.all(e, axis=2)): bad.append("empty records of x0")
    for k, lo in (("qs", 0), ("wt", 1)):
        v = np.asarray(d[k]).astype(np.float32)
        if not np.all((v >= lo) & (v <= 255) & (np.floor(v) == v)): bad.append("range of " + k)
    k = np.asarray(d["kk"])
    if np.min(k) < 1 or np.max(k) > 2047: bad.append("range of kk")
    k = k.reshape(N, 8, 16, A)
    if np.any(k != k[:, :, :1]): bad.append("rows of kk")
    return bad
def reference(x0, qs, wt, kk):
    X = x0.astype(np.float32).astype(np.int32).reshape(N, 8, 16, W); q = qs.astype(np.float32).astype(np.int32).reshape(N, 8, 16, S, Q)
    wv = wt.astype(np.float32).astype(np.int32).reshape(N, 8, 16, 1); kv = kk.reshape(N, 8, 16, A)[:, :, 0].astype(np.int64)
    come = np.full((N, 8, 16, C), 512, np.int32)
    for s in range(S):
        X, out = step(X, np.concatenate([q[:, :, :, s], come], axis=3), wv, kv)
        come = np.roll(out, 1, axis=0)
    return {"y": X.reshape(N, 128, W).astype(np.float32).astype(BF)}

@@ -1,0 +1,521 @@
+from concourse.mybir import AluOpType, AxisListType, ActivationFunctionType
+
+A = AluOpType
+ACT = ActivationFunctionType
+X = AxisListType.X
+S = 5
+E11 = 2048.0
+OFFS = -8388608.0
+PEN = -33554432.0
+BASE = (96, 384, 1536)
+SCAL = 4
+ORDER = "lc rq g3 k3 x1 d0 k1 r2 x3 fq fe d1 k2 ph d2 r3 s1 m1 d6 fa s2 d4 s6 d5 p12 m3 s0 s4 d7 m6 m2 m0 m4 fp lv fg pp s5 s7 m5 m7 r12 pg"
+
+SCRATCH = {}
+for _t, _l in (
+        ("bfloat16", "XB:2432 QS:480 WTS:1 MT:128 MT2:128 ML:128 IO16:384 EK:2048 WR:2048 WBD:128 ONE:512 IB:128 NIB:128 IPEN:128"
+                     " IOFF:128 BDB:128 LTB:128 MKB:64 OCC1:512 OCC2:2048 OCC3:2048 AB1:512 AB2:2048 DF:8192 FE1:32 DEAD:8 FQ2:128"
+                     " FA:128 FB:128 FP:512 FG:512 OLD:512 ND:8 SB0:256 SB1:256 SB2:256 SB3:256 ARR1:32 ARR2:32 ARR3:32 ARR4:32"),
+        ("float32", "KF:4 KG:4 KH:4 K32:4 MASK:384 PMF:1 LN0:8 LN:8 TRC:24 TRD:24 TL:8 IX3F:512 RS:32 RQ:2 RE:32 RF:2 LV:8 LIVE:8 NEQ:8"
+                    " M12:8 M3:8 MD:8 ML12:8 CFM:8 CFX:8 CL:8 GO:8 W1:24 W2:24 W3:24 NE:8 D2:8 D3:8"),
+        ("float16", "IH:128 BDH:128 NTL:8 IX3:512 SELM:384 PH:160"),
+        ("int32", "KKI:4 PIN:1 PMI:1 BH:8 PLW:2048 P1A:120 UI:128 U:128 Z:512 Y:512 MI:8 PG:8 PO:24"),
+        ("uint16", "OF:672 L1U:120 POU:24 XL:24 DLU:24 SLU:8")):
+    for _w in _l.split():
+        SCRATCH[_w.split(":")[0]] = ("sbuf", [128, int(_w.split(":")[1])], _t)
+for _n, _s, _t in (("QR", [128, 30, 1024], "bfloat16"), ("QRR", [128, 2, 512], "bfloat16"), ("IX12F", [128, 8, 20], "float32"),
+                   ("IX12", [128, 8, 20], "float16"), ("NH", [128, 8, 4], "float32"), ("N1", [128, 8, 2], "float32"),
+                   ("OTHH", [128, 3, 128], "float16"), ("EQ", [128, 72, 128], "bfloat16"), ("JK", [128, 36, 112], "bfloat16")):
+    SCRATCH[_n] = ("sbuf", _s, _t)
+BANKS = ("SD", "SR", "K12", "K3", "DA", "DB", "OT", "OW")
+for _n, _s in (("SD", [128, 128]), ("SR", [128, 128]), ("K12", [128, 8, 20]), ("K3", [128, 512]), ("DA", [128, 512]), ("DB", [128, 512]),
+               ("OT", [128, 384]), ("OW", [128, 64])):
+    SCRATCH[_n] = ("psum", _s, "float32")
+SEMAPHORES = ["cv", "cs", "cp", "cg", "sent"] + ["arr%d" % (i + 1) for i in range(S - 1)] + ["d%d" % i for i in range(40)]
+
+
+def make_queue(g, T):
+    eng = {"v": g.vector, "s": g.scalar, "p": g.tensor, "g": g, "y": g.sync}
+    count = {"cv": 0, "cs": 0, "cp": 0, "cg": 0}
+    known = {q: {} for q in eng}
+    snap, writer, readers, touch = {}, {}, {}, {}
+    dmas = [0]
+
+    def before(q, rd, wr):
+        evs = []
+        for t in rd:
+            if t in BANKS:
+                evs += [e for e in touch.get(t, {}).values() if e[2] != q]
+            elif t in writer:
+                evs.append(writer[t])
+        for t in wr:
+            if t in BANKS:
+                evs += [e for e in touch.get(t, {}).values() if e[2] != q]
+            elif readers.get(t):
+                evs += list(readers[t].values()) + ([writer[t]] if t in writer else [])
+            elif t in writer and writer[t][2] != q:
+                evs.append(writer[t])
+        best = {}
+        for sem, val, _ in evs:
+            best[sem] = max(best.get(sem, 0), val)
+        for sem in sorted(best):
+            val = best[sem]
+            if known[q].get(sem, 0) < val:
+                eng[q].wait_ge(T.sem[sem], val)
+                for k, n in snap.get((sem, val), {}).items():
+                    known[q][k] = max(known[q].get(k, 0), n)
+                known[q][sem] = val
+
+    def after(ev, rd, wr):
+        for t in rd:
+            if t in BANKS:
+                touch.setdefault(t, {})[ev[2]] = ev
+            else:
+                readers.setdefault(t, {})[(ev[2], ev[0])] = ev
+        for t in wr:
+            if t in BANKS:
+                touch.setdefault(t, {})[ev[2]] = ev
+            else:
+                writer[t] = ev
+                readers[t] = {}
+
+    def op(q, rd, wr, call):
+        before(q, rd, wr)
+        sem = "c" + q
+        count[sem] += 1
+        call(eng[q]).then_inc(T.sem[sem], 1)
+        snap[(sem, count[sem])] = dict(known[q])
+        after((sem, count[sem], q), rd, wr)
+
+    def dma(q, rd, wr, out, in_):
+        before(q, rd, wr)
+        sem = "d%d" % dmas[0]
+        dmas[0] += 1
+        eng[q].dma_start(out, in_).then_inc(T.sem[sem], 16)
+        snap[(sem, 16)] = dict(known[q])
+        after((sem, 16, "dma"), rd, wr)
+
+    def outside(sem, val, wr):
+        after((sem, val, "far"), [], wr)
+
+    def finish():
+        for sem in ("cv", "cs", "cp", "cg"):
+            if known["g"].get(sem, 0) < count[sem]:
+                g.wait_ge(T.sem[sem], count[sem])
+        for i in range(dmas[0]):
+            g.wait_ge(T.sem["d%d" % i], 16)
+    return op, dma, outside, before, finish
+
+
+def rank_program(g, core, T, topo):
+    rank = T.rank_of(core)
+    if rank is None:
+        return
+    op, dma, outside, before, finish = make_queue(g, T)
+    nxt = T.cores[(rank + 1) % len(T.cores)]
+    rid, pid = topo.addr(nxt, core)
+    wire = topo.mask(core, nxt)
+    nwire = len(topo.engines(core, nxt))
+    nland = len(topo.engines(T.cores[(rank - 1) % len(T.cores)], core))
+
+    dma("y", [], ["QS"], T.QS[:], T.qs[:])
+    dma("s", [], ["WTS"], T.WTS[:], T.wt[:])
+    dma("s", [], ["KKI"], T.KKI[:], T.kk[:])
+    dma("y", [], ["QR0"], T.QR[:, 0:6, 0:16], T.qs[:, 0:96])
+    dma("s", [], ["XBx"], T.XB[:, 256:1280], T.x0[:, 0:1024])
+    dma("y", [], ["XBx2"], T.XB[:, 1280:2304], T.x0[:, 1024:2048])
+    for s in range(1, S):
+        dma("y", [], ["QR%d" % s], T.QR[:, 6 * s:6 * s + 6, 0:16], T.qs[:, 96 * s:96 * s + 96])
+    dma("y", [], ["XBqD"], T.XB[:, 0:96], T.qs[:, 0:96])
+    dma("y", [], ["OLDqD"], T.OLD[:, 384:480], T.qs[:, 0:96])
+
+    def iota(tok, out, pattern, base, cm, small=True):
+        if small:
+            op("g", [], [tok], lambda e: e.iota(out, pattern, base, cm, allow_small_or_imprecise_dtypes=True))
+        else:
+            op("g", [], [tok], lambda e: e.iota(out, pattern, base, cm))
+
+    def sel(rd, tok, out, in_, pattern, cmp, fill, base, cm):
+        op("g", [rd], [tok], lambda e: e.affine_select(out, in_, pattern, cmp, fill, base, cm))
+
+    def vset(tok, out, c):
+        op("v", [], [tok], lambda e: e.memset(out, c))
+
+    def ts(rd, wr, out, in0, s1, s2, op0, op1=None):
+        if op1 is None:
+            op("v", rd, wr, lambda e: e.tensor_scalar(out, in0, s1, None, op0=op0))
+        else:
+            op("v", rd, wr, lambda e: e.tensor_scalar(out, in0, s1, s2, op0=op0, op1=op1))
+
+    def tt(rd, wr, out, a, b, o):
+        op("v", rd, wr, lambda e: e.tensor_tensor(out, a, b, o))
+
+    def cp(rd, wr, out, a):
+        op("v", rd, wr, lambda e: e.tensor_copy(out, a))
+
+    def red(rd, wr, out, a, o):
+        op("v", rd, wr, lambda e: e.tensor_reduce(out, a, X, o))
+
+    def act(rd, wr, out, a, func):
+        op("s", rd, wr, lambda e: e.activation(out, a, func))
+
+    def mm(rd, bank, out, lhsT, rhs, start, stop):
+        op("p", rd, [bank], lambda e: e.matmul(out, lhsT, rhs, start, stop))
+
+    iota("MT", T.MT[:], [[0, 8], [1, 16]], 0, 0)
+    sel("MT", "MT2", T.MT2[:], T.MT[:], [[-16, 8], [0, 16]], A.is_ge, -1.0, 0, 1)
+    sel("MT2", "ML", T.ML[:], T.MT2[:], [[16, 8], [0, 16]], A.is_ge, -1.0, 15, -1)
+    vset("ONE", T.ONE[:], 1.0)
+    sel("ONE", "IB", T.IB[:], T.ONE[:, 0:128], [[-1, 128]], A.is_equal, 0.0, 0, 1)
+    iota("PIN", T.PIN[:], [[0, 1]], 0, 1, False)
+    iota("IO16", T.IO16[:], [[0, 24], [1, 16]], 0, 0)
+    iota("LN0", T.LN0[:], [[16, 8]], 0, 0)
+    iota("BH", T.BH[:], [[1, 8]], 8, 0, False)
+    iota("IX12F", T.IX12F[:, :, 0:4], [[4, 8], [1, 4]], BASE[0], 0)
+    iota("IX12F", T.IX12F[:, :, 4:20], [[16, 8], [1, 16]], BASE[1], 0)
+    iota("IX3F", T.IX3F[:], [[1, 512]], BASE[2], 0)
+    op("v", [], ["XBq", "XBt"], lambda e: e.memset(T.XB[:, 96:256], 0.0))
+    vset("XBt2", T.XB[:, 2304:2432], 0.0)
+    vset("PLW0", T.PLW[:], -256)
+    vset("NH", T.NH[:], 0.0)
+    vset("M12", T.M12[:], OFFS)
+    vset("M3", T.M3[:], OFFS)
+    vset("NEQ", T.NEQ[:], 1.0)
+    for r in range(16):
+        ts(["ML", "WTS"], ["WR"], T.WR[:, 128 * r:128 * r + 128], T.ML[:], float(r), T.WTS[:, 0:1], A.is_equal, A.mult)
+    cp(["KKI"], ["KF"], T.KF[:], T.KKI[:])
+    ts(["KF"], ["KG"], T.KG[:], T.KF[:], 1024.0, -2048.0, A.is_gt, A.mult)
+    tt(["KF", "KG"], ["KH"], T.KH[:], T.KF[:], T.KG[:], A.add)
+    ts(["KH"], ["K32"], T.K32[:], T.KH[:], 32.0, None, A.mult)
+
+    def places(rd, src, n, dst, dtok):
+        cp(rd, ["UI"], T.UI[:, 0:n], src)
+        ts(["UI"], ["U"], T.U[:, 0:n], T.UI[:, 0:n], 2047, None, A.bitwise_and)
+        for a in range(4):
+            ts(["U", "K32"], ["Z%d" % a], T.Z[:, a * n:a * n + n], T.U[:, 0:n], T.K32[:, a:a + 1], None, A.add)
+        for a in range(4):
+            tt(["Z%d" % a, "U"], ["Y"], T.Y[:, a:4 * n:4], T.Z[:, a * n:a * n + n], T.U[:, 0:n], A.mult)
+        ts(["Y"], [dtok], dst, T.Y[:, 0:4 * n], 5, 2047, A.arith_shift_right, A.bitwise_and)
+
+    def wrapsum(mat, rd, bank, out, rhs, start, stop):
+        for r in range(16):
+            mm([mat] + rd, bank, out, T[mat][:, 128 * r:128 * r + 128], rhs(r), start and r == 0, stop and r == 15)
+
+    wrapsum("WR", ["QS"], "SD", T.SD[:, 0:30], lambda r: T.QS[:, r:480:16], True, True)
+    places(["SD"], T.SD[:, 0:30], 30, T.P1A[:], "P1A")
+    cp(["P1A"], ["L1U"], T.L1U[:], T.P1A[:])
+    w = 16
+    while w < 512:
+        act(["QR0"], ["QR0"], T.QR[:, 0:6, w:2 * w], T.QR[:, 0:6, 0:w], ACT.Copy)
+        w *= 2
+    dma("y", ["QR0"], ["QX0"], T.QR[:, 0:6, 512:1024], T.QR[:, 0:6, 0:512])
+    XR = ["XBx", "XBx2"]
+
+    def constants():
+        for r in range(16):
+            ts(["ML"], ["EK"], T.EK[:, 128 * r:128 * r + 128], T.ML[:], float(r), E11, A.is_equal, A.mult)
+        ts(["IB"], ["NIB"], T.NIB[:], T.IB[:], -1.0, None, A.mult)
+        ts(["IB"], ["IPEN"], T.IPEN[:], T.IB[:], PEN, None, A.mult)
+        ts(["IB"], ["IOFF"], T.IOFF[:], T.IB[:], OFFS, None, A.mult)
+        cp(["IX12F"], ["IX12"], T.IX12[:], T.IX12F[:])
+        cp(["IX3F"], ["IX3"], T.IX3[:], T.IX3F[:])
+        cp(["IB"], ["IH"], T.IH[:], T.IB[:])
+        ts(["ML"], ["BDB"], T.BDB[:], T.ML[:], 0.0, None, A.is_ge)
+        ts(["ML"], ["BDH"], T.BDH[:], T.ML[:], 0.0, None, A.is_ge)
+        ts(["ML", "WTS"], ["WBD"], T.WBD[:], T.ML[:], 0.0, T.WTS[:, 0:1], A.is_ge, A.mult)
+        ts(["PIN"], ["PMI"], T.PMI[:], T.PIN[:], 15, None, A.bitwise_and)
+        cp(["PMI"], ["PMF"], T.PMF[:], T.PMI[:])
+        ts(["LN0", "PMF"], ["LN"], T.LN[:], T.LN0[:], T.PMF[:, 0:1], None, A.add)
+        ts(["LN", "PLW0"], ["PLWA"], T.PLW[:, 24:32], T.LN[:], -256.0, None, A.add)
+        ts(["LN", "PLW0"], ["PLWB"], T.PLW[:, 8:16], T.LN[:], -128.0, None, A.add)
+
+    def gather(q, rd, wr, out, lst):
+        if q == "v":
+            cp(rd + XR, wr, out, T.XB[:, 256:2304].indirect(lst))
+        else:
+            act(rd + XR, wr, out, T.XB[:, 256:2304].indirect(lst), ACT.Copy)
+
+    diffs = [0]
+
+    def diff(rd, rt, occ, reps, n, out, otok):
+        bank = ("DA", "DB")[diffs[0] % 2]
+        diffs[0] += 1
+        ps = T[bank][:, 0:n]
+        mm(["IB"] + rd, bank, ps, T.IB[:], occ, True, False)
+        mm(["NIB", rt], bank, ps, T.NIB[:], reps, False, True)
+        act([bank], [otok], out, ps, ACT.Abs)
+
+    def first(s):
+        gather("s", ["L1U"], ["OCC1Ds"], T.OCC1[:, 0:192], T.L1U[:, 24 * s:24 * s + 12])
+        gather("v", ["L1U"], ["OCC1Dv"], T.OCC1[:, 192:384], T.L1U[:, 24 * s + 12:24 * s + 24])
+        cp(["P1A"], ["PLW1D"], T.PLW[:, 96:120], T.P1A[:, 24 * s:24 * s + 24])
+
+    for s in range(S):
+        arrivals = s > 0
+        send = s + 1 < S
+        H = 8 if arrivals else 6
+        both = ("D", "R") if arrivals else ("D",)
+        at, qt = "ARR%d" % s, "QR%d" % s
+        arr = T[at] if arrivals else None
+        PL1, PL2, PL3 = (["PLW%d%s" % (l, b) for b in both] for l in (1, 2, 3))
+        if arrivals:
+            outside("arr%d" % s, nland, [at])
+            dma("y", [], ["XBqD"], T.XB[:, 0:96], T.qs[:, 96 * s:96 * s + 96])
+            dma("y", [], ["OLDqD"], T.OLD[:, 384:480], T.qs[:, 96 * s:96 * s + 96])
+        else:
+            first(0)
+            constants()
+
+        wrapsum("WR", ["OCC1Ds", "OCC1Dv"], "SD", T.SD[:, 0:24], lambda r: T.OCC1[:, r:384:16], True, True)
+        diff(["OCC1Ds", "OCC1Dv"], qt, T.OCC1[:, 0:384], T.QR[:, 6 * s:6 * s + 6, 0:64], 384, T.AB1[:, 0:384], "AB1D")
+        places(["SD"], T.SD[:, 0:24], 24, T.PLW[:, 384:480], "PLW2D")
+        cp(["PLW2D"], ["OF2D"], T.OF[:, 32:128], T.PLW[:, 384:480])
+        gather("s", ["OF2D"], ["OCC2Ds"], T.OCC2[:, 0:768], T.OF[:, 32:80])
+        gather("v", ["OF2D"], ["OCC2Dv"], T.OCC2[:, 768:1536], T.OF[:, 80:128])
+        wrapsum("WR", ["OCC2Ds", "OCC2Dv"], "SD", T.SD[:, 32:128], lambda r: T.OCC2[:, r:1536:16], True, True)
+        for c in range(3):
+            diff((["OCC2Ds"], ["OCC2Ds", "OCC2Dv"], ["OCC2Dv"])[c], qt, T.OCC2[:, 512 * c:512 * c + 512],
+                 T.QR[:, 6 * s + 2 * c:6 * s + 2 * c + 2, 0:256], 512, T.AB2[:, 512 * c:512 * c + 512], "AB2%d" % c)
+        places(["SD"], T.SD[:, 32:128], 96, T.PLW[:, 1536:1920], "PLW3D")
+        cp(["PLW3D"], ["OF3D"], T.OF[:, 160:544], T.PLW[:, 1536:1920])
+
+        if arrivals:
+            for k in range(2):
+                sel(at, "QRR", T.QRR[:, k, 0:16], arr[:, 16 * k:16 * k + 16], [[0, 16]], A.is_equal, 0.0, 0, 0)
+            w = 16
+            while w < 512:
+                sel("QRR", "QRR", T.QRR[:, :, w:2 * w], T.QRR[:, :, 0:w], [[0, 2], [0, w]], A.is_equal, 0.0, 0, 0)
+                w *= 2
+            dma("y", [at], ["XBqR"], T.XB[:, 96:128], arr[:])
+            dma("y", [at], ["OLDqR"], T.OLD[:, 480:512], arr[:])
+        if send:
+            w, nt, lo = 16, "QR%d" % (s + 1), 6 * (s + 1)
+            while w < 512:
+                sel(nt, nt, T.QR[:, lo:lo + 6, w:2 * w], T.QR[:, lo:lo + 6, 0:w], [[0, 6], [0, w]], A.is_equal, 0.0, 0, 0)
+                w *= 2
+            dma("y", [nt], ["QX%d" % (s + 1)], T.QR[:, lo:lo + 6, 512:1024], T.QR[:, lo:lo + 6, 0:512])
+
+        def df(hi):
+            return T.DF[:, 1024 * hi:1024 * hi + 1024]
+
+        def p_d(hi):
+            if hi < 6:
+                tt(["OF3D", qt, "QX%d" % s] + XR, ["DF%d" % hi], df(hi),
+                   T.XB[:, 256:2304].indirect(T.OF[:, 160 + 64 * hi:224 + 64 * hi]), T.QR[:, 6 * s + hi, :], A.subtract)
+            else:
+                for c in range(2):
+                    o, l = 1024 * hi + 512 * c, 160 + 64 * hi + 32 * c
+                    tt(["OF3R", "QRR"] + XR, ["DF%d" % hi], T.DF[:, o:o + 512],
+                       T.XB[:, 256:2304].indirect(T.OF[:, l:l + 32]), T.QRR[:, hi - 6, :], A.subtract)
+
+        def p_s(hi):
+            act(["DF%d" % hi], ["DF%d" % hi], df(hi), df(hi), ACT.Abs)
+
+        def p_m(hi):
+            wrapsum("EK", ["DF%d" % hi], "K3", T.K3[:, 64 * hi:64 * hi + 64], lambda r: T.DF[:, 1024 * hi + r:1024 * hi + 1024:16], False, False)
+
+        def p_g(hi):
+            k = 1024 * (hi % 2)
+            gather("s", ["OF3D" if hi < 6 else "OF3R"], ["OCC3%d" % (hi % 2)], T.OCC3[:, k:k + 1024], T.OF[:, 160 + 64 * hi:224 + 64 * hi])
+
+        def p_x(hi):
+            if hi == 1:
+                diff(["OCC1R"], "QRR", T.OCC1[:, 384:512], T.QRR[:, :, 0:64], 128, T.AB1[:, 384:512], "AB1R")
+                return
+            for c in range(2):
+                o, k = 1024 * hi + 512 * c, 1024 * (hi % 2) + 512 * c
+                reps = T.QR[:, 6 * s + hi, 0:512] if hi < 6 else T.QRR[:, hi - 6, :]
+                diff(["OCC3%d" % (hi % 2)], qt if hi < 6 else "QRR", T.OCC3[:, k:k + 512], reps, 512, T.DF[:, o:o + 512], "DF%d" % hi)
+
+        def p_rq():
+            mm(["WBD", at], "SR", T.SR[:, 0:32], T.WBD[:], arr[:], True, True)
+            tt(["MASK", "SR"], ["RS"], T.RS[:], T.SR[:, 0:32], T.MASK[:, 0:32], A.mult)
+            tt(["MASK", at], ["RE"], T.RE[:], arr[:], T.MASK[:, 0:32], A.mult)
+            for k in range(2):
+                red(["RS"], ["RQ"], T.RQ[:, k:k + 1], T.RS[:, 16 * k:16 * k + 16], A.add)
+            places(["RQ"], T.RQ[:], 2, T.PLW[:, 120:128], "PLW1R")
+            cp(["PLW1R"], ["OF1R"], T.OF[:, 24:32], T.PLW[:, 120:128])
+            gather("s", ["OF1R"], ["OCC1R"], T.OCC1[:, 384:512], T.OF[:, 24:32])
+            wrapsum("WR", ["OCC1R"], "SR", T.SR[:, 32:40], lambda r: T.OCC1[:, 384 + r:512:16], True, True)
+            for k in range(2):
+                red(["RE"], ["RF"], T.RF[:, k:k + 1], T.RE[:, 16 * k:16 * k + 16], A.add)
+            ts(["RF"], ["NEQ"], T.NEQ[:, 6:8], T.RF[:], 512.0, None, A.is_lt)
+
+        def p_r2():
+            places(["SR"], T.SR[:, 32:40], 8, T.PLW[:, 480:512], "PLW2R")
+            cp(["PLW2R"], ["OF2R"], T.OF[:, 128:160], T.PLW[:, 480:512])
+            gather("s", ["OF2R"], ["OCC2R"], T.OCC2[:, 1536:2048], T.OF[:, 128:160])
+            wrapsum("WR", ["OCC2R"], "SR", T.SR[:, 64:96], lambda r: T.OCC2[:, 1536 + r:2048:16], True, True)
+            diff(["OCC2R"], "QRR", T.OCC2[:, 1536:2048], T.QRR[:, :, 0:256], 512, T.AB2[:, 1536:2048], "AB23")
+
+        def p_r3():
+            places(["SR"], T.SR[:, 64:96], 32, T.PLW[:, 1920:2048], "PLW3R")
+            cp(["PLW3R"], ["OF3R"], T.OF[:, 544:672], T.PLW[:, 1920:2048])
+
+        def p_lc():
+            ts(["IO16", "PMF"], ["MASK"], T.MASK[:], T.IO16[:], T.PMF[:, 0:1], None, A.is_equal)
+            for t, c in enumerate((0.0, 128.0, 2304.0)):
+                ts(["LN"], ["TRC"], T.TRC[:, 8 * t:8 * t + 8], T.LN[:], c, None, A.add)
+                ts(["LN"], ["TRD"], T.TRD[:, 8 * t:8 * t + 8], T.LN[:], -1.0, 256.0 - c, A.mult, A.add)
+            ts(["LN"], ["TL"], T.TL[:], T.LN[:], 128.0, None, A.add)
+            ts(["TL"], ["NTL"], T.NTL[:], T.TL[:], -1.0, None, A.mult)
+            vset("CL0", T.CL[:], 0.0)
+            ts(["IO16", "PMF"], ["MKB"], T.MKB[:], T.IO16[:, 0:64], T.PMF[:, 0:1], -16.0, A.is_ge, A.mult)
+            for i in range(S - 1):
+                vset("SB%d" % i, T["SB%d" % i][:], 512.0)
+            vset("OLDqR", T.OLD[:, 480:512], 0.0)
+            sel("BDB", "LTB", T.LTB[:], T.BDB[:], [[1, 128]], A.is_gt, 0.0, 0, -1)
+
+        def p_k3():
+            mm(["IOFF", "ONE"], "K3", T.K3[:, 0:64 * H], T.IOFF[:], T.ONE[:, 0:64 * H], True, False)
+            mm(["IH", "IX3"], "K3", T.K3[:, 0:64 * H], T.IH[:], T.IX3[:, 0:64 * H], False, False)
+
+        def p_k1():
+            mm(["IOFF", "ONE"], "K12", T.K12[:, 0:H, 0:4], T.IOFF[:], T.ONE[:, 0:4 * H], True, False)
+            mm(["IH", "IX12"], "K12", T.K12[:, 0:H, 0:4], T.IH[:], T.IX12[:, 0:H, 0:4], False, False)
+            wrapsum("EK", ["AB1" + b for b in both], "K12", T.K12[:, 0:H, 0:4], lambda r: T.AB1[:, r:64 * H:16], False, True)
+
+        def p_fe():
+            ts(["K12"], ["FE1"], T.FE1[:, 0:4 * H], T.K12[:, 0:H, 0:4], 0.0, None, A.is_ge)
+            ts(["K12"], ["NH"], T.NH[:, 0:H, :], T.K12[:, 0:H, 0:4], OFFS + E11, None, A.is_ge)
+
+        def p_fq():
+            for a in range(4):
+                tt(PL2 + PL1, ["FQ2"], T.FQ2[:, a:16 * H:4], T.PLW[:, 384 + a:384 + 16 * H:4], T.PLW[:, 96:96 + 4 * H], A.is_equal)
+
+        def p_k2():
+            mm(["IOFF", "ONE"], "K12", T.K12[:, 0:H, 4:20], T.IOFF[:], T.ONE[:, 0:16 * H], True, False)
+            mm(["IH", "IX12"], "K12", T.K12[:, 0:H, 4:20], T.IH[:], T.IX12[:, 0:H, 4:20], False, False)
+            wrapsum("EK", ["AB2%d" % i for i in range(H // 2)], "K12", T.K12[:, 0:H, 4:20], lambda r: T.AB2[:, r:256 * H:16], False, False)
+            for a in range(4):
+                mm(["IPEN", "FE1"], "K12", T.K12[:, 0:H, 4 + a:20:4], T.IPEN[:], T.FE1[:, 0:4 * H], False, False)
+            mm(["IPEN", "FQ2"], "K12", T.K12[:, 0:H, 4:20], T.IPEN[:], T.FQ2[:, 0:16 * H], False, True)
+
+        def p_fa():
+            for f, c, o in (("FA", 0.0, A.is_ge), ("FB", OFFS, A.is_lt)):
+                ts(["K12"], [f], T[f][:, 0:16 * H], T.K12[:, 0:H, 4:20], c, None, o)
+
+        def p_p12():
+            for a in range(4):
+                for f in ("FA", "FB"):
+                    mm(["IPEN", f], "K3", T.K3[:, a:64 * H:4], T.IPEN[:], T[f][:, 0:16 * H], False, False)
+
+        def p_ph():
+            cp(PL1, ["PH1"], T.PH[:, 0:4 * H], T.PLW[:, 96:96 + 4 * H])
+            cp(PL2, ["PH2"], T.PH[:, 32:32 + 16 * H], T.PLW[:, 384:384 + 16 * H])
+            mm(["IH", "PH2"], "OT", T.OT[:, 0:16 * H], T.IH[:], T.PH[:, 32:32 + 16 * H], True, True)
+            for a in range(4):
+                mm(["IH", "PH1"], "OT", T.OT[:, 128 + a:128 + 16 * H:4], T.IH[:], T.PH[:, 0:4 * H], True, True)
+
+        def p_fp():
+            for a in range(4):
+                tt(PL3 + ["OT"], ["FP"], T.FP[:, a:64 * H:4], T.PLW[:, 1536 + a:1536 + 64 * H:4], T.OT[:, 0:16 * H], A.is_equal)
+
+        def p_fg():
+            for a in range(4):
+                tt(PL3 + ["OT"], ["FG"], T.FG[:, a:64 * H:4], T.PLW[:, 1536 + a:1536 + 64 * H:4], T.OT[:, 128:128 + 16 * H], A.is_equal)
+
+        def p_pp():
+            mm(["IPEN", "FP"], "K3", T.K3[:, 0:64 * H], T.IPEN[:], T.FP[:, 0:64 * H], False, False)
+
+        def p_pg():
+            mm(["IPEN", "FG"], "K3", T.K3[:, 0:64 * H], T.IPEN[:], T.FG[:, 0:64 * H], False, True)
+
+        def p_lv():
+            tt(["NH"], ["N1"], T.N1[:], T.NH[:, :, 0:2], T.NH[:, :, 2:4], A.mult)
+            tt(["N1"], ["LV"], T.LV[:], T.N1[:, :, 0], T.N1[:, :, 1], A.mult)
+            tt(["LV", "NEQ"], ["LIVE"], T.LIVE[:], T.LV[:], T.NEQ[:], A.mult)
+            ts(["LIVE"], ["MD"], T.MD[:], T.LIVE[:], -33554432.0, 16777216.0, A.mult, A.add)
+            ts(["LIVE"], ["DEAD"], T.DEAD[:], T.LIVE[:], -16.0, 16.0, A.mult, A.add)
+
+        def p_r12():
+            for hi in range(H):
+                red(["K12"], ["M12"], T.M12[:, hi:hi + 1], T.K12[:, hi, :], A.max)
+            tt(["M12", "MD"], ["ML12"], T.ML12[:], T.M12[:], T.MD[:], A.max)
+
+        by_block = {"d": p_d, "s": p_s, "m": p_m, "g": p_g, "x": p_x}
+        whole = {"rq": p_rq, "r2": p_r2, "r3": p_r3, "lc": p_lc, "k3": p_k3, "k1": p_k1, "fe": p_fe, "fq": p_fq, "k2": p_k2, "fa": p_fa,
+                 "p12": p_p12, "fp": p_fp, "fg": p_fg, "pp": p_pp, "ph": p_ph, "pg": p_pg, "lv": p_lv, "r12": p_r12}
+        for w in ORDER.split():
+            if w == "lc" and s > 0:
+                continue
+            if not arrivals and (w in ("rq", "r2", "r3", "x1") or w[0] in "dsmgx" and w[1:] in ("6", "7")):
+                continue
+            if w in whole:
+                whole[w]()
+            else:
+                by_block[w[0]](int(w[1:]))
+
+        for hi in range(H):
+            red(["K3"], ["M3"], T.M3[:, hi:hi + 1], T.K3[:, 64 * hi:64 * hi + 64], A.max)
+        tt(["ML12", "M3"], ["MI"], T.MI[:], T.ML12[:], T.M3[:], A.max)
+        ts(["MI"], ["PG"], T.PG[:], T.MI[:], 4, 127, A.arith_shift_right, A.bitwise_and)
+        ts(["MI"], ["PO"], T.PO[:, 0:8], T.MI[:], 2047, None, A.bitwise_and)
+        ts(["MI"], ["PO"], T.PO[:, 8:16], T.MI[:], 2, 511, A.arith_shift_right, A.bitwise_and)
+        tt(["PG", "BH"], ["PO"], T.PO[:, 16:24], T.PG[:], T.BH[:], A.max)
+        cp(["PO"], ["POU"], T.POU[:], T.PO[:])
+        ts(["MI"], ["NE"], T.NE[:], T.MI[:], 0.0, None, A.is_lt)
+        tt(["POU", "MASK", "PLW0", "PLWA", "PLWB"] + PL1 + PL2 + PL3, ["SELM"],
+           T.SELM[:], T.PLW[:, 0:2048].indirect(T.POU[:, 0:24]), T.MASK[:], A.mult)
+        mm(["BDH", "SELM"], "OT", T.OT[:], T.BDH[:], T.SELM[:], True, True)
+        for r in range(16):
+            mm(["IH", "SELM"], "OW", T.OW[:, 0:24], T.IH[:], T.SELM[:, r:384:16], r == 0, r == 15)
+        cp(["OT"], ["OTHH"], T.OTHH[:], T.OT[:])
+        ts(["OW"], ["XL"], T.XL[:], T.OW[:, 0:24], 256.0, None, A.add)
+        xall = XR + ["XBqD", "XBqR", "XBq", "XBt", "XBt2"]
+
+        def own_blocks(h0):
+            out = T.DB[:, 16 * h0:16 * h0 + 64]
+            mm(["IB", "MKB"], "DB", out, T.IB[:], T.MKB[:], True, False)
+            mm(["IB", "DEAD"], "DB", T.DB[:, 16 * h0:16 * h0 + 64:16], T.IB[:], T.DEAD[:, h0:h0 + 4], False, False)
+            for k in range(9):
+                mm(["IB"] + ["EQ%d" % h for h in range(h0, h0 + 4)], "DB", out, T.IB[:],
+                   T.EQ[:, 8 * k + h0:8 * k + h0 + 4, 112:128], False, k == 8)
+
+        for hi in range(7, -1, -1):
+            n = 16 * (hi + 1)
+            for t in range(3):
+                ts(["OTHH", "OW"], ["EQ%d" % hi], T.EQ[:, 24 * t + hi:24 * t + hi + 17:8, 128 - n:128], T.OTHH[:, :, 0:n],
+                   T.OW[:, 8 * t + hi:8 * t + hi + 1], None, A.is_equal)
+            if hi >= SCAL:
+                k = 9 * (hi - SCAL)
+                op("s", ["EQ%d" % hi], ["CL%d" % hi, "JK%d" % hi], lambda e: e.activation(
+                    T.JK[:, k:k + 9, 0:16 * hi], T.EQ[:, hi:72:8, 112 - 16 * hi:112], ACT.Copy, accum_out=T.CL[:, hi:hi + 1]))
+            elif hi > 0:
+                for k in range(9):
+                    mm(["IB", "EQ%d" % hi], "DA", T.DA[:, 64 * hi:80 * hi], T.IB[:], T.EQ[:, 8 * k + hi, 112 - 16 * hi:112], k == 0, k == 8)
+            if hi in (4, 0):
+                own_blocks(hi)
+        act(["XL"] + xall, ["OLD"], T.OLD[:, 0:384], T.XB[:, 0:2432].indirect(T.XL[:, 0:24]), ACT.Copy)
+        tt(["OW", "TRD"], ["W1"], T.W1[:], T.OW[:, 0:24], T.TRD[:], A.add)
+        for hi in range(SCAL - 1, 0, -1):
+            red(["DA"], ["CL%d" % hi], T.CL[:, hi:hi + 1], T.DA[:, 64 * hi:80 * hi], A.max)
+        for hi in range(7, -1, -1):
+            red(["DB"], ["CFM"], T.CFM[:, hi:hi + 1], T.DB[:, 16 * hi:16 * hi + 16], A.max)
+        tt(["CFM", "CL0"] + ["CL%d" % h for h in range(1, 8)], ["CFX"], T.CFX[:], T.CFM[:], T.CL[:], A.max)
+        ts(["CFX"], ["GO"], T.GO[:], T.CFX[:], 0.5, None, A.is_lt)
+        if send:
+            tt(["GO", "NE"], ["ND"], T.ND[:], T.GO[:], T.NE[:], A.mult)
+            mm(["IH", "NTL"], "OW", T.OW[:, 32:40], T.IH[:], T.NTL[:], True, False)
+            mm(["LTB", "ND"], "OW", T.OW[:, 32:40], T.LTB[:], T.ND[:], False, False)
+            for d in range(1, 8):
+                mm(["BDB", "ND"], "OW", T.OW[:, 32 + d:40], T.BDB[:], T.ND[:, 0:8 - d], False, d == 7)
+        for t in range(3):
+            tt(["GO", "W1"], ["W2"], T.W2[:, 8 * t:8 * t + 8], T.W1[:, 8 * t:8 * t + 8], T.GO[:], A.mult)
+        tt(["W2", "TRC"], ["W3"], T.W3[:], T.W2[:], T.TRC[:], A.add)
+        cp(["W3"], ["DLU"], T.DLU[:], T.W3[:])
+        op("v", ["DLU", "OLD", "OLDqD", "OLDqR"], xall,
+           lambda e: e.tensor_copy(T.XB[:, 0:2432].indirect(T.DLU[:, 0:24]), T.OLD[:, 128:512]))
+        if send:
+            first(s + 1)
+            sb = "SB%d" % s
+            tt(["OW", "ND"], ["D2"], T.D2[:], T.OW[:, 32:40], T.ND[:], A.mult)
+            tt(["D2", "TL"], ["D3"], T.D3[:], T.D2[:], T.TL[:], A.add)
+            cp(["D3"], ["SLU"], T.SLU[:], T.D3[:])
+            op("v", ["SLU", "OLD"], [sb], lambda e: e.tensor_copy(T[sb][:, 0:256].indirect(T.SLU[:, 0:8]), T.OLD[:, 0:128]))
+            before("g", [sb], [])
+            g.remote_dma(T["ARR%d" % (s + 1)][:], T[sb][:, 0:32], T.sem["arr%d" % (s + 1)], T.sem.sent, pid, rid, wire)
+    dma("y", XR, ["y0"], T.y[:, 0:1024], T.XB[:, 256:1280])
+    dma("s", XR, ["y1"], T.y[:, 1024:2048], T.XB[:, 1280:2304])
+    g.wait_ge(T.sem.sent, nwire * (S - 1))
+    finish()

@@ -4,54 +4,139 @@ A = AluOpType
 ACT = ActivationFunctionType
 X = AxisListType.X
 S = 5
-E11 = 2048.0
-OFFS = -8388608.0
-PEN = -33554432.0
-BASE = (96, 384, 1536)
-SCAL = 4
-ORDER = "lc rq g3 k3 x1 d0 k1 r2 x3 fq fe d1 k2 ph d2 r3 s1 m1 d6 fa s2 d4 s6 d5 p12 m3 s0 s4 d7 m6 m2 m0 m4 fp lv fg pp s5 s7 m5 m7 r12 pg"
+PEN = -16777216.0
+DEADKEY = 12582912.0
+ON_PE = (7, 6)
+CVT = "ssvsv"
+PIECE = 32
+CYC, PEC, GATHER, SCATTER, HOP, LOCAL, FAR = 0.00083, 0.0005, 1.6, 3.8, 0.2, 2.2, 3.2
+SLACK, ROUNDS, JIT = 0.1, 6, 0.3
+PLANNED = {}
 
 SCRATCH = {}
 for _t, _l in (
-        ("bfloat16", "XB:2432 QS:480 WTS:1 MT:128 MT2:128 ML:128 IO16:384 EK:2048 WR:2048 WBD:128 ONE:512 IB:128 NIB:128 IPEN:128"
-                     " IOFF:128 BDB:128 LTB:128 MKB:64 OCC1:512 OCC2:2048 OCC3:2048 AB1:512 AB2:2048 DF:8192 FE1:32 DEAD:8 FQ2:128"
-                     " FA:128 FB:128 FP:512 FG:512 OLD:512 ND:8 SB0:256 SB1:256 SB2:256 SB3:256 ARR1:32 ARR2:32 ARR3:32 ARR4:32"),
-        ("float32", "KF:4 KG:4 KH:4 K32:4 MASK:384 PMF:1 LN0:8 LN:8 TRC:24 TRD:24 TL:8 IX3F:512 RS:32 RQ:2 RE:32 RF:2 LV:8 LIVE:8 NEQ:8"
-                    " M12:8 M3:8 MD:8 ML12:8 CFM:8 CFX:8 CL:8 GO:8 W1:24 W2:24 W3:24 NE:8 D2:8 D3:8"),
-        ("float16", "IH:128 BDH:128 NTL:8 IX3:512 SELM:384 PH:160"),
-        ("int32", "KKI:4 PIN:1 PMI:1 BH:8 PLW:2048 P1A:120 UI:128 U:128 Z:512 Y:512 MI:8 PG:8 PO:24"),
-        ("uint16", "OF:672 L1U:120 POU:24 XL:24 DLU:24 SLU:8")):
+        ("bfloat16", "XB:2688 QS:480 WTS:1 CQ:128 CM:128 CG:128 CR:128 WX:512 XS:128 XT:128 XU:128 IB:128 IB5:128 IPEN:128 BDB:128 LTB:128 MKB:128 BD2:8"
+                     " QR4:2560 QR16:10240 MX1:512 MX2:2048 OLD:512 ND:8 NTL:8 DEAD:8 MASK:384 SB:1024 ARR:160"),
+        ("float16", "LX:512 UX:512 AM:128 AT:128 AU:128 BM:128 BT:128 BU:128 IOT:512 BD1:8 HI:8 ST:384 G1:512 G2:2048 DFV:6144 DFC:2048 QTH:640 PH:640"
+                    " SELM:384 SELN:128 TH:128 OLDT:256"),
+        ("float32", "TB:2688 QT:480 PCW:1024 NEWT:384 MS:960 RST:160 RS16:128 CFS:128 IOF:512 KF:4 KM:4 KC1:4 PF:4 IO4:8 PX:4 BX:4 EX:4 EA:4 SC:18"
+                    " LN0:8 LN:8 TRC:24 TL:8 SM:512 MD:16"),
+        ("int32", "KKI:4 PIN:1 PI:6 UI:640 U:640 Z:640 Y:640 P:640 MI:8 PO:24"),
+        ("uint16", "L1U:120 OF1:8 OF2:128 OFV:384 OFC:128 POU:24 NEU:8 XL:24 DLU:24 SLU:8")):
     for _w in _l.split():
         SCRATCH[_w.split(":")[0]] = ("sbuf", [128, int(_w.split(":")[1])], _t)
-for _n, _s, _t in (("QR", [128, 30, 1024], "bfloat16"), ("QRR", [128, 2, 512], "bfloat16"), ("IX12F", [128, 8, 20], "float32"),
-                   ("IX12", [128, 8, 20], "float16"), ("NH", [128, 8, 4], "float32"), ("N1", [128, 8, 2], "float32"),
-                   ("OTHH", [128, 3, 128], "float16"), ("EQ", [128, 72, 128], "bfloat16"), ("JK", [128, 36, 112], "bfloat16")):
-    SCRATCH[_n] = ("sbuf", _s, _t)
-BANKS = ("SD", "SR", "K12", "K3", "DA", "DB", "OT", "OW")
-for _n, _s in (("SD", [128, 128]), ("SR", [128, 128]), ("K12", [128, 8, 20]), ("K3", [128, 512]), ("DA", [128, 512]), ("DB", [128, 512]),
-               ("OT", [128, 384]), ("OW", [128, 64])):
-    SCRATCH[_n] = ("psum", _s, "float32")
-SEMAPHORES = ["cv", "cs", "cp", "cg", "sent"] + ["arr%d" % (i + 1) for i in range(S - 1)] + ["d%d" % i for i in range(40)]
+for _n, _s, _t in (("CA", [8, 16], "bfloat16"), ("MAS", [8, 16], "float16"), ("CV", [32, 16], "float16"), ("RK1", [32, 5], "float16"),
+                   ("RK2", [8, 5], "float16"), ("RP2", [16, 4], "float16"), ("RQP", [32, 32], "float16"), ("RQC", [32, 8], "float16"),
+                   ("RQK", [128, 5], "float16"), ("RQF", [128, 5], "float32"), ("RCF", [4, 8], "float32"), ("FG", [16, 32], "bfloat16"),
+                   ("OTHH", [3, 128], "float16"), ("EQ", [72, 128], "bfloat16"), ("JK", [63, 112], "bfloat16")):
+    SCRATCH[_n] = ("sbuf", [128] + _s, _t)
+BANKS = ("LD", "LR", "KA", "KB", "KC", "PA", "PB", "PC")
+for _n, _s in zip(BANKS, ([512], [512], [64, 5], [32, 5], [512], [16, 32], [16, 32], [64, 8])):
+    SCRATCH[_n] = ("psum", [128] + _s, "float32")
+SEMAPHORES = ["cv", "cs", "cp", "cg", "sent"] + ["arr%d" % (i + 1) for i in range(S - 1)] + ["d%d" % i for i in range(60)]
 
 
-def make_queue(g, T):
+def plan(calls):
+    n = len(calls)
+    preds, writer, readers = [], {}, {}
+    for i, c in enumerate(calls):
+        p = {}
+        for t in c["rd"]:
+            if t in writer:
+                p[writer[t]] = HOP
+        for t in c["wr"]:
+            for r in readers.get(t, []):
+                p[r] = 0.0 if t in BANKS and calls[r]["q"] == c["q"] else HOP
+            if t in writer:
+                w = writer[t]
+                p[w] = max(p.get(w, 0.0), 0.0 if calls[w]["q"] == c["q"] and calls[w]["kind"] == "op" else HOP)
+        if c["q"] == "p":
+            for t in c["rd"]:
+                if t in BANKS and t in writer and calls[writer[t]]["q"] == "p":
+                    p[writer[t]] = 0.0
+        p.pop(i, None)
+        preds.append(p)
+        for t in c["rd"]:
+            readers.setdefault(t, []).append(i)
+        for t in c["wr"]:
+            writer[t] = i
+            readers[t] = []
+    succ, back = [[] for _ in calls], [[] for _ in calls]
+    for i, p in enumerate(preds):
+        for j, lat in p.items():
+            succ[j].append((i, lat + calls[j]["late"]))
+            back[i].append((j, lat + calls[j]["late"]))
+
+    def walk(after, way):
+        left = [0] * n
+        for i in range(n):
+            for j, _ in after[i]:
+                left[j] += 1
+        ready, end = [0.0] * n, [0.0] * n
+        free = {q: 0.0 for q in "vspgy"}
+        may = {q: [i for i in range(n) if calls[i]["q"] == q and not left[i]] for q in free}
+        order = []
+        while len(order) < n:
+            pick = None
+            for q in free:
+                if not may[q]:
+                    continue
+                top = None
+                may[q].sort(key=lambda k: -way[k])
+                for i in may[q]:
+                    t = max(free[q], ready[i])
+                    if top is None or t < top[0] and t + calls[i]["cost"] <= top[0] + SLACK:
+                        top = (t, i)
+                        if t == free[q]:
+                            break
+                if pick is None or top < pick:
+                    pick = top
+            t, i = pick
+            q = calls[i]["q"]
+            may[q].remove(i)
+            free[q] = end[i] = t + calls[i]["cost"]
+            order.append(i)
+            for j, lat in after[i]:
+                ready[j] = max(ready[j], end[i] + lat)
+                left[j] -= 1
+                if not left[j]:
+                    may[calls[j]["q"]].append(j)
+        return order, end
+
+    way = [0.0] * n
+    for i in range(n - 1, -1, -1):
+        way[i] = calls[i]["cost"] + max([lat + way[j] for j, lat in succ[i]] + [0.0])
+    best = None
+    for k in range(ROUNDS):
+        order, end = walk(succ, way)
+        if best is None or max(end) < best[0]:
+            best = (max(end), order, end)
+        shift = [JIT * ((i * 7919 + k * 104729) % 1009) / 1009.0 for i in range(n)]
+        way = walk(back, [e + d for e, d in zip(best[2], shift)])[1]
+    return best[1]
+
+
+def issue(g, T, calls):
     eng = {"v": g.vector, "s": g.scalar, "p": g.tensor, "g": g, "y": g.sync}
     count = {"cv": 0, "cs": 0, "cp": 0, "cg": 0}
     known = {q: {} for q in eng}
     snap, writer, readers, touch = {}, {}, {}, {}
-    dmas = [0]
-
-    def before(q, rd, wr):
+    dmas = 0
+    if len(calls) not in PLANNED:
+        PLANNED[len(calls)] = plan(calls)
+    for i in PLANNED[len(calls)]:
+        c = calls[i]
+        q, rd, wr = c["q"], c["rd"], c["wr"]
         evs = []
-        for t in rd:
+        for t in rd + wr:
             if t in BANKS:
                 evs += [e for e in touch.get(t, {}).values() if e[2] != q]
-            elif t in writer:
+            elif t in rd and t in writer:
                 evs.append(writer[t])
         for t in wr:
             if t in BANKS:
-                evs += [e for e in touch.get(t, {}).values() if e[2] != q]
-            elif readers.get(t):
+                continue
+            if readers.get(t):
                 evs += list(readers[t].values()) + ([writer[t]] if t in writer else [])
             elif t in writer and writer[t][2] != q:
                 evs.append(writer[t])
@@ -62,460 +147,531 @@ def make_queue(g, T):
             val = best[sem]
             if known[q].get(sem, 0) < val:
                 eng[q].wait_ge(T.sem[sem], val)
-                for k, n in snap.get((sem, val), {}).items():
-                    known[q][k] = max(known[q].get(k, 0), n)
+                for k, m in snap.get((sem, val), {}).items():
+                    known[q][k] = max(known[q].get(k, 0), m)
                 known[q][sem] = val
-
-    def after(ev, rd, wr):
-        for t in rd:
+        if c["kind"] == "op":
+            sem = "c" + q
+            count[sem] += 1
+            c["call"](eng[q]).then_inc(T.sem[sem], 1)
+            ev = (sem, count[sem], q)
+        elif c["kind"] == "dma":
+            sem = "d%d" % dmas
+            dmas += 1
+            c["call"](eng[q]).then_inc(T.sem[sem], 16)
+            ev = (sem, 16, "dma")
+        else:
+            c["call"](g)
+            ev = c["ev"]
+        if c["kind"] != "far":
+            snap[ev[:2]] = dict(known[q])
+        for t in rd + wr:
             if t in BANKS:
                 touch.setdefault(t, {})[ev[2]] = ev
-            else:
-                readers.setdefault(t, {})[(ev[2], ev[0])] = ev
-        for t in wr:
-            if t in BANKS:
-                touch.setdefault(t, {})[ev[2]] = ev
-            else:
+            elif t in wr:
                 writer[t] = ev
                 readers[t] = {}
-
-    def op(q, rd, wr, call):
-        before(q, rd, wr)
-        sem = "c" + q
-        count[sem] += 1
-        call(eng[q]).then_inc(T.sem[sem], 1)
-        snap[(sem, count[sem])] = dict(known[q])
-        after((sem, count[sem], q), rd, wr)
-
-    def dma(q, rd, wr, out, in_):
-        before(q, rd, wr)
-        sem = "d%d" % dmas[0]
-        dmas[0] += 1
-        eng[q].dma_start(out, in_).then_inc(T.sem[sem], 16)
-        snap[(sem, 16)] = dict(known[q])
-        after((sem, 16, "dma"), rd, wr)
-
-    def outside(sem, val, wr):
-        after((sem, val, "far"), [], wr)
-
-    def finish():
-        for sem in ("cv", "cs", "cp", "cg"):
-            if known["g"].get(sem, 0) < count[sem]:
-                g.wait_ge(T.sem[sem], count[sem])
-        for i in range(dmas[0]):
-            g.wait_ge(T.sem["d%d" % i], 16)
-    return op, dma, outside, before, finish
+            elif c["kind"] != "far":
+                readers.setdefault(t, {})[(ev[2], ev[0])] = ev
+    for sem in count:
+        if known["g"].get(sem, 0) < count[sem]:
+            g.wait_ge(T.sem[sem], count[sem])
+    for i in range(dmas):
+        g.wait_ge(T.sem["d%d" % i], 16)
 
 
 def rank_program(g, core, T, topo):
     rank = T.rank_of(core)
     if rank is None:
         return
-    op, dma, outside, before, finish = make_queue(g, T)
     nxt = T.cores[(rank + 1) % len(T.cores)]
     rid, pid = topo.addr(nxt, core)
     wire = topo.mask(core, nxt)
     nwire = len(topo.engines(core, nxt))
     nland = len(topo.engines(T.cores[(rank - 1) % len(T.cores)], core))
+    calls = []
 
-    dma("y", [], ["QS"], T.QS[:], T.qs[:])
-    dma("s", [], ["WTS"], T.WTS[:], T.wt[:])
-    dma("s", [], ["KKI"], T.KKI[:], T.kk[:])
-    dma("y", [], ["QR0"], T.QR[:, 0:6, 0:16], T.qs[:, 0:96])
-    dma("s", [], ["XBx"], T.XB[:, 256:1280], T.x0[:, 0:1024])
-    dma("y", [], ["XBx2"], T.XB[:, 1280:2304], T.x0[:, 1024:2048])
-    for s in range(1, S):
-        dma("y", [], ["QR%d" % s], T.QR[:, 6 * s:6 * s + 6, 0:16], T.qs[:, 96 * s:96 * s + 96])
-    dma("y", [], ["XBqD"], T.XB[:, 0:96], T.qs[:, 0:96])
-    dma("y", [], ["OLDqD"], T.OLD[:, 384:480], T.qs[:, 0:96])
+    def size(ap):
+        n = 1
+        for k in ap.shape[1:]:
+            n *= int(k)
+        return n
+
+    def op(q, rd, wr, cost, call):
+        calls.append({"q": q, "rd": list(rd), "wr": list(wr), "cost": cost, "late": 0.0, "kind": "op", "call": call})
+
+    def dma(q, rd, wr, out, in_, late=LOCAL):
+        calls.append({"q": q, "rd": rd, "wr": wr, "cost": 0.05, "late": late, "kind": "dma", "call": lambda e: e.dma_start(out, in_)})
+
+    def cyc(n):
+        return max(64, n) * CYC
 
     def iota(tok, out, pattern, base, cm, small=True):
         if small:
-            op("g", [], [tok], lambda e: e.iota(out, pattern, base, cm, allow_small_or_imprecise_dtypes=True))
+            op("g", [], [tok], 0.13 + 2 * size(out) * CYC, lambda e: e.iota(out, pattern, base, cm, allow_small_or_imprecise_dtypes=True))
         else:
-            op("g", [], [tok], lambda e: e.iota(out, pattern, base, cm))
+            op("g", [], [tok], 0.13 + 2 * size(out) * CYC, lambda e: e.iota(out, pattern, base, cm))
 
     def sel(rd, tok, out, in_, pattern, cmp, fill, base, cm):
-        op("g", [rd], [tok], lambda e: e.affine_select(out, in_, pattern, cmp, fill, base, cm))
+        op("g", [rd], [tok], 0.17 + 2 * size(out) * CYC, lambda e: e.affine_select(out, in_, pattern, cmp, fill, base, cm))
 
-    def vset(tok, out, c):
-        op("v", [], [tok], lambda e: e.memset(out, c))
+    def paint(tok, ap, pattern, base, w):
+        sel(tok, tok, ap, ap, pattern, A.not_equal, w, base, -1)
 
-    def ts(rd, wr, out, in0, s1, s2, op0, op1=None):
+    def vset(toks, out, c, k=0.5):
+        op("v", [], toks, cyc(k * size(out)), lambda e: e.memset(out, c))
+
+    def ts(rd, wr, out, in0, s1, s2, op0, op1=None, k=1.0):
         if op1 is None:
-            op("v", rd, wr, lambda e: e.tensor_scalar(out, in0, s1, None, op0=op0))
+            op("v", rd, wr, cyc(k * size(out)), lambda e: e.tensor_scalar(out, in0, s1, None, op0=op0))
         else:
-            op("v", rd, wr, lambda e: e.tensor_scalar(out, in0, s1, s2, op0=op0, op1=op1))
+            op("v", rd, wr, cyc(k * size(out)), lambda e: e.tensor_scalar(out, in0, s1, s2, op0=op0, op1=op1))
 
     def tt(rd, wr, out, a, b, o):
-        op("v", rd, wr, lambda e: e.tensor_tensor(out, a, b, o))
+        k = 1 if [t for t in rd if t in BANKS] else 2
+        op("v", rd, wr, cyc(k * size(out)), lambda e: e.tensor_tensor(out, a, b, o))
 
     def cp(rd, wr, out, a):
-        op("v", rd, wr, lambda e: e.tensor_copy(out, a))
+        op("v", rd, wr, cyc(size(out)), lambda e: e.tensor_copy(out, a))
 
-    def red(rd, wr, out, a, o):
-        op("v", rd, wr, lambda e: e.tensor_reduce(out, a, X, o))
-
-    def act(rd, wr, out, a, func):
-        op("s", rd, wr, lambda e: e.activation(out, a, func))
-
-    def mm(rd, bank, out, lhsT, rhs, start, stop):
-        op("p", rd, [bank], lambda e: e.matmul(out, lhsT, rhs, start, stop))
-
-    iota("MT", T.MT[:], [[0, 8], [1, 16]], 0, 0)
-    sel("MT", "MT2", T.MT2[:], T.MT[:], [[-16, 8], [0, 16]], A.is_ge, -1.0, 0, 1)
-    sel("MT2", "ML", T.ML[:], T.MT2[:], [[16, 8], [0, 16]], A.is_ge, -1.0, 15, -1)
-    vset("ONE", T.ONE[:], 1.0)
-    sel("ONE", "IB", T.IB[:], T.ONE[:, 0:128], [[-1, 128]], A.is_equal, 0.0, 0, 1)
-    iota("PIN", T.PIN[:], [[0, 1]], 0, 1, False)
-    iota("IO16", T.IO16[:], [[0, 24], [1, 16]], 0, 0)
-    iota("LN0", T.LN0[:], [[16, 8]], 0, 0)
-    iota("BH", T.BH[:], [[1, 8]], 8, 0, False)
-    iota("IX12F", T.IX12F[:, :, 0:4], [[4, 8], [1, 4]], BASE[0], 0)
-    iota("IX12F", T.IX12F[:, :, 4:20], [[16, 8], [1, 16]], BASE[1], 0)
-    iota("IX3F", T.IX3F[:], [[1, 512]], BASE[2], 0)
-    op("v", [], ["XBq", "XBt"], lambda e: e.memset(T.XB[:, 96:256], 0.0))
-    vset("XBt2", T.XB[:, 2304:2432], 0.0)
-    vset("PLW0", T.PLW[:], -256)
-    vset("NH", T.NH[:], 0.0)
-    vset("M12", T.M12[:], OFFS)
-    vset("M3", T.M3[:], OFFS)
-    vset("NEQ", T.NEQ[:], 1.0)
-    for r in range(16):
-        ts(["ML", "WTS"], ["WR"], T.WR[:, 128 * r:128 * r + 128], T.ML[:], float(r), T.WTS[:, 0:1], A.is_equal, A.mult)
-    cp(["KKI"], ["KF"], T.KF[:], T.KKI[:])
-    ts(["KF"], ["KG"], T.KG[:], T.KF[:], 1024.0, -2048.0, A.is_gt, A.mult)
-    tt(["KF", "KG"], ["KH"], T.KH[:], T.KF[:], T.KG[:], A.add)
-    ts(["KH"], ["K32"], T.K32[:], T.KH[:], 32.0, None, A.mult)
-
-    def places(rd, src, n, dst, dtok):
-        cp(rd, ["UI"], T.UI[:, 0:n], src)
-        ts(["UI"], ["U"], T.U[:, 0:n], T.UI[:, 0:n], 2047, None, A.bitwise_and)
-        for a in range(4):
-            ts(["U", "K32"], ["Z%d" % a], T.Z[:, a * n:a * n + n], T.U[:, 0:n], T.K32[:, a:a + 1], None, A.add)
-        for a in range(4):
-            tt(["Z%d" % a, "U"], ["Y"], T.Y[:, a:4 * n:4], T.Z[:, a * n:a * n + n], T.U[:, 0:n], A.mult)
-        ts(["Y"], [dtok], dst, T.Y[:, 0:4 * n], 5, 2047, A.arith_shift_right, A.bitwise_and)
-
-    def wrapsum(mat, rd, bank, out, rhs, start, stop):
-        for r in range(16):
-            mm([mat] + rd, bank, out, T[mat][:, 128 * r:128 * r + 128], rhs(r), start and r == 0, stop and r == 15)
-
-    wrapsum("WR", ["QS"], "SD", T.SD[:, 0:30], lambda r: T.QS[:, r:480:16], True, True)
-    places(["SD"], T.SD[:, 0:30], 30, T.P1A[:], "P1A")
-    cp(["P1A"], ["L1U"], T.L1U[:], T.P1A[:])
-    w = 16
-    while w < 512:
-        act(["QR0"], ["QR0"], T.QR[:, 0:6, w:2 * w], T.QR[:, 0:6, 0:w], ACT.Copy)
-        w *= 2
-    dma("y", ["QR0"], ["QX0"], T.QR[:, 0:6, 512:1024], T.QR[:, 0:6, 0:512])
-    XR = ["XBx", "XBx2"]
-
-    def constants():
-        for r in range(16):
-            ts(["ML"], ["EK"], T.EK[:, 128 * r:128 * r + 128], T.ML[:], float(r), E11, A.is_equal, A.mult)
-        ts(["IB"], ["NIB"], T.NIB[:], T.IB[:], -1.0, None, A.mult)
-        ts(["IB"], ["IPEN"], T.IPEN[:], T.IB[:], PEN, None, A.mult)
-        ts(["IB"], ["IOFF"], T.IOFF[:], T.IB[:], OFFS, None, A.mult)
-        cp(["IX12F"], ["IX12"], T.IX12[:], T.IX12F[:])
-        cp(["IX3F"], ["IX3"], T.IX3[:], T.IX3F[:])
-        cp(["IB"], ["IH"], T.IH[:], T.IB[:])
-        ts(["ML"], ["BDB"], T.BDB[:], T.ML[:], 0.0, None, A.is_ge)
-        ts(["ML"], ["BDH"], T.BDH[:], T.ML[:], 0.0, None, A.is_ge)
-        ts(["ML", "WTS"], ["WBD"], T.WBD[:], T.ML[:], 0.0, T.WTS[:, 0:1], A.is_ge, A.mult)
-        ts(["PIN"], ["PMI"], T.PMI[:], T.PIN[:], 15, None, A.bitwise_and)
-        cp(["PMI"], ["PMF"], T.PMF[:], T.PMI[:])
-        ts(["LN0", "PMF"], ["LN"], T.LN[:], T.LN0[:], T.PMF[:, 0:1], None, A.add)
-        ts(["LN", "PLW0"], ["PLWA"], T.PLW[:, 24:32], T.LN[:], -256.0, None, A.add)
-        ts(["LN", "PLW0"], ["PLWB"], T.PLW[:, 8:16], T.LN[:], -128.0, None, A.add)
-
-    def gather(q, rd, wr, out, lst):
+    def offsets(q, rd, wr, out, a):
         if q == "v":
-            cp(rd + XR, wr, out, T.XB[:, 256:2304].indirect(lst))
+            cp(rd, wr, out, a)
         else:
-            act(rd + XR, wr, out, T.XB[:, 256:2304].indirect(lst), ACT.Copy)
+            act(rd, wr, out, a, ACT.Copy)
 
-    diffs = [0]
+    def runmax(rd, wr, out, reset, a):
+        op("v", rd, wr, cyc(size(out)), lambda e: e.tensor_tensor_scan(out, reset, a, 0.0, A.add, A.max))
 
-    def diff(rd, rt, occ, reps, n, out, otok):
-        bank = ("DA", "DB")[diffs[0] % 2]
-        diffs[0] += 1
-        ps = T[bank][:, 0:n]
-        mm(["IB"] + rd, bank, ps, T.IB[:], occ, True, False)
-        mm(["NIB", rt], bank, ps, T.NIB[:], reps, False, True)
-        act([bank], [otok], out, ps, ACT.Abs)
+    def act(rd, wr, out, a, func, bias=0.0, scale=1.0):
+        op("s", rd, wr, cyc(size(out)), lambda e: e.activation(out, a, func, bias=bias, scale=scale))
 
-    def first(s):
-        gather("s", ["L1U"], ["OCC1Ds"], T.OCC1[:, 0:192], T.L1U[:, 24 * s:24 * s + 12])
-        gather("v", ["L1U"], ["OCC1Dv"], T.OCC1[:, 192:384], T.L1U[:, 24 * s + 12:24 * s + 24])
-        cp(["P1A"], ["PLW1D"], T.PLW[:, 96:120], T.P1A[:, 24 * s:24 * s + 24])
+    def sset(toks, out, src, rd, c):
+        act([rd], toks, out, src, ACT.Identity, c, 0.0)
+
+    def count(rd, wr, out, a, acc):
+        op("s", rd, wr, cyc(size(out)) + 0.02, lambda e: e.activation(out, a, ACT.Copy, scale=65536.0, accum_out=acc))
+
+    def gather(q, rd, wr, out, win, lst, other=None, o=None, bias=None):
+        cost = 0.06 + GATHER * size(out) * CYC
+        if q == "v":
+            op(q, rd, wr, cost, lambda e: e.tensor_tensor(out, win.indirect(lst), other, o))
+        elif bias is None:
+            op(q, rd, wr, cost, lambda e: e.activation(out, win.indirect(lst), ACT.Copy))
+        else:
+            op(q, rd, wr, cost, lambda e: e.activation(out, win.indirect(lst), ACT.Abs, bias=bias, scale=-1.0))
+
+    def scatter(rd, wr, win, lst, a):
+        op("v", rd, wr, 0.05 + SCATTER * size(a) * CYC, lambda e: e.tensor_copy(win.indirect(lst), a))
+
+    def mm(rd, bank, out, lhsT, rhs, start, stop, free=False):
+        op("p", rd + [bank] * free, [bank] * (not free), max(min(64, size(lhsT)), size(rhs)) * PEC, lambda e: e.matmul(out, lhsT, rhs, start, stop))
+
+    def quad(mat, rd, bank, out, rhs, start=True, stop=True):
+        for x in range(4):
+            mm([mat] + rd, bank, out(x), T[mat][:, 128 * x:128 * x + 128], rhs(x), start and x == 0, stop and x == 3)
+
+    def col(name, i):
+        return T[name][:, i:i + 1]
+
+    def sm(name, a=0, b=8, st=1):
+        o = 32 * "L1 L2 H1 H2 H3 W1 W2 W3 D2 D3".split().index(name)
+        return T.SM[:, o + a:o + b:st]
+
+    XR, TR = ["XB0", "XB1"], ["TB0", "TB1", "TB2", "TB3"]
+    xall, tall = XR + ["XBqD", "XBqR", "XBz", "XBy"], TR + ["TBqD", "TBqR", "TBz", "TBy"]
+    XW, TW = T.XB[:, 256:2304], T.TB[:, 256:2304]
+    dma("y", [], ["QS"], T.QS[:], T.qs[:], 9.0)
+    dma("s", [], ["WTS"], T.WTS[:], T.wt[:], 9.0)
+    dma("s", [], ["KKI"], T.KKI[:], T.kk[:], 8.0)
+    dma("s", [], ["XB0"], T.XB[:, 256:1280], T.x0[:, 0:1024], 4.0)
+    dma("y", [], ["XB1"], T.XB[:, 1280:2304], T.x0[:, 1024:2048], 4.0)
+    for c in calls[0:3]:
+        c["late"] = LOCAL
+    dma("y", [], ["XBqD", "XBqR", "XBz"], T.XB[:, 0:256], T.qs[:, 0:256])
+    dma("y", [], ["XBy"], T.XB[:, 2304:2688], T.qs[:, 0:384])
+    dma("y", [], ["OLDqD", "OLDqR"], T.OLD[:, 384:512], T.qs[:, 0:128])
+    dma("y", [], ["MX1R"], T.MX1[:, 0:128], T.qs[:, 0:128])
+    dma("y", [], ["MX2_0"], T.MX2[:, 0:256], T.qs[:, 0:256])
+    dma("y", [], ["MX2_1"], T.MX2[:, 256:512], T.qs[:, 0:256])
+
+    iota("PIN", T.PIN[:], [[0, 1]], 0, 1, False)
+    iota("IO4", T.IO4[:, 0:4], [[4, 4]], 0, 0)
+    iota("IO4", T.IO4[:, 4:8], [[1, 4]], 0, 0)
+    iota("CQ", T.CQ[:], [[4, 32], [0, 4]], 0, 0)
+    iota("CA", T.CA[:], [[16, 8], [0, 4], [1, 4]], 0, 0)
+    iota("CM", T.CM[:], [[1, 128]], 0, 0)
+    iota("IOF", T.IOF[0:64, :], [[1, 512]], 0, 0)
+    iota("PX", T.PX[:], [[4, 4]], 0, 1)
+    iota("CG", T.CG[:], [[16, 8], [0, 16]], 0, 0)
+    iota("CR", T.CR[:], [[0, 8], [1, 16]], 0, 0)
+    iota("LN0", T.LN0[:], [[16, 8]], 0, 0)
+    for n in ("RK1", "RK2", "RP2", "RQP", "RQC", "ST", "MAS"):
+        vset([n], T[n][:], 0.0)
+    vset(["IOT1"], T.IOT[64:128, :], 1.0)
+    vset(["G2_0", "G2_1"], T.G2[:, 0:512], 0.0)
+    dma("y", ["G2_0", "G2_1"], ["G1R"], T.G1[:, 0:128], T.G2[:, 0:128])
+    for i in range(4):
+        dma("y", ["G2_0", "G2_1"], ["DF%d_0" % i, "DF%d_1" % i], T.DFV[:, 1536 * i:1536 * i + 512], T.G2[:, 0:512])
+    for i, (sh, m) in enumerate(((0, 112), (0, 15), (0, 3), (2, 3))):
+        ts(["PIN"], ["PI"], col("PI", i), T.PIN[:], sh, m, A.arith_shift_right, A.bitwise_and)
+    cp(["PI"], ["PF"], T.PF[:], T.PI[:, 0:4])
+    ts(["IO4", "PF"], ["BX"], T.BX[:], T.IO4[:, 0:4], col("PF", 0), None, A.add)
+    ts(["IO4", "PF"], ["EA"], T.EA[:], T.IO4[:, 4:8], col("PF", 2), None, A.is_equal)
+    ts(["IO4", "PF"], ["EX"], T.EX[:], T.IO4[:, 4:8], col("PF", 3), None, A.is_equal)
+    vset(["CV"], T.CV[:, :, 0:4], 0.0)
+    vset(["CV"], T.CV[0:64, :, 12:16], 0.0)
+    vset(["CV"], T.CV[64:128, :, 12:14], 0.0)
+    vset(["CV"], T.CV[0:64, :, 4:8], -16.0)
+    vset(["CV"], T.CV[0:64, :, 8:12], 16.0)
+    vset(["CV"], T.CV[64:128, :, 14], -16.0)
+    vset(["CV"], T.CV[64:128, :, 15], 1.0 / 64)
+    for b in range(4):
+        vset(["CV"], T.CV[64:128, 8 * b:8 * b + 8, 4:8], -16.0 - 8192.0 * b)
+        vset(["CV"], T.CV[64:128, 8 * b:8 * b + 8, 8:12], 8192.0 * b)
+    cp(["WTS"], ["WTF"], col("KC1", 3), T.WTS[:])
+    for x in range(4):
+        ts(["CQ", "BX", "WTF"], ["WX"], T.WX[:, 128 * x:128 * x + 128], T.CQ[:], col("BX", x), col("KC1", 3), A.is_equal, A.mult, 0.5)
+    cp(["KKI"], ["KF"], T.KF[:], T.KKI[:])
+    tt(["KF", "EA"], ["KM"], T.KM[:], T.KF[:], T.EA[:], A.mult)
+    op("v", ["KM"], ["K0"], cyc(4), lambda e: e.tensor_reduce(col("KC1", 0), T.KM[:], X, A.add))
+    ts(["K0"], ["K1"], col("KC1", 1), col("KC1", 0), 1024.0, -2048.0, A.is_gt, A.mult)
+    ts(["K0", "K1"], ["K32"], col("KC1", 2), col("KC1", 0), col("KC1", 1), 32.0, A.add, A.mult)
+
+    def places(rd, src, o, n):
+        k = "%d" % o
+        cp(rd, ["UI" + k], T.UI[:, o:o + n], src)
+        ts(["UI" + k], ["U" + k], T.U[:, o:o + n], T.UI[:, o:o + n], 2047, None, A.bitwise_and)
+        ts(["U" + k, "K32"], ["Z" + k], T.Z[:, o:o + n], T.U[:, o:o + n], col("KC1", 2), None, A.add)
+        tt(["Z" + k, "U" + k], ["Y" + k], T.Y[:, o:o + n], T.Z[:, o:o + n], T.U[:, o:o + n], A.mult)
+        ts(["Y" + k], ["P" + k], T.P[:, o:o + n], T.Y[:, o:o + n], 5, 2047, A.arith_shift_right, A.bitwise_and)
+        cp(["P" + k], ["PH" + k], T.PH[:, o:o + n], T.P[:, o:o + n])
+
+    ts(["PF"], ["SC0"], col("SC", 0), col("PF", 0), col("PF", 2), None, A.add)
+    ts(["PF"], ["SC10"], col("SC", 10), col("PF", 1), 8.0, 12.0, A.is_ge, A.add)
+    ts(["PF"], ["SC2"], col("SC", 2), col("PF", 0), 14.0, None, A.add)
+    ts(["PF"], ["SC3"], col("SC", 3), col("PF", 1), 0.0, 4.0, A.is_equal, A.mult)
+    ts(["PF", "SC10"], ["SC1"], col("SC", 1), col("SC", 10), col("PF", 0), None, A.add)
+    for lo, hi, w in ((0, 4, 1.0), (4, 8, 1024.0), (8, 12, -1024.0)):
+        ts(["CA", "SC0", "MAS"], ["MAS%d" % lo], T.MAS[:, :, lo:hi], T.CA[:, :, lo:hi], col("SC", 0), w, A.is_equal, A.mult)
+    ts(["CM", "SC1"], ["XT"], T.XT[:], T.CM[:], col("SC", 1), None, A.is_equal, None, 0.5)
+    ts(["CM", "SC2", "SC3"], ["XU"], T.XU[:], T.CM[:], col("SC", 2), col("SC", 3), A.is_equal, A.mult, 0.5)
+    act(["IOF"], ["IOT0"], T.IOT[0:64, :], T.IOF[0:64, :], ACT.Copy)
+    tt(["XT", "XU"], ["XS"], T.XS[:], T.XT[:], T.XU[:], A.add)
+    for x in range(4):
+        act(["MAS0", "MAS4", "MAS8", "EX"], ["UX"], T.UX[:, 128 * x:128 * x + 128], T.MAS[:], ACT.Identity, 0.0, col("EX", x))
+    ts(["PF"], ["SC11"], col("SC", 11), col("PF", 1), 14.0, None, A.is_equal)
+    ts(["PF"], ["SC6"], col("SC", 6), col("PF", 1), 15.0, -1024.0, A.is_equal, A.mult)
+    ts(["PF"], ["SC13"], col("SC", 13), col("PF", 1), 15.0, None, A.is_equal)
+    ts(["EX"], ["SC7"], col("SC", 7), col("EX", 1), -1024.0, None, A.mult)
+    ts(["EX"], ["SC12"], col("SC", 12), col("EX", 1), -8192.0, 8192.0, A.mult, A.add)
+    ts(["SC11", "EX"], ["SC14"], col("SC", 14), col("SC", 11), col("EX", 2), -7168.0, A.add, A.mult)
+    ts(["SC11", "SC13"], ["SC9"], col("SC", 9), col("SC", 11), -1024.0, col("SC", 13), A.mult, A.add)
+    ts(["SC14", "SC12"], ["SC8"], col("SC", 8), col("SC", 14), col("SC", 12), None, A.add)
+    ts(["EX"], ["SC16"], col("SC", 16), col("EX", 0), col("EX", 3), None, A.add)
+    ts(["PF"], ["SC4"], col("SC", 4), col("PF", 1), 4.0, None, A.is_lt)
+    ts(["PF"], ["SC5"], col("SC", 5), col("PF", 1), 12.0, None, A.is_ge)
+    for x in range(4):
+        ts(["CM", "PX", "SC4"], ["LX"], T.LX[:, 128 * x:128 * x + 128], T.CM[:], col("PX", x), col("SC", 4), A.is_equal, A.mult, 0.5)
+
+    for i in range(4):
+        iota("RQF", T.RQF[:, 32 * i:32 * i + 32, 0], [[8, 8], [1, 4]], 128 + 64 * (i // 2) + 4 * (i % 2), 0)
+        iota("RQF", T.RQF[:, 32 * i:32 * i + 32, 1:5], [[32, 8], [4, 4], [1, 4]], 512 + 256 * (i // 2) + 16 * (i % 2), 0)
+    sel("RQF", "RQK", T.RQK[:], T.RQF[:], [[0, 4], [16, 8], [0, 20]], A.is_equal, 0.0, 15, -1)
+    iota("RCF", T.RCF[:], [[2, 8], [16, 2], [1, 2]], 32, 0)
+    sel("RCF", "RQC", T.RQC[:, 8:12, :], T.RCF[:], [[16, 8], [0, 4]], A.is_equal, 0.0, 15, -1)
+    for r in (12, 13):
+        paint("RQK", T.RQK[:, :, 0], [[0, 4], [16, 8], [0, 4]], r, -1024.0)
+        paint("RQC", T.RQC[:, 8:12, :], [[16, 8], [0, 4]], r, -1024.0)
+        paint("RQC", T.RQC[:, 12, :], [[16, 8]], r, 1.0)
+        paint("RK2", T.RK2[:, :, 0], [[16, 8]], r, -1024.0)
+    paint("RQC", T.RQC[:, 4:8, :], [[2, 2], [16, 8], [1, 2]], 0, 1.0)
+    for h in range(2):
+        paint("RQP", T.RQP[:, 16 * h + 8:16 * h + 16, :], [[16, 8], [1, 2], [0, 16]], 2 * h, -1.0)
+    for r in (4, 8):
+        paint("RK1", T.RK1[:], [[16, 8], [1, 4], [0, 5]], r, 16384.0)
+        paint("RK2", T.RK2[:, :, 1:5], [[16, 8], [1, 4]], r, 16384.0)
+    paint("RK1", T.RK1[:], [[16, 8], [0, 20]], 14, -16384.0)
+    paint("RK2", T.RK2[:, :, 1:5], [[16, 8], [0, 4]], 14, -16384.0)
+    paint("RP2", T.RP2[:], [[0, 2], [16, 8], [1, 4]], 0, 1.0)
+    paint("ST", T.ST[:], [[8, 3], [1, 8], [0, 16]], 0, 1.0)
+
+    quad("WX", ["QS"], "KC", lambda x: T.KC[:, 256:376], lambda x: T.QS[:, x:480:4])
+    places(["KC"], T.KC[:, 256:376], 512, 120)
+    cp(["P512"], ["L1U"], T.L1U[:], T.P[:, 512:632])
+    for j in range(4):
+        act(["QS"], ["QR4D0"], T.QR4[:, 128 + j:512:4], T.QS[:, 0:96], ACT.Copy)
+    for j in range(4):
+        act(["QR4D0"], ["QRD0"], T.QR16[:, 512 + j:2048:4], T.QR4[:, 128:512], ACT.Copy)
+    mm(["XS", "QS"], "PC", T.PC[:, 0:60, :], T.XS[:], T.QS[:], True, False)
+    quad("UX", ["PH512"], "PC", lambda x: T.PC[:, 0:60, x:8:4], lambda x: T.PH[:, 512:632], False)
+    act(["PC", "SC9", "SC16"], ["QT"], T.QT[:], T.PC[:, 0:60, :], ACT.Identity, col("SC", 9), col("SC", 16))
+    for s in range(S):
+        act(["QT"], ["QTD%d" % s], T.QTH[:, 128 * s + 32:128 * s + 128], T.QT[:, 96 * s:96 * s + 96], ACT.Copy)
+    dma("y", ["QT"], ["TBqD", "TBqR", "TBz"], T.TB[:, 0:256], T.QT[:, 0:256])
+    dma("y", ["QT"], ["TBy"], T.TB[:, 2304:2688], T.QT[:, 0:384])
+
+    TBANK = ("PA", "PB", "LR", "LD")
+    for h in range(2):
+        hb = ("LD", "KC")[h]
+        quad("WX", [XR[h]], hb, lambda x: T[hb][:, 0:256], lambda x: T.XB[:, 256 + 1024 * h + x:1280 + 1024 * h:4])
+        places([hb], T[hb][:, 0:256], 256 * h, 256)
+    for b in range(4):
+        tb = TBANK[b]
+        mm(["CV", "IOT0", "IOT1"], tb, T[tb][:], T.CV[:, 8 * b:8 * b + 8, :], T.IOT[:], True, False)
+        mm(["XS", XR[b // 2]], tb, T[tb][:], T.XS[:], T.XB[:, 256 + 512 * b:768 + 512 * b], False, False)
+        quad("UX", ["PH%d" % (256 * (b // 2))], tb, lambda x: T[tb][..., x::4], lambda x: T.PH[:, 128 * b:128 * b + 128], False)
+        ts([tb, "SC7", "SC8"], [TR[b]], T.TB[:, 256 + 512 * b:768 + 512 * b], T[tb][:], col("SC", 7), col("SC", 8), A.max, A.min)
+
+    ts(["CG", "PF"], ["BD1"], T.BD1[:], T.CG[:, 0:128:16], col("PF", 0), 1024.0, A.is_equal, A.mult)
+    ts(["CG", "PF"], ["BD2"], T.BD2[:], T.CG[:, 0:128:16], col("PF", 0), 2048.0, A.is_equal, A.mult)
+    sset(["QTR0"], T.QTH[:, 0:32], T.QS[:, 0:32], "QS", 4096.0)
+    sset(["PCz", "PC12"], T.PCW[:, 0:256], T.QS[:, 0:256], "QS", -256.0)
+    sset(["PCy"], T.PCW[:, 256:512], T.QS[:, 0:256], "QS", -256.0)
+    sset(["RST"], T.RST[:], T.QS[:, 0:160], "QS", 0.0)
+    sset(["RS16"] + ["CL%d" % h for h in range(1, 8)], T.RS16[:], T.QS[:, 0:128], "QS", 0.0)
+    sset(["MS0"], T.MS[:, 0:160], T.QS[:, 0:160], "QS", 0.0)
+    sset(["RST"], T.RST[:, 0:160:20], T.RST[:, 0:160:20], "RST", -1e9)
+    sset(["RS16"], T.RS16[:, 0:128:16], T.RS16[:, 0:128:16], "RS16", -1e9)
+    for i in range(S - 1):
+        sset(["SB%d" % i], T.SB[:, 256 * i:256 * i + 32], T.QS[:, 0:32], "QS", 512.0)
+    ts(["PIN"], ["PI4"], col("PI", 4), T.PIN[:], 96.0, None, A.add)
+    ts(["CM", "PX"], ["IB"], T.IB[:], T.CM[:], col("PX", 0), None, A.is_equal, None, 0.5)
+    ts(["CM", "PX"], ["IPEN"], T.IPEN[:], T.CM[:], col("PX", 0), PEN, A.is_equal, A.mult, 0.5)
+    ts(["PI4"], ["PI5"], col("PI", 5), col("PI", 4), 127, None, A.bitwise_and)
+    ts(["PI5"], ["SC15"], col("SC", 15), col("PI", 5), -256.0, None, A.add)
+    for t in range(3):
+        ts(["CR", "PF"], ["MASK"], T.MASK[:, 128 * t:128 * t + 128], T.CR[:], col("PF", 1), None, A.is_equal, None, 0.5)
+    ts(["PCz", "LN0", "SC15"], ["PCz"], T.PCW[:, 8:16], T.LN0[:], 0.0, col("SC", 15), A.mult, A.add)
+    ts(["PCz"], ["PCz"], T.PCW[:, 2:4], T.PCW[:, 8:10], 128.0, None, A.add)
+    ts(["PCz", "IO4"], ["PCz"], T.PCW[:, 4:6], T.IO4[:, 4:6], -60000.0, None, A.mult)
+    ts(["CG", "PF"], ["BDB"], T.BDB[:], T.CG[:], col("PF", 0), None, A.is_equal, None, 0.5)
+    ts(["CG", "PF"], ["HI"], T.HI[:, 0:6], T.CG[:, 32:128:16], col("PF", 0), None, A.is_equal)
+    ts(["CG", "PF"], ["HI"], T.HI[:, 6:8], T.CG[:, 0:32:16], col("PF", 0), None, A.is_equal)
+    ts(["LN0", "PF"], ["LN"], T.LN[:], T.LN0[:], col("PF", 1), None, A.add)
+    sel("BDB", "LTB", T.LTB[:], T.BDB[:], [[1, 128]], A.is_gt, 0.0, 0, -1)
+    ts(["CQ", "BX", "SC6"], ["AU"], T.AU[:], T.CQ[:], col("BX", 1), col("SC", 6), A.is_equal, A.mult, 0.5)
+    ts(["CM", "PX", "SC5"], ["AT"], T.AT[:], T.CM[:], col("PX", 0), col("SC", 5), A.is_equal, A.mult, 0.5)
+    tt(["AU", "UX"], ["AU"], T.AU[:], T.AU[:], T.UX[:, 0:128], A.add)
+    tt(["AU", "AT"], ["AM"], T.AM[:], T.AU[:], T.AT[:], A.add)
+    ts(["CQ", "BX"], ["BU"], T.BU[:], T.CQ[:], col("BX", 1), -64.0, A.is_equal, A.mult, 0.5)
+    ts(["CQ", "BX"], ["BT"], T.BT[:], T.CQ[:], col("BX", 2), 64.0, A.is_equal, A.mult, 0.5)
+    tt(["BU", "BT"], ["BM"], T.BM[:], T.BU[:], T.BT[:], A.add)
+    for t in range(3):
+        act(["LN"], ["TRC"], T.TRC[:, 8 * t:8 * t + 8], T.LN[:], ACT.Identity, 2048.0 + 128 * t)
+    act(["LN"], ["TL"], T.TL[:], T.LN[:], ACT.Identity, 128.0)
+    sset(["NTL"], T.NTL[:], T.LN[:], "LN", 256.0)
+    ts(["CR", "PF", "XS"], ["MKA"], T.XT[:], T.CR[:], col("PF", 1), -48640.0, A.is_ge, A.mult, 0.5)
+    act(["MKA"], ["MKB"], T.MKB[:], T.XT[:], ACT.Identity, -2560.0)
+    act(["IB"], ["IB5"], T.IB5[:], T.IB[:], ACT.Identity, 0.0, 5120.0)
+    paint("LTB", T.LTB[:], [[1, 128]], 0, -256.0)
+
+    def repeat(rd, t4, t16, src, o4, n):
+        for j in range(4):
+            sel(rd, t4, T.QR4[:, o4 + j:o4 + 4 * n:4], src, [[0, n]], A.is_equal, 0.0, 0, 0)
+        for j in range(4):
+            sel(t4, t16, T.QR16[:, 4 * o4 + j:4 * o4 + 16 * n:4], T.QR4[:, o4:o4 + 4 * n], [[0, 4 * n]], A.is_equal, 0.0, 0, 0)
+
+    def blocks(name, lo, hi):
+        return ["%s_%d" % (name, k) for k in range(lo // 16, (hi + 15) // 16)]
 
     for s in range(S):
         arrivals = s > 0
         send = s + 1 < S
-        H = 8 if arrivals else 6
-        both = ("D", "R") if arrivals else ("D",)
-        at, qt = "ARR%d" % s, "QR%d" % s
-        arr = T[at] if arrivals else None
-        PL1, PL2, PL3 = (["PLW%d%s" % (l, b) for b in both] for l in (1, 2, 3))
+        at, qd, qr, q0 = "ARR%d" % s, "QRD%d" % s, "QRR%d" % s, 2048 * s
+        a0 = 32 * s
+        arr = T.ARR[:, a0:a0 + 32]
+        QTT = ["QTD%d" % s, "QTR%d" % s]
+        qth = T.QTH[:, 128 * s:128 * s + 128]
+        first = 0 if arrivals else 32
         if arrivals:
-            outside("arr%d" % s, nland, [at])
+            dma("y", ["QT"], ["TBqD"], T.TB[:, 0:96], T.QT[:, 96 * s:96 * s + 96])
             dma("y", [], ["XBqD"], T.XB[:, 0:96], T.qs[:, 96 * s:96 * s + 96])
             dma("y", [], ["OLDqD"], T.OLD[:, 384:480], T.qs[:, 96 * s:96 * s + 96])
-        else:
-            first(0)
-            constants()
+            repeat(at, "QR4R%d" % s, qr, arr, 512 * s, 32)
+            dma("y", [at], ["XBqR"], T.XB[:, 96:128], arr)
+            dma("y", [at], ["OLDqR"], T.OLD[:, 480:512], arr)
+            repeat("QS", "QR4D%d" % s, qd, T.QS[:, 96 * s:96 * s + 96], 512 * s + 128, 96)
 
-        wrapsum("WR", ["OCC1Ds", "OCC1Dv"], "SD", T.SD[:, 0:24], lambda r: T.OCC1[:, r:384:16], True, True)
-        diff(["OCC1Ds", "OCC1Dv"], qt, T.OCC1[:, 0:384], T.QR[:, 6 * s:6 * s + 6, 0:64], 384, T.AB1[:, 0:384], "AB1D")
-        places(["SD"], T.SD[:, 0:24], 24, T.PLW[:, 384:480], "PLW2D")
-        cp(["PLW2D"], ["OF2D"], T.OF[:, 32:128], T.PLW[:, 384:480])
-        gather("s", ["OF2D"], ["OCC2Ds"], T.OCC2[:, 0:768], T.OF[:, 32:80])
-        gather("v", ["OF2D"], ["OCC2Dv"], T.OCC2[:, 768:1536], T.OF[:, 80:128])
-        wrapsum("WR", ["OCC2Ds", "OCC2Dv"], "SD", T.SD[:, 32:128], lambda r: T.OCC2[:, r:1536:16], True, True)
-        for c in range(3):
-            diff((["OCC2Ds"], ["OCC2Ds", "OCC2Dv"], ["OCC2Dv"])[c], qt, T.OCC2[:, 512 * c:512 * c + 512],
-                 T.QR[:, 6 * s + 2 * c:6 * s + 2 * c + 2, 0:256], 512, T.AB2[:, 512 * c:512 * c + 512], "AB2%d" % c)
-        places(["SD"], T.SD[:, 32:128], 96, T.PLW[:, 1536:1920], "PLW3D")
-        cp(["PLW3D"], ["OF3D"], T.OF[:, 160:544], T.PLW[:, 1536:1920])
+        l1 = T.L1U[:, 24 * s:24 * s + 24]
+        gather("s", ["L1U"] + TR, ["G1D"], T.G1[:, 128:512], TW, l1)
+        quad("LX", ["G1D"], "LD", lambda x: T.LD[:, 0:96], lambda x: T.G1[:, 128 + x:512:4])
+        offsets(CVT[0], ["LD"], ["OF2D"], T.OF2[:, 32:128], T.LD[:, 0:96])
+        gather("s", ["OF2D"] + TR, blocks("G2", 96, 128), T.G2[:, 1536:2048], TW, T.OF2[:, 96:128])
+        quad("LX", blocks("G2", 96, 128), "LD", lambda x: T.LD[:, 96:224], lambda x: T.G2[:, 1536 + x:2048:4])
+        offsets(CVT[1], ["LD"], ["OFC"], T.OFC[:], T.LD[:, 96:224])
+        for k, pb in ((32, "PB"), (64, "PA")):
+            gather("s", ["OF2D"] + TR, blocks("G2", k, k + 32), T.G2[:, 16 * k:16 * k + 512], TW, T.OF2[:, k:k + 32])
+            quad("LX", blocks("G2", k, k + 32), pb, lambda x: T[pb][:, 0:4, :], lambda x: T.G2[:, 16 * k + x:16 * k + 512:4])
+            for i in range(4):
+                offsets(CVT[2], [pb], ["OFV%d_%d" % (i, k)], T.OFV[:, 96 * i + k:96 * i + k + 32], T[pb][:, 0:4, i:32:4])
+        gather("v", ["L1U", "QR4D%d" % s] + XR, ["MX1D"], T.MX1[:, 128:512], XW, l1, T.QR4[:, 512 * s + 128:512 * s + 512], A.max)
 
         if arrivals:
-            for k in range(2):
-                sel(at, "QRR", T.QRR[:, k, 0:16], arr[:, 16 * k:16 * k + 16], [[0, 16]], A.is_equal, 0.0, 0, 0)
-            w = 16
-            while w < 512:
-                sel("QRR", "QRR", T.QRR[:, :, w:2 * w], T.QRR[:, :, 0:w], [[0, 2], [0, w]], A.is_equal, 0.0, 0, 0)
-                w *= 2
-            dma("y", [at], ["XBqR"], T.XB[:, 96:128], arr[:])
-            dma("y", [at], ["OLDqR"], T.OLD[:, 480:512], arr[:])
-        if send:
-            w, nt, lo = 16, "QR%d" % (s + 1), 6 * (s + 1)
-            while w < 512:
-                sel(nt, nt, T.QR[:, lo:lo + 6, w:2 * w], T.QR[:, lo:lo + 6, 0:w], [[0, 6], [0, w]], A.is_equal, 0.0, 0, 0)
-                w *= 2
-            dma("y", [nt], ["QX%d" % (s + 1)], T.QR[:, lo:lo + 6, 512:1024], T.QR[:, lo:lo + 6, 0:512])
+            quad("WX", [at], "LR", lambda x: T.LR[:, 0:8], lambda x: T.ARR[:, a0 + x:a0 + 32:4])
+            places(["LR"], T.LR[:, 0:8], 632, 8)
+            cp(["P632"], ["OF1"], T.OF1[:], T.P[:, 632:640])
+            gather("s", ["OF1"] + TR, ["G1R"], T.G1[:, 0:128], TW, T.OF1[:])
+            mm(["XS", at], "KC", T.KC[:, 0:32], T.XS[:], arr, True, False)
+            quad("UX", ["PH632"], "KC", lambda x: T.KC[:, x:32:4], lambda x: T.PH[:, 632:640], False)
+            quad("LX", ["G1R"], "LR", lambda x: T.LR[:, 16:48], lambda x: T.G1[:, x:128:4])
+            act(["KC", "SC9", "SC16"], [QTT[1]], T.QTH[:, 128 * s:128 * s + 32], T.KC[:, 0:32], ACT.Identity, col("SC", 9), col("SC", 16))
+            if send:
+                act(["KC", "SC9", "SC16"], ["TBqR"], T.TB[:, 96:128], T.KC[:, 0:32], ACT.Identity, col("SC", 9), col("SC", 16))
+            offsets(CVT[3], ["LR"], ["OF2R"], T.OF2[:, 0:32], T.LR[:, 16:48])
+            gather("s", ["OF2R"] + TR, blocks("G2", 0, 32), T.G2[:, 0:512], TW, T.OF2[:, 0:32])
+            quad("LX", blocks("G2", 0, 32), "LR", lambda x: T.LR[:, 64:192], lambda x: T.G2[:, x:512:4])
+            for i in range(4):
+                offsets(CVT[4], ["LR"], ["OFV%d_0" % i], T.OFV[:, 96 * i:96 * i + 32], T.LR[:, 64 + i:192:4])
+            gather("v", ["OF1", "QR4R%d" % s] + XR, ["MX1R"], T.MX1[:, 0:128], XW, T.OF1[:], T.QR4[:, 512 * s:512 * s + 128], A.max)
 
-        def df(hi):
-            return T.DF[:, 1024 * hi:1024 * hi + 1024]
+        for k in range(first, 128, PIECE):
+            gather("v", ["OF2R", qr] * (k < 32) + ["OF2D", qd] * (k >= 32) + XR, blocks("MX2", k, k + PIECE), T.MX2[:, 16 * k:16 * (k + PIECE)], XW,
+                   T.OF2[:, k:k + PIECE], T.QR16[:, q0 + 16 * k:q0 + 16 * (k + PIECE)], A.max)
+        for j in range(32):
+            gather("s", ["OFC", "QS"] + XR, ["DFC%d" % j], T.DFC[:, 64 * j:64 * j + 64], XW, T.OFC[:, 4 * j:4 * j + 4], bias=col("QS", 96 * s + 64 + j))
+        for i in range(4):
+            for k in range(first, 96, PIECE):
+                tok = blocks("DF%d" % i, k, k + PIECE)
+                a = T.DFV[:, 1536 * i + 16 * k:1536 * i + 16 * (k + PIECE)]
+                gather("v", ["OFV%d_%d" % (i, k // 32 * 32), qr if k < 32 else qd] + XR, tok, a, XW, T.OFV[:, 96 * i + k:96 * i + k + PIECE],
+                       T.QR16[:, q0 + 16 * k:q0 + 16 * (k + PIECE)], A.subtract)
+                act(tok, tok, a, a, ACT.Abs)
 
-        def p_d(hi):
-            if hi < 6:
-                tt(["OF3D", qt, "QX%d" % s] + XR, ["DF%d" % hi], df(hi),
-                   T.XB[:, 256:2304].indirect(T.OF[:, 160 + 64 * hi:224 + 64 * hi]), T.QR[:, 6 * s + hi, :], A.subtract)
-            else:
-                for c in range(2):
-                    o, l = 1024 * hi + 512 * c, 160 + 64 * hi + 32 * c
-                    tt(["OF3R", "QRR"] + XR, ["DF%d" % hi], T.DF[:, o:o + 512],
-                       T.XB[:, 256:2304].indirect(T.OF[:, l:l + 32]), T.QRR[:, hi - 6, :], A.subtract)
+        G1T, G2T = ["G1D", "G1R"], blocks("G2", 0, 128)
 
-        def p_s(hi):
-            act(["DF%d" % hi], ["DF%d" % hi], df(hi), df(hi), ACT.Abs)
+        def rows(i, j, c, p0=0, p1=128):
+            if i == 3:
+                return T.KC[p0:p1, 5 * j + c:160:20]
+            return T[("KA", "KA", "KB")[i]][p0:p1, 32 * (i == 1) + j:32 * (i == 1) + 32:4, c]
 
-        def p_m(hi):
-            wrapsum("EK", ["DF%d" % hi], "K3", T.K3[:, 64 * hi:64 * hi + 64], lambda r: T.DF[:, 1024 * hi + r:1024 * hi + 1024:16], False, False)
+        mm(QTT + ["RQC"], "PC", T.PC[:, 0:32, :], qth, T.RQC[:], True, False)
+        mm(QTT + ["RQK"], "KA", T.KA[:], qth, T.RQK[:, 0:64, :], True, False)
+        mm(QTT + ["RQK"], "KB", T.KB[:], qth, T.RQK[:, 64:96, :], True, False)
+        mm(QTT + ["RQK"], "KC", T.KC[:, 0:160], qth, T.RQK[:, 96:128, :], True, False)
+        mm(QTT + ["RQP"], "PA", T.PA[:], qth, T.RQP[:, 0:16, :], True, False)
+        mm(QTT + ["RQP"], "PB", T.PB[:], qth, T.RQP[:, 16:32, :], True, False)
+        for i in range(4):
+            r, c = 16 + 8 * (i // 2), 4 * (i % 2)
+            mm(G1T + ["RP2"], "PC", T.PC[:, r:r + 8, c:c + 4], T.G1[:, i:512:4], T.RP2[:, 0:8, :], False, False, True)
+            mm(G1T + ["RK2"], "PC", T.PC[:, 8:12, i:8:4], T.G1[:, i:512:4], T.RK2[:, :, 0], False, False, True)
+        for i in range(4):
+            mm(["MX1D", "MX1R", "BD2"], "PC", T.PC[:, 8:12, i:8:4], T.MX1[:, i:512:4], T.BD2[:], False, i == 3, i < 3)
+        act(["PC"], ["PC12"], T.PCW[:, 32:256], T.PC[:, 4:32, :], ACT.Copy)
+        for h, pb in enumerate(("PA", "PB")):
+            for j in range(8):
+                mm(G2T + ["RP2"], pb, T[pb][:, :, 4 * j:4 * j + 4], T.G2[:, 8 * h + j:2048:16], T.RP2[:], False, j == 7, j < 7)
+            ts([pb], ["FG%d" % h], T.FG[:, 8 * h:8 * h + 8, :], T[pb][:, 8:16, :], 0.0, None, A.is_equal)
+            act([pb], ["PC3" + "ab"[h]], T.PCW[:, 512 + 256 * h:768 + 256 * h], T[pb][:, 0:8, :], ACT.Copy)
+        tt(["PC12"], ["L1"], sm("L1", 0, 16), T.PCW[:, 64:96:2], T.PCW[:, 65:96:2], A.min)
+        tt(["PC12"], ["H1"], sm("H1", 0, 16), T.PCW[:, 64:96:2], T.PCW[:, 65:96:2], A.max)
+        ts(["PC12"], ["MD1"], T.MD[:, 8:16], T.PCW[:, 96:104], 8192.0, DEADKEY, A.is_ge, A.mult)
+        tt(["L1"], ["L2"], sm("L2"), sm("L1", 0, 16, 2), sm("L1", 1, 16, 2), A.min)
+        tt(["H1"], ["H2"], sm("H2"), sm("H1", 0, 16, 2), sm("H1", 1, 16, 2), A.max)
+        ts(["L2"], ["MD0"], T.MD[:, 0:8], sm("L2"), 1024.0, DEADKEY, A.is_lt, A.mult)
+        tt(["H2", "MD1"], ["H3"], sm("H3"), sm("H2"), T.MD[:, 8:16], A.max)
+        tt(["H3", "MD0"], ["MS0"], T.MS[:, 0:160:20], sm("H3"), T.MD[:, 0:8], A.max)
+        for i in range(4):
+            b, o = ("KA", "KA", "KB", "KC")[i], 32 * (i == 1)
+            h, c = i // 2, 16 * (i % 2)
+            fg = ["FG%d" % h, "IPEN"]
+            mm(G1T + ["RK1"], b, T.KC[:, 0:160] if i == 3 else T[b][:, o:o + 32, :], T.G1[:, i:512:4], T.RK1[:], False, False, True)
+            if i < 3:
+                mm(fg, b, T[b][:, o:o + 32, 1:5], T.IPEN[:], T.FG[:, 8 * h:8 * h + 8, c:c + 16], False, False, True)
+            for j in range(4):
+                g2 = T.G2[:, 4 * i + j:2048:16]
+                if i < 3:
+                    mm(G2T + ["RK2"], b, T[b][:, o + j:o + 32:4, :], g2, T.RK2[:], False, False, True)
+                    continue
+                for k in range(5):
+                    mm(G2T + ["RK2"], b, rows(i, j, k), g2, T.RK2[:, :, k], False, False, True)
+                for k in range(4):
+                    mm(fg, b, rows(i, j, 1 + k), T.IPEN[:], T.FG[:, 8:16, 16 + 4 * j + k], False, False, True)
+            for r in range(16):
+                mm(["DFC%d" % k for k in range(32)] + ["BD1"], b, rows(i, r // 4, 1 + r % 4, 96), T.DFC[:, 16 * i + r:2048:64], T.BD1[:],
+                   False, False, True)
+                mm(blocks("DF%d" % i, 0, 96) + ["BD1"], b, rows(i, r // 4, 1 + r % 4, 0, 96), T.DFV[:, 1536 * i + r:1536 * i + 1536:16], T.BD1[:],
+                   False, False, True)
+            for j in range(4):
+                last = j == 3 and i != 0
+                mm(blocks("MX2", 0, 128) + ["BD2"], b, rows(i, j, 0), T.MX2[:, 4 * i + j:2048:16], T.BD2[:], False, last, not last)
+        for i in range(3):
+            b, o = ("KA", "KA", "KB")[i], 32 * (i == 1)
+            tt([b, "MS%d" % i], ["MS%d" % (i + 1)], T.MS[:, 160 * i + 160:160 * i + 320], T[b][:, o:o + 32, :], T.MS[:, 160 * i:160 * i + 160], A.max)
+        runmax(["MS3", "RST"], ["MS4"], T.MS[:, 640:800], T.RST[:], T.MS[:, 480:640])
+        runmax(["KC", "RST"], ["MS5"], T.MS[:, 800:960], T.RST[:], T.KC[:, 0:160])
 
-        def p_g(hi):
-            k = 1024 * (hi % 2)
-            gather("s", ["OF3D" if hi < 6 else "OF3R"], ["OCC3%d" % (hi % 2)], T.OCC3[:, k:k + 1024], T.OF[:, 160 + 64 * hi:224 + 64 * hi])
-
-        def p_x(hi):
-            if hi == 1:
-                diff(["OCC1R"], "QRR", T.OCC1[:, 384:512], T.QRR[:, :, 0:64], 128, T.AB1[:, 384:512], "AB1R")
-                return
-            for c in range(2):
-                o, k = 1024 * hi + 512 * c, 1024 * (hi % 2) + 512 * c
-                reps = T.QR[:, 6 * s + hi, 0:512] if hi < 6 else T.QRR[:, hi - 6, :]
-                diff(["OCC3%d" % (hi % 2)], qt if hi < 6 else "QRR", T.OCC3[:, k:k + 512], reps, 512, T.DF[:, o:o + 512], "DF%d" % hi)
-
-        def p_rq():
-            mm(["WBD", at], "SR", T.SR[:, 0:32], T.WBD[:], arr[:], True, True)
-            tt(["MASK", "SR"], ["RS"], T.RS[:], T.SR[:, 0:32], T.MASK[:, 0:32], A.mult)
-            tt(["MASK", at], ["RE"], T.RE[:], arr[:], T.MASK[:, 0:32], A.mult)
-            for k in range(2):
-                red(["RS"], ["RQ"], T.RQ[:, k:k + 1], T.RS[:, 16 * k:16 * k + 16], A.add)
-            places(["RQ"], T.RQ[:], 2, T.PLW[:, 120:128], "PLW1R")
-            cp(["PLW1R"], ["OF1R"], T.OF[:, 24:32], T.PLW[:, 120:128])
-            gather("s", ["OF1R"], ["OCC1R"], T.OCC1[:, 384:512], T.OF[:, 24:32])
-            wrapsum("WR", ["OCC1R"], "SR", T.SR[:, 32:40], lambda r: T.OCC1[:, 384 + r:512:16], True, True)
-            for k in range(2):
-                red(["RE"], ["RF"], T.RF[:, k:k + 1], T.RE[:, 16 * k:16 * k + 16], A.add)
-            ts(["RF"], ["NEQ"], T.NEQ[:, 6:8], T.RF[:], 512.0, None, A.is_lt)
-
-        def p_r2():
-            places(["SR"], T.SR[:, 32:40], 8, T.PLW[:, 480:512], "PLW2R")
-            cp(["PLW2R"], ["OF2R"], T.OF[:, 128:160], T.PLW[:, 480:512])
-            gather("s", ["OF2R"], ["OCC2R"], T.OCC2[:, 1536:2048], T.OF[:, 128:160])
-            wrapsum("WR", ["OCC2R"], "SR", T.SR[:, 64:96], lambda r: T.OCC2[:, 1536 + r:2048:16], True, True)
-            diff(["OCC2R"], "QRR", T.OCC2[:, 1536:2048], T.QRR[:, :, 0:256], 512, T.AB2[:, 1536:2048], "AB23")
-
-        def p_r3():
-            places(["SR"], T.SR[:, 64:96], 32, T.PLW[:, 1920:2048], "PLW3R")
-            cp(["PLW3R"], ["OF3R"], T.OF[:, 544:672], T.PLW[:, 1920:2048])
-
-        def p_lc():
-            ts(["IO16", "PMF"], ["MASK"], T.MASK[:], T.IO16[:], T.PMF[:, 0:1], None, A.is_equal)
-            for t, c in enumerate((0.0, 128.0, 2304.0)):
-                ts(["LN"], ["TRC"], T.TRC[:, 8 * t:8 * t + 8], T.LN[:], c, None, A.add)
-                ts(["LN"], ["TRD"], T.TRD[:, 8 * t:8 * t + 8], T.LN[:], -1.0, 256.0 - c, A.mult, A.add)
-            ts(["LN"], ["TL"], T.TL[:], T.LN[:], 128.0, None, A.add)
-            ts(["TL"], ["NTL"], T.NTL[:], T.TL[:], -1.0, None, A.mult)
-            vset("CL0", T.CL[:], 0.0)
-            ts(["IO16", "PMF"], ["MKB"], T.MKB[:], T.IO16[:, 0:64], T.PMF[:, 0:1], -16.0, A.is_ge, A.mult)
-            for i in range(S - 1):
-                vset("SB%d" % i, T["SB%d" % i][:], 512.0)
-            vset("OLDqR", T.OLD[:, 480:512], 0.0)
-            sel("BDB", "LTB", T.LTB[:], T.BDB[:], [[1, 128]], A.is_gt, 0.0, 0, -1)
-
-        def p_k3():
-            mm(["IOFF", "ONE"], "K3", T.K3[:, 0:64 * H], T.IOFF[:], T.ONE[:, 0:64 * H], True, False)
-            mm(["IH", "IX3"], "K3", T.K3[:, 0:64 * H], T.IH[:], T.IX3[:, 0:64 * H], False, False)
-
-        def p_k1():
-            mm(["IOFF", "ONE"], "K12", T.K12[:, 0:H, 0:4], T.IOFF[:], T.ONE[:, 0:4 * H], True, False)
-            mm(["IH", "IX12"], "K12", T.K12[:, 0:H, 0:4], T.IH[:], T.IX12[:, 0:H, 0:4], False, False)
-            wrapsum("EK", ["AB1" + b for b in both], "K12", T.K12[:, 0:H, 0:4], lambda r: T.AB1[:, r:64 * H:16], False, True)
-
-        def p_fe():
-            ts(["K12"], ["FE1"], T.FE1[:, 0:4 * H], T.K12[:, 0:H, 0:4], 0.0, None, A.is_ge)
-            ts(["K12"], ["NH"], T.NH[:, 0:H, :], T.K12[:, 0:H, 0:4], OFFS + E11, None, A.is_ge)
-
-        def p_fq():
-            for a in range(4):
-                tt(PL2 + PL1, ["FQ2"], T.FQ2[:, a:16 * H:4], T.PLW[:, 384 + a:384 + 16 * H:4], T.PLW[:, 96:96 + 4 * H], A.is_equal)
-
-        def p_k2():
-            mm(["IOFF", "ONE"], "K12", T.K12[:, 0:H, 4:20], T.IOFF[:], T.ONE[:, 0:16 * H], True, False)
-            mm(["IH", "IX12"], "K12", T.K12[:, 0:H, 4:20], T.IH[:], T.IX12[:, 0:H, 4:20], False, False)
-            wrapsum("EK", ["AB2%d" % i for i in range(H // 2)], "K12", T.K12[:, 0:H, 4:20], lambda r: T.AB2[:, r:256 * H:16], False, False)
-            for a in range(4):
-                mm(["IPEN", "FE1"], "K12", T.K12[:, 0:H, 4 + a:20:4], T.IPEN[:], T.FE1[:, 0:4 * H], False, False)
-            mm(["IPEN", "FQ2"], "K12", T.K12[:, 0:H, 4:20], T.IPEN[:], T.FQ2[:, 0:16 * H], False, True)
-
-        def p_fa():
-            for f, c, o in (("FA", 0.0, A.is_ge), ("FB", OFFS, A.is_lt)):
-                ts(["K12"], [f], T[f][:, 0:16 * H], T.K12[:, 0:H, 4:20], c, None, o)
-
-        def p_p12():
-            for a in range(4):
-                for f in ("FA", "FB"):
-                    mm(["IPEN", f], "K3", T.K3[:, a:64 * H:4], T.IPEN[:], T[f][:, 0:16 * H], False, False)
-
-        def p_ph():
-            cp(PL1, ["PH1"], T.PH[:, 0:4 * H], T.PLW[:, 96:96 + 4 * H])
-            cp(PL2, ["PH2"], T.PH[:, 32:32 + 16 * H], T.PLW[:, 384:384 + 16 * H])
-            mm(["IH", "PH2"], "OT", T.OT[:, 0:16 * H], T.IH[:], T.PH[:, 32:32 + 16 * H], True, True)
-            for a in range(4):
-                mm(["IH", "PH1"], "OT", T.OT[:, 128 + a:128 + 16 * H:4], T.IH[:], T.PH[:, 0:4 * H], True, True)
-
-        def p_fp():
-            for a in range(4):
-                tt(PL3 + ["OT"], ["FP"], T.FP[:, a:64 * H:4], T.PLW[:, 1536 + a:1536 + 64 * H:4], T.OT[:, 0:16 * H], A.is_equal)
-
-        def p_fg():
-            for a in range(4):
-                tt(PL3 + ["OT"], ["FG"], T.FG[:, a:64 * H:4], T.PLW[:, 1536 + a:1536 + 64 * H:4], T.OT[:, 128:128 + 16 * H], A.is_equal)
-
-        def p_pp():
-            mm(["IPEN", "FP"], "K3", T.K3[:, 0:64 * H], T.IPEN[:], T.FP[:, 0:64 * H], False, False)
-
-        def p_pg():
-            mm(["IPEN", "FG"], "K3", T.K3[:, 0:64 * H], T.IPEN[:], T.FG[:, 0:64 * H], False, True)
-
-        def p_lv():
-            tt(["NH"], ["N1"], T.N1[:], T.NH[:, :, 0:2], T.NH[:, :, 2:4], A.mult)
-            tt(["N1"], ["LV"], T.LV[:], T.N1[:, :, 0], T.N1[:, :, 1], A.mult)
-            tt(["LV", "NEQ"], ["LIVE"], T.LIVE[:], T.LV[:], T.NEQ[:], A.mult)
-            ts(["LIVE"], ["MD"], T.MD[:], T.LIVE[:], -33554432.0, 16777216.0, A.mult, A.add)
-            ts(["LIVE"], ["DEAD"], T.DEAD[:], T.LIVE[:], -16.0, 16.0, A.mult, A.add)
-
-        def p_r12():
-            for hi in range(H):
-                red(["K12"], ["M12"], T.M12[:, hi:hi + 1], T.K12[:, hi, :], A.max)
-            tt(["M12", "MD"], ["ML12"], T.ML12[:], T.M12[:], T.MD[:], A.max)
-
-        by_block = {"d": p_d, "s": p_s, "m": p_m, "g": p_g, "x": p_x}
-        whole = {"rq": p_rq, "r2": p_r2, "r3": p_r3, "lc": p_lc, "k3": p_k3, "k1": p_k1, "fe": p_fe, "fq": p_fq, "k2": p_k2, "fa": p_fa,
-                 "p12": p_p12, "fp": p_fp, "fg": p_fg, "pp": p_pp, "ph": p_ph, "pg": p_pg, "lv": p_lv, "r12": p_r12}
-        for w in ORDER.split():
-            if w == "lc" and s > 0:
-                continue
-            if not arrivals and (w in ("rq", "r2", "r3", "x1") or w[0] in "dsmgx" and w[1:] in ("6", "7")):
-                continue
-            if w in whole:
-                whole[w]()
-            else:
-                by_block[w[0]](int(w[1:]))
-
-        for hi in range(H):
-            red(["K3"], ["M3"], T.M3[:, hi:hi + 1], T.K3[:, 64 * hi:64 * hi + 64], A.max)
-        tt(["ML12", "M3"], ["MI"], T.MI[:], T.ML12[:], T.M3[:], A.max)
-        ts(["MI"], ["PG"], T.PG[:], T.MI[:], 4, 127, A.arith_shift_right, A.bitwise_and)
-        ts(["MI"], ["PO"], T.PO[:, 0:8], T.MI[:], 2047, None, A.bitwise_and)
-        ts(["MI"], ["PO"], T.PO[:, 8:16], T.MI[:], 2, 511, A.arith_shift_right, A.bitwise_and)
-        tt(["PG", "BH"], ["PO"], T.PO[:, 16:24], T.PG[:], T.BH[:], A.max)
+        tt(["MS4", "MS5"], ["MI"], T.MI[:], T.MS[:, 659:800:20], T.MS[:, 819:960:20], A.max)
+        for t in range(3):
+            ts(["MI"], ["PO"], T.PO[:, 8 * t:8 * t + 8], T.MI[:], 2 * t, 1023 >> 2 * t, A.arith_shift_right, A.bitwise_and)
         cp(["PO"], ["POU"], T.POU[:], T.PO[:])
-        ts(["MI"], ["NE"], T.NE[:], T.MI[:], 0.0, None, A.is_lt)
-        tt(["POU", "MASK", "PLW0", "PLWA", "PLWB"] + PL1 + PL2 + PL3, ["SELM"],
-           T.SELM[:], T.PLW[:, 0:2048].indirect(T.POU[:, 0:24]), T.MASK[:], A.mult)
-        mm(["BDH", "SELM"], "OT", T.OT[:], T.BDH[:], T.SELM[:], True, True)
+        PCT = ["MASK", "PCz", "PCy", "PC12", "PC3a", "PC3b"]
+        gather("v", ["POU"] + PCT, ["SELM"], T.SELM[:], T.PCW[:], T.POU[:], T.MASK[:], A.mult)
         for r in range(16):
-            mm(["IH", "SELM"], "OW", T.OW[:, 0:24], T.IH[:], T.SELM[:, r:384:16], r == 0, r == 15)
-        cp(["OT"], ["OTHH"], T.OTHH[:], T.OT[:])
-        ts(["OW"], ["XL"], T.XL[:], T.OW[:, 0:24], 256.0, None, A.add)
-        xall = XR + ["XBqD", "XBqR", "XBq", "XBt", "XBt2"]
+            mm(["HI", "SELM"], "LR", T.LR[0:24, r:128:16], T.SELM[:, r:384:16], T.HI[:], True, True)
+        for t in range(3):
+            mm(["HI", "SELM"], "PC", T.PC[:, t, :], T.SELM[:, 128 * t:128 * t + 128], T.HI[:], True, True)
+        cp(["LR"], ["TH"], T.TH[0:24, :], T.LR[0:24, 0:128])
+        for t in range(3):
+            mm(["ST", "TH"], "LD", T.LD[:, 128 * t:128 * t + 128], T.ST[0:24, 128 * t:128 * t + 128], T.TH[0:24, :], True, True)
+        ts(["PC"], ["XL"], T.XL[:], T.PC[:, 0:3, :], 256.0, None, A.add)
+        ts(["PC"], ["DEAD"], T.DEAD[:], T.PC[:, 0, :], 0.0, 16.0, A.is_lt, A.mult)
+        cp(["LD"], ["OTHH"], T.OTHH[:], T.LD[:, 0:384])
+        if send:
+            ts(["MI"], ["NEU"], T.NEU[:], T.MI[:], 4194304.0, 4.0, A.is_ge, A.add)
+            gather("v", ["NEU"] + PCT, ["SELN"], T.SELN[:], T.PCW[:], T.NEU[:], T.MASK[:, 0:128], A.mult)
+            mm(["HI", "SELN"], "KB", T.KB[:, 0:8, 0], T.SELN[:], T.HI[:], True, True)
+            gather("s", ["XL"] + tall, ["OLDT"], T.OLDT[:], T.TB[:], T.XL[:, 8:24])
+            mm(["BM", "OTHH"], "PA", T.PA[:, 0:12, :], T.BM[:], T.OTHH[:], True, False)
+            mm(["AM"] + QTT, "PA", T.PA[:, 8:11, :], T.AM[:], T.QTH[:, 128 * s + 32:128 * s + 128], False, False)
+            mm(["AM"] + QTT, "PA", T.PA[:, 11, :], T.AM[:], T.QTH[:, 128 * s:128 * s + 32], False, False)
+            mm(["AM", "OLDT"], "PA", T.PA[:, 0:8, :], T.AM[:], T.OLDT[:], False, True)
+            ts(["PA", "SC7", "SC8"], ["NEWT"], T.NEWT[:], T.PA[:, 0:12, :], col("SC", 7), col("SC", 8), A.max, A.min)
+        gather("s", ["XL"] + xall, ["OLD"], T.OLD[:, 0:384], T.XB[:], T.XL[:])
 
-        def own_blocks(h0):
-            out = T.DB[:, 16 * h0:16 * h0 + 64]
-            mm(["IB", "MKB"], "DB", out, T.IB[:], T.MKB[:], True, False)
-            mm(["IB", "DEAD"], "DB", T.DB[:, 16 * h0:16 * h0 + 64:16], T.IB[:], T.DEAD[:, h0:h0 + 4], False, False)
-            for k in range(9):
-                mm(["IB"] + ["EQ%d" % h for h in range(h0, h0 + 4)], "DB", out, T.IB[:],
-                   T.EQ[:, 8 * k + h0:8 * k + h0 + 4, 112:128], False, k == 8)
-
-        for hi in range(7, -1, -1):
+        mm(["IB", "MKB"], "LD", T.LD[:, 384:512], T.IB[:], T.MKB[:], True, False)
+        mm(["IB5", "DEAD"], "LD", T.LD[:, 384:512:16], T.IB5[:], T.DEAD[:], False, False)
+        for hi in range(8):
             n = 16 * (hi + 1)
             for t in range(3):
-                ts(["OTHH", "OW"], ["EQ%d" % hi], T.EQ[:, 24 * t + hi:24 * t + hi + 17:8, 128 - n:128], T.OTHH[:, :, 0:n],
-                   T.OW[:, 8 * t + hi:8 * t + hi + 1], None, A.is_equal)
-            if hi >= SCAL:
-                k = 9 * (hi - SCAL)
-                op("s", ["EQ%d" % hi], ["CL%d" % hi, "JK%d" % hi], lambda e: e.activation(
-                    T.JK[:, k:k + 9, 0:16 * hi], T.EQ[:, hi:72:8, 112 - 16 * hi:112], ACT.Copy, accum_out=T.CL[:, hi:hi + 1]))
-            elif hi > 0:
-                for k in range(9):
-                    mm(["IB", "EQ%d" % hi], "DA", T.DA[:, 64 * hi:80 * hi], T.IB[:], T.EQ[:, 8 * k + hi, 112 - 16 * hi:112], k == 0, k == 8)
-            if hi in (4, 0):
-                own_blocks(hi)
-        act(["XL"] + xall, ["OLD"], T.OLD[:, 0:384], T.XB[:, 0:2432].indirect(T.XL[:, 0:24]), ACT.Copy)
-        tt(["OW", "TRD"], ["W1"], T.W1[:], T.OW[:, 0:24], T.TRD[:], A.add)
-        for hi in range(SCAL - 1, 0, -1):
-            red(["DA"], ["CL%d" % hi], T.CL[:, hi:hi + 1], T.DA[:, 64 * hi:80 * hi], A.max)
-        for hi in range(7, -1, -1):
-            red(["DB"], ["CFM"], T.CFM[:, hi:hi + 1], T.DB[:, 16 * hi:16 * hi + 16], A.max)
-        tt(["CFM", "CL0"] + ["CL%d" % h for h in range(1, 8)], ["CFX"], T.CFX[:], T.CFM[:], T.CL[:], A.max)
-        ts(["CFX"], ["GO"], T.GO[:], T.CFX[:], 0.5, None, A.is_lt)
-        if send:
-            tt(["GO", "NE"], ["ND"], T.ND[:], T.GO[:], T.NE[:], A.mult)
-            mm(["IH", "NTL"], "OW", T.OW[:, 32:40], T.IH[:], T.NTL[:], True, False)
-            mm(["LTB", "ND"], "OW", T.OW[:, 32:40], T.LTB[:], T.ND[:], False, False)
-            for d in range(1, 8):
-                mm(["BDB", "ND"], "OW", T.OW[:, 32 + d:40], T.BDB[:], T.ND[:, 0:8 - d], False, d == 7)
+                ts(["OTHH", "PC"], ["EQ%d" % hi], T.EQ[:, 24 * t + hi:24 * t + hi + 17:8, 128 - n:128], T.OTHH[:, :, 0:n],
+                   T.PC[:, t, hi:hi + 1], None, A.is_equal, None, 0.5)
+        for hi in range(1, 8):
+            k, cl = 9 * (hi - 1), col("RS16", 16 * hi + 15)
+            if hi in ON_PE:
+                pb = ("LR", "KC")[ON_PE.index(hi)]
+                for j in range(9):
+                    mm(["IB", "EQ%d" % hi], pb, T[pb][:, 128:128 + 16 * hi], T.IB[:], T.EQ[:, 8 * j + hi, 112 - 16 * hi:112], j == 0, j == 8)
+                count([pb], ["CL%d" % hi, "JK%d" % hi], T.JK[:, k, 0:16 * hi], T[pb][:, 128:128 + 16 * hi], cl)
+            else:
+                count(["EQ%d" % hi], ["CL%d" % hi, "JK%d" % hi], T.JK[:, k:k + 9, 0:16 * hi], T.EQ[:, hi:72:8, 112 - 16 * hi:112], cl)
+        for h0 in (4, 0):
+            for k in range(9):
+                last = h0 == 0 and k == 8
+                mm(["IB5"] + ["EQ%d" % h for h in range(h0, h0 + 4)], "LD", T.LD[:, 384 + 16 * h0:448 + 16 * h0], T.IB5[:],
+                   T.EQ[:, 8 * k + h0:8 * k + h0 + 4, 112:128], False, last, not last)
+        runmax(["LD", "RS16"] + ["CL%d" % h for h in range(1, 8)], ["CFS"], T.CFS[:], T.RS16[:], T.LD[:, 384:512])
+        met = T.CFS[:, 15:128:16]
         for t in range(3):
-            tt(["GO", "W1"], ["W2"], T.W2[:, 8 * t:8 * t + 8], T.W1[:, 8 * t:8 * t + 8], T.GO[:], A.mult)
-        tt(["W2", "TRC"], ["W3"], T.W3[:], T.W2[:], T.TRC[:], A.add)
-        cp(["W3"], ["DLU"], T.DLU[:], T.W3[:])
-        op("v", ["DLU", "OLD", "OLDqD", "OLDqR"], xall,
-           lambda e: e.tensor_copy(T.XB[:, 0:2432].indirect(T.DLU[:, 0:24]), T.OLD[:, 128:512]))
+            tt(["CFS", "PC"], ["W2"], sm("W2", 8 * t, 8 * t + 8), T.PC[:, t, :], met, A.max)
+        tt(["W2", "TRC"], ["W3"], sm("W3", 0, 24), sm("W2", 0, 24), T.TRC[:], A.min)
+        ts(["W3"], ["DLU"], T.DLU[:], sm("W3", 0, 24), 256.0, None, A.add)
         if send:
-            first(s + 1)
+            tt(["CFS", "KB"], ["ND"], T.ND[:], met, T.KB[:, 0:8, 0], A.is_lt)
+            mm(["IB", "NTL"], "KC", T.KC[:, 0:8], T.IB[:], T.NTL[:], True, False)
+            mm(["LTB", "ND"], "KC", T.KC[:, 0:8], T.LTB[:], T.ND[:], False, False)
+            for d in range(1, 8):
+                mm(["BDB", "ND"], "KC", T.KC[:, d:8], T.BDB[:], T.ND[:, 0:8 - d], False, d == 7)
             sb = "SB%d" % s
-            tt(["OW", "ND"], ["D2"], T.D2[:], T.OW[:, 32:40], T.ND[:], A.mult)
-            tt(["D2", "TL"], ["D3"], T.D3[:], T.D2[:], T.TL[:], A.add)
-            cp(["D3"], ["SLU"], T.SLU[:], T.D3[:])
-            op("v", ["SLU", "OLD"], [sb], lambda e: e.tensor_copy(T[sb][:, 0:256].indirect(T.SLU[:, 0:8]), T.OLD[:, 0:128]))
-            before("g", [sb], [])
-            g.remote_dma(T["ARR%d" % (s + 1)][:], T[sb][:, 0:32], T.sem["arr%d" % (s + 1)], T.sem.sent, pid, rid, wire)
+            tt(["KC", "TL"], ["D3"], sm("D3"), T.KC[:, 0:8], T.TL[:], A.min)
+            cp(["D3"], ["SLU"], T.SLU[:], sm("D3"))
+            scatter(["DLU", "NEWT"], tall, T.TB[:], T.DLU[:], T.NEWT[:])
+            scatter(["SLU", "OLD"], [sb], T.SB[:, 256 * s:256 * s + 256], T.SLU[:], T.OLD[:, 0:128])
+            calls.append({"q": "g", "rd": [sb], "wr": ["ARR%d" % (s + 1)], "cost": 0.5, "late": FAR, "kind": "far", "ev": ("arr%d" % (s + 1), nland, "far"),
+                          "call": lambda e, k=s: e.remote_dma(T.ARR[:, 32 * k + 32:32 * k + 64], T.SB[:, 256 * k:256 * k + 32],
+                                                              T.sem["arr%d" % (k + 1)], T.sem.sent, pid, rid, wire)})
+        scatter(["DLU", "OLD", "OLDqD", "OLDqR"], xall, T.XB[:], T.DLU[:], T.OLD[:, 128:512])
     dma("y", XR, ["y0"], T.y[:, 0:1024], T.XB[:, 256:1280])
     dma("s", XR, ["y1"], T.y[:, 1024:2048], T.XB[:, 1280:2304])
+    issue(g, T, calls)
     g.wait_ge(T.sem.sent, nwire * (S - 1))
-    finish()

@@ -6,23 +6,37 @@ X = AxisListType.X
 S = 5
 PEN = -16777216.0
 DEADKEY = 12582912.0
-ON_PE = (7, 6)
-CVT = "ssvsv"
+ON_PE = (7, 6, 5)
+FIXED = {"v": "-D3 -TB0 -SB# -XB0 MX1D MX2_2 MX2_6 MX2_4 OF3_2 DF8 OF3_1 DF9a UI632 DF4a U632 DF9b Z632 Y632 DF4b P632 DF5a OF1 PH632 DF5b MX1R DF6 "
+              "MX2_0 DF10 OF3_0 L1 DF1 L2 FG1 MD0 H3 FG0 DF0 DF2 MS0 DF11 DF3 MS1 MS2 MS3 POU SELM SELN OTHH EQ4 EQ7 EQ3 EQ6 EQ5 EQ2 EQ1 EQ0",
+         "s": "G1D OF2D G2_6 G2_4 OF3_3 G2_2 DF14 DF12 OCC3 DF13 G1R DF7 TBqR OF2R QTR# G2_0 DF4 PC12 DF8 DF15 DF10 DF5 DF6 DF1 DF9 DF0 DF2 "
+              "DF11 DF3 PC3b PC3a"}
+FIXED0 = {"v": "MX1D MX2_6 MX2_4 MX2_2 DF8 DF4 DF9 DF5 DF10 DF6 DF11 DF7 POU SELM SELN OTHH EQ4 EQ7 EQ3 EQ6 EQ5 EQ2 EQ1 EQ0",
+          "s": "G1D OF2D G2_6 G2_4 OF3_3 G2_2 DF12 PC12 DF15"}
+MODE = ("ssss", "sssp", "ssss", "c")
+MODE0 = ("", "vsss", "vsss", "c")
+WIDE = (3, 3, 3, 0)
+G2Q0 = "ssss"
+G2Q = "ssss"
+CVT = "svvvss"
 PIECE = 32
-CYC, PEC, GATHER, SCATTER, HOP, LOCAL, FAR = 0.00083, 0.0005, 1.6, 3.8, 0.2, 2.2, 3.2
-SLACK, ROUNDS, JIT = 0.1, 6, 0.3
+CYC, PEC, GATHER, SCATTER, HOP, LOCAL, FAR = 0.00083, 0.00045, 1.56, 3.8, 0.22, 2.2, 4.6
+SLACK, ROUNDS, KEEP, GAIN = 0.1, 4, 3, (-0.3, 0.0, 0.1)
+RUN = 0.65
+HALVES = ("DF9", "DF4", "DF5")
+MARGIN = {"OF3_0": 1.0, "FG0": 1.0, "FG1": 1.0, "MS2": 1.0, "MS3": 0.5}
 PLANNED = {}
 
 SCRATCH = {}
 for _t, _l in (
-        ("bfloat16", "XB:2688 QS:480 WTS:1 CQ:128 CM:128 CG:128 CR:128 WX:512 XS:128 XT:128 XU:128 IB:128 IB5:128 IPEN:128 BDB:128 LTB:128 MKB:128 BD2:8"
+        ("bfloat16", "XB:2688 QS:480 WTS:1 CQ:128 CM:128 CG:128 CR:128 WX:512 XS:128 XT:128 XU:128 IB:128 IB5:128 NIB:128 OCC:2048 IPEN:128 BDB:128 LTB:128 MKB:128 BD2:8"
                      " QR4:2560 QR16:10240 MX1:512 MX2:2048 OLD:512 ND:8 NTL:8 DEAD:8 MASK:384 SB:1024 ARR:160"),
-        ("float16", "LX:512 UX:512 AM:128 AT:128 AU:128 BM:128 BT:128 BU:128 IOT:512 BD1:8 HI:8 ST:384 G1:512 G2:2048 DFV:6144 DFC:2048 QTH:640 PH:640"
-                    " SELM:384 SELN:128 TH:128 OLDT:256"),
+        ("float16", "LX:512 UX:512 AM:128 AT:128 AU:128 BM:128 BT:128 BU:128 IOT:512 BD1:8 BDN:8 HI:8 ST:384 G1:512 G2:2048 DF:8192 RL:8192 QTH:640 PH:640"
+                    " ONE:128 RQS:32 SELM:384 SELN:128 TH:128 OLDT:256"),
         ("float32", "TB:2688 QT:480 PCW:1024 NEWT:384 MS:960 RST:160 RS16:128 CFS:128 IOF:512 KF:4 KM:4 KC1:4 PF:4 IO4:8 PX:4 BX:4 EX:4 EA:4 SC:18"
                     " LN0:8 LN:8 TRC:24 TL:8 SM:512 MD:16"),
         ("int32", "KKI:4 PIN:1 PI:6 UI:640 U:640 Z:640 Y:640 P:640 MI:8 PO:24"),
-        ("uint16", "L1U:120 OF1:8 OF2:128 OFV:384 OFC:128 POU:24 NEU:8 XL:24 DLU:24 SLU:8")):
+        ("uint16", "L1U:120 OF1:8 OF2:128 OF3:512 POU:24 NEU:8 XL:24 DLU:24 SLU:8")):
     for _w in _l.split():
         SCRATCH[_w.split(":")[0]] = ("sbuf", [128, int(_w.split(":")[1])], _t)
 for _n, _s, _t in (("CA", [8, 16], "bfloat16"), ("MAS", [8, 16], "float16"), ("CV", [32, 16], "float16"), ("RK1", [32, 5], "float16"),
@@ -37,6 +51,16 @@ SEMAPHORES = ["cv", "cs", "cp", "cg", "sent"] + ["arr%d" % (i + 1) for i in rang
 
 
 def plan(calls):
+    runs = []
+    for i, c in enumerate(calls):
+        r = runs[-1] if runs else None
+        if r and (r["q"], r["rd"], r["wr"], r["kind"]) == (c["q"], c["rd"], c["wr"], "op") and r["cost"] + c["cost"] < RUN and not set(c["rd"]) & set(c["wr"]):
+            r["cost"] += c["cost"]
+            r["ids"].append(i)
+        else:
+            runs.append(dict(c, ids=[i], margin=max([MARGIN.get(t, 0.0) for t in c["wr"]] + [0.0])))
+    calls = runs
+    run = {i: k for k, r in enumerate(runs) for i in r["ids"]}
     n = len(calls)
     preds, writer, readers = [], {}, {}
     for i, c in enumerate(calls):
@@ -54,6 +78,8 @@ def plan(calls):
             for t in c["rd"]:
                 if t in BANKS and t in writer and calls[writer[t]]["q"] == "p":
                     p[writer[t]] = 0.0
+        for k in c.get("behind", []):
+            p.setdefault(run[k], -calls[run[k]]["late"])
         p.pop(i, None)
         preds.append(p)
         for t in c["rd"]:
@@ -65,9 +91,9 @@ def plan(calls):
     for i, p in enumerate(preds):
         for j, lat in p.items():
             succ[j].append((i, lat + calls[j]["late"]))
-            back[i].append((j, lat + calls[j]["late"]))
+            back[i].append((j, lat + calls[j]["late"] + calls[j]["margin"]))
 
-    def walk(after, way):
+    def walk(after, way, gain, early):
         left = [0] * n
         for i in range(n):
             for j, _ in after[i]:
@@ -78,17 +104,19 @@ def plan(calls):
         order = []
         while len(order) < n:
             pick = None
+            goal = max([max(free[q], ready[i]) + way[i] for q in free for i in may[q]]) - gain
             for q in free:
                 if not may[q]:
                     continue
-                top = None
-                may[q].sort(key=lambda k: -way[k])
+                top, limit = None, 1e9
+                may[q].sort(key=lambda k: -way[k] - early[k])
                 for i in may[q]:
                     t = max(free[q], ready[i])
-                    if top is None or t < top[0] and t + calls[i]["cost"] <= top[0] + SLACK:
+                    if top is None or t < top[0] and t + calls[i]["cost"] <= limit:
                         top = (t, i)
                         if t == free[q]:
                             break
+                    limit = min(limit, max(t + SLACK, goal - way[i] - early[i]))
                 if pick is None or top < pick:
                     pick = top
             t, i = pick
@@ -103,17 +131,16 @@ def plan(calls):
                     may[calls[j]["q"]].append(j)
         return order, end
 
-    way = [0.0] * n
-    for i in range(n - 1, -1, -1):
-        way[i] = calls[i]["cost"] + max([lat + way[j] for j, lat in succ[i]] + [0.0])
+    way = walk(back, [0.0] * n, 0.0, [0.0] * n)[1]
     best = None
+    early = [c.get("early", 0.0) for c in calls]
     for k in range(ROUNDS):
-        order, end = walk(succ, way)
+        order, end = walk(succ, way, GAIN[k % len(GAIN)], early)
         if best is None or max(end) < best[0]:
             best = (max(end), order, end)
-        shift = [JIT * ((i * 7919 + k * 104729) % 1009) / 1009.0 for i in range(n)]
-        way = walk(back, [e + d for e, d in zip(best[2], shift)])[1]
-    return best[1]
+        way = walk(back, end if k % KEEP else best[2], GAIN[(k // 2) % len(GAIN)], [-e for e in early])[1]
+    PLANNED["time"] = best[0]
+    return [i for k in best[1] for i in calls[k]["ids"]]
 
 
 def issue(g, T, calls):
@@ -254,7 +281,9 @@ def rank_program(g, core, T, topo):
 
     def gather(q, rd, wr, out, win, lst, other=None, o=None, bias=None):
         cost = 0.06 + GATHER * size(out) * CYC
-        if q == "v":
+        if q == "v" and other is None:
+            op(q, rd, wr, cost, lambda e: e.tensor_copy(out, win.indirect(lst)))
+        elif q == "v":
             op(q, rd, wr, cost, lambda e: e.tensor_tensor(out, win.indirect(lst), other, o))
         elif bias is None:
             op(q, rd, wr, cost, lambda e: e.activation(out, win.indirect(lst), ACT.Copy))
@@ -281,19 +310,21 @@ def rank_program(g, core, T, topo):
     XR, TR = ["XB0", "XB1"], ["TB0", "TB1", "TB2", "TB3"]
     xall, tall = XR + ["XBqD", "XBqR", "XBz", "XBy"], TR + ["TBqD", "TBqR", "TBz", "TBy"]
     XW, TW = T.XB[:, 256:2304], T.TB[:, 256:2304]
-    dma("y", [], ["QS"], T.QS[:], T.qs[:], 9.0)
-    dma("s", [], ["WTS"], T.WTS[:], T.wt[:], 9.0)
-    dma("s", [], ["KKI"], T.KKI[:], T.kk[:], 8.0)
+    dma("s", [], ["WTS"], T.WTS[:], T.wt[:])
+    dma("s", [], ["KKI"], T.KKI[:], T.kk[:])
     dma("s", [], ["XB0"], T.XB[:, 256:1280], T.x0[:, 0:1024], 4.0)
+    dma("y", [], ["QS"], T.QS[:], T.qs[:])
     dma("y", [], ["XB1"], T.XB[:, 1280:2304], T.x0[:, 1024:2048], 4.0)
-    for c in calls[0:3]:
-        c["late"] = LOCAL
     dma("y", [], ["XBqD", "XBqR", "XBz"], T.XB[:, 0:256], T.qs[:, 0:256])
     dma("y", [], ["XBy"], T.XB[:, 2304:2688], T.qs[:, 0:384])
     dma("y", [], ["OLDqD", "OLDqR"], T.OLD[:, 384:512], T.qs[:, 0:128])
     dma("y", [], ["MX1R"], T.MX1[:, 0:128], T.qs[:, 0:128])
     dma("y", [], ["MX2_0"], T.MX2[:, 0:256], T.qs[:, 0:256])
     dma("y", [], ["MX2_1"], T.MX2[:, 256:512], T.qs[:, 0:256])
+    for i in range(len(calls)):
+        calls[i]["early"] = 1000.0
+        if i % 3 or i > 3:
+            calls[i]["behind"] = [i - 1]
 
     iota("PIN", T.PIN[:], [[0, 1]], 0, 1, False)
     iota("IO4", T.IO4[:, 0:4], [[4, 4]], 0, 0)
@@ -306,29 +337,25 @@ def rank_program(g, core, T, topo):
     iota("CG", T.CG[:], [[16, 8], [0, 16]], 0, 0)
     iota("CR", T.CR[:], [[0, 8], [1, 16]], 0, 0)
     iota("LN0", T.LN0[:], [[16, 8]], 0, 0)
-    for n in ("RK1", "RK2", "RP2", "RQP", "RQC", "ST", "MAS"):
-        vset([n], T[n][:], 0.0)
-    vset(["IOT1"], T.IOT[64:128, :], 1.0)
     vset(["G2_0", "G2_1"], T.G2[:, 0:512], 0.0)
-    dma("y", ["G2_0", "G2_1"], ["G1R"], T.G1[:, 0:128], T.G2[:, 0:128])
-    for i in range(4):
-        dma("y", ["G2_0", "G2_1"], ["DF%d_0" % i, "DF%d_1" % i], T.DFV[:, 1536 * i:1536 * i + 512], T.G2[:, 0:512])
+    vset(["MAS"], T.MAS[:], 0.0)
+    vset(["ONE"], T.ONE[:], 1.0)
+    vset(["IOT1"], T.IOT[64:128, :], 1.0)
+    for n, out in (("RQC", T.RQC[:]), ("RK1", T.RK1[:]), ("RK2", T.RK2[:]), ("RP2", T.RP2[:]), ("RQS", T.RQS[:]), ("RQPa", T.RQP[:, 0:16, :]),
+                   ("RQPb", T.RQP[:, 16:32, :]), ("ST", T.ST[:]), ("G1R", T.G1[:, 0:128])):
+        dma("y", ["G2_0", "G2_1"], [n], out, T.G2[:, 0:size(out)])
     for i, (sh, m) in enumerate(((0, 112), (0, 15), (0, 3), (2, 3))):
         ts(["PIN"], ["PI"], col("PI", i), T.PIN[:], sh, m, A.arith_shift_right, A.bitwise_and)
     cp(["PI"], ["PF"], T.PF[:], T.PI[:, 0:4])
     ts(["IO4", "PF"], ["BX"], T.BX[:], T.IO4[:, 0:4], col("PF", 0), None, A.add)
     ts(["IO4", "PF"], ["EA"], T.EA[:], T.IO4[:, 4:8], col("PF", 2), None, A.is_equal)
     ts(["IO4", "PF"], ["EX"], T.EX[:], T.IO4[:, 4:8], col("PF", 3), None, A.is_equal)
-    vset(["CV"], T.CV[:, :, 0:4], 0.0)
-    vset(["CV"], T.CV[0:64, :, 12:16], 0.0)
-    vset(["CV"], T.CV[64:128, :, 12:14], 0.0)
-    vset(["CV"], T.CV[0:64, :, 4:8], -16.0)
-    vset(["CV"], T.CV[0:64, :, 8:12], 16.0)
-    vset(["CV"], T.CV[64:128, :, 14], -16.0)
-    vset(["CV"], T.CV[64:128, :, 15], 1.0 / 64)
+    parts = [(0, 0, 32, 0, 4, 0.0), (64, 0, 32, 0, 4, 0.0), (0, 0, 32, 12, 16, 0.0), (64, 0, 32, 12, 14, 0.0), (0, 0, 32, 4, 8, -16.0),
+             (0, 0, 32, 8, 12, 16.0), (64, 0, 32, 14, 15, -16.0), (64, 0, 32, 15, 16, 1.0 / 64)]
     for b in range(4):
-        vset(["CV"], T.CV[64:128, 8 * b:8 * b + 8, 4:8], -16.0 - 8192.0 * b)
-        vset(["CV"], T.CV[64:128, 8 * b:8 * b + 8, 8:12], 8192.0 * b)
+        parts += [(64, 8 * b, 8 * b + 8, 4, 8, -16.0 - 8192.0 * b), (64, 8 * b, 8 * b + 8, 8, 12, 8192.0 * b)]
+    for p, r0, r1, c0, c1, c in parts:
+        sset(["CV"], T.CV[p:p + 64, r0:r1, c0:c1], T.CQ[p:p + 64, 0:(r1 - r0) * (c1 - c0)], "CQ", c)
     cp(["WTS"], ["WTF"], col("KC1", 3), T.WTS[:])
     for x in range(4):
         ts(["CQ", "BX", "WTF"], ["WX"], T.WX[:, 128 * x:128 * x + 128], T.CQ[:], col("BX", x), col("KC1", 3), A.is_equal, A.mult, 0.5)
@@ -338,14 +365,14 @@ def rank_program(g, core, T, topo):
     ts(["K0"], ["K1"], col("KC1", 1), col("KC1", 0), 1024.0, -2048.0, A.is_gt, A.mult)
     ts(["K0", "K1"], ["K32"], col("KC1", 2), col("KC1", 0), col("KC1", 1), 32.0, A.add, A.mult)
 
-    def places(rd, src, o, n):
+    def places(rd, src, o, n, q="v"):
         k = "%d" % o
-        cp(rd, ["UI" + k], T.UI[:, o:o + n], src)
+        offsets(q, rd, ["UI" + k], T.UI[:, o:o + n], src)
         ts(["UI" + k], ["U" + k], T.U[:, o:o + n], T.UI[:, o:o + n], 2047, None, A.bitwise_and)
         ts(["U" + k, "K32"], ["Z" + k], T.Z[:, o:o + n], T.U[:, o:o + n], col("KC1", 2), None, A.add)
         tt(["Z" + k, "U" + k], ["Y" + k], T.Y[:, o:o + n], T.Z[:, o:o + n], T.U[:, o:o + n], A.mult)
         ts(["Y" + k], ["P" + k], T.P[:, o:o + n], T.Y[:, o:o + n], 5, 2047, A.arith_shift_right, A.bitwise_and)
-        cp(["P" + k], ["PH" + k], T.PH[:, o:o + n], T.P[:, o:o + n])
+        offsets(q, ["P" + k], ["PH" + k], T.PH[:, o:o + n], T.P[:, o:o + n])
 
     ts(["PF"], ["SC0"], col("SC", 0), col("PF", 0), col("PF", 2), None, A.add)
     ts(["PF"], ["SC10"], col("SC", 10), col("PF", 1), 8.0, 12.0, A.is_ge, A.add)
@@ -381,13 +408,13 @@ def rank_program(g, core, T, topo):
     iota("RCF", T.RCF[:], [[2, 8], [16, 2], [1, 2]], 32, 0)
     sel("RCF", "RQC", T.RQC[:, 8:12, :], T.RCF[:], [[16, 8], [0, 4]], A.is_equal, 0.0, 15, -1)
     for r in (12, 13):
-        paint("RQK", T.RQK[:, :, 0], [[0, 4], [16, 8], [0, 4]], r, -1024.0)
+        paint("RQS", T.RQS[:], [[16, 8], [0, 4]], r, -1024.0)
         paint("RQC", T.RQC[:, 8:12, :], [[16, 8], [0, 4]], r, -1024.0)
         paint("RQC", T.RQC[:, 12, :], [[16, 8]], r, 1.0)
         paint("RK2", T.RK2[:, :, 0], [[16, 8]], r, -1024.0)
     paint("RQC", T.RQC[:, 4:8, :], [[2, 2], [16, 8], [1, 2]], 0, 1.0)
     for h in range(2):
-        paint("RQP", T.RQP[:, 16 * h + 8:16 * h + 16, :], [[16, 8], [1, 2], [0, 16]], 2 * h, -1.0)
+        paint("RQP" + "ab"[h], T.RQP[:, 16 * h + 8:16 * h + 16, :], [[16, 8], [1, 2], [0, 16]], 2 * h, -1.0)
     for r in (4, 8):
         paint("RK1", T.RK1[:], [[16, 8], [1, 4], [0, 5]], r, 16384.0)
         paint("RK2", T.RK2[:, :, 1:5], [[16, 8], [1, 4]], r, 16384.0)
@@ -412,10 +439,16 @@ def rank_program(g, core, T, topo):
     dma("y", ["QT"], ["TBy"], T.TB[:, 2304:2688], T.QT[:, 0:384])
 
     TBANK = ("PA", "PB", "LR", "LD")
+    table = len(calls)
     for h in range(2):
         hb = ("LD", "KC")[h]
         quad("WX", [XR[h]], hb, lambda x: T[hb][:, 0:256], lambda x: T.XB[:, 256 + 1024 * h + x:1280 + 1024 * h:4])
-        places([hb], T[hb][:, 0:256], 256 * h, 256)
+        places([hb], T[hb][:, 0:256], 256 * h, 256, "s")
+    for c in calls[table:]:
+        c["early"] = 5.0
+    for c in calls:
+        if c["wr"][0] in ("QRD0", "PCz", "PCy", "MS0", "RST", "RS16"):
+            c["behind"] = [i for i in range(table, len(calls)) if calls[i]["wr"][0][0:2] == "UI"]
     for b in range(4):
         tb = TBANK[b]
         mm(["CV", "IOT0", "IOT1"], tb, T[tb][:], T.CV[:, 8 * b:8 * b + 8, :], T.IOT[:], True, False)
@@ -424,6 +457,7 @@ def rank_program(g, core, T, topo):
         ts([tb, "SC7", "SC8"], [TR[b]], T.TB[:, 256 + 512 * b:768 + 512 * b], T[tb][:], col("SC", 7), col("SC", 8), A.max, A.min)
 
     ts(["CG", "PF"], ["BD1"], T.BD1[:], T.CG[:, 0:128:16], col("PF", 0), 1024.0, A.is_equal, A.mult)
+    ts(["CG", "PF"], ["BDN"], T.BDN[:], T.CG[:, 0:128:16], col("PF", 0), -1024.0, A.is_equal, A.mult)
     ts(["CG", "PF"], ["BD2"], T.BD2[:], T.CG[:, 0:128:16], col("PF", 0), 2048.0, A.is_equal, A.mult)
     sset(["QTR0"], T.QTH[:, 0:32], T.QS[:, 0:32], "QS", 4096.0)
     sset(["PCz", "PC12"], T.PCW[:, 0:256], T.QS[:, 0:256], "QS", -256.0)
@@ -464,6 +498,7 @@ def rank_program(g, core, T, topo):
     ts(["CR", "PF", "XS"], ["MKA"], T.XT[:], T.CR[:], col("PF", 1), -48640.0, A.is_ge, A.mult, 0.5)
     act(["MKA"], ["MKB"], T.MKB[:], T.XT[:], ACT.Identity, -2560.0)
     act(["IB"], ["IB5"], T.IB5[:], T.IB[:], ACT.Identity, 0.0, 5120.0)
+    act(["IB"], ["NIB"], T.NIB[:], T.IB[:], ACT.Identity, 0.0, -1.0)
     paint("LTB", T.LTB[:], [[1, 128]], 0, -256.0)
 
     def repeat(rd, t4, t16, src, o4, n):
@@ -475,6 +510,20 @@ def rank_program(g, core, T, topo):
     def blocks(name, lo, hi):
         return ["%s_%d" % (name, k) for k in range(lo // 16, (hi + 15) // 16)]
 
+    def level3(k, tok, mode):
+        b, g2 = k // 32, blocks("G2", k, k + 32)
+        pb = ("LR", "PB", "PA", "LD")[b]
+        gather((G2Q if mode[0] else G2Q0)[b], [tok] + TR, g2, T.G2[:, 16 * k:16 * k + 512], TW, T.OF2[:, k:k + 32])
+        out = T[pb][:, 0:4, :] if pb[0] == "P" else T[pb][:, 96:224]
+        if mode[b] == "c":
+            quad("LX", g2, pb, lambda x: out, lambda x: T.G2[:, 16 * k + x:16 * k + 512:4])
+        else:
+            for i in range(4):
+                quad("LX", g2, pb, lambda x: T[pb][:, i, :] if pb[0] == "P" else T[pb][:, 96 + 32 * i:128 + 32 * i],
+                     lambda x: T.G2[:, 16 * k + 4 * i + x:16 * k + 512:16])
+        offsets(CVT[1 + b], [pb], ["OF3_%d" % b], T.OF3[:, 4 * k:4 * k + 128], out)
+
+    marks = [len(calls)]
     for s in range(S):
         arrivals = s > 0
         send = s + 1 < S
@@ -484,6 +533,7 @@ def rank_program(g, core, T, topo):
         QTT = ["QTD%d" % s, "QTR%d" % s]
         qth = T.QTH[:, 128 * s:128 * s + 128]
         first = 0 if arrivals else 32
+        mode = MODE if arrivals else MODE0
         if arrivals:
             dma("y", ["QT"], ["TBqD"], T.TB[:, 0:96], T.QT[:, 96 * s:96 * s + 96])
             dma("y", [], ["XBqD"], T.XB[:, 0:96], T.qs[:, 96 * s:96 * s + 96])
@@ -497,14 +547,8 @@ def rank_program(g, core, T, topo):
         gather("s", ["L1U"] + TR, ["G1D"], T.G1[:, 128:512], TW, l1)
         quad("LX", ["G1D"], "LD", lambda x: T.LD[:, 0:96], lambda x: T.G1[:, 128 + x:512:4])
         offsets(CVT[0], ["LD"], ["OF2D"], T.OF2[:, 32:128], T.LD[:, 0:96])
-        gather("s", ["OF2D"] + TR, blocks("G2", 96, 128), T.G2[:, 1536:2048], TW, T.OF2[:, 96:128])
-        quad("LX", blocks("G2", 96, 128), "LD", lambda x: T.LD[:, 96:224], lambda x: T.G2[:, 1536 + x:2048:4])
-        offsets(CVT[1], ["LD"], ["OFC"], T.OFC[:], T.LD[:, 96:224])
-        for k, pb in ((32, "PB"), (64, "PA")):
-            gather("s", ["OF2D"] + TR, blocks("G2", k, k + 32), T.G2[:, 16 * k:16 * k + 512], TW, T.OF2[:, k:k + 32])
-            quad("LX", blocks("G2", k, k + 32), pb, lambda x: T[pb][:, 0:4, :], lambda x: T.G2[:, 16 * k + x:16 * k + 512:4])
-            for i in range(4):
-                offsets(CVT[2], [pb], ["OFV%d_%d" % (i, k)], T.OFV[:, 96 * i + k:96 * i + k + 32], T[pb][:, 0:4, i:32:4])
+        for k in (96, 64, 32):
+            level3(k, "OF2D", mode)
         gather("v", ["L1U", "QR4D%d" % s] + XR, ["MX1D"], T.MX1[:, 128:512], XW, l1, T.QR4[:, 512 * s + 128:512 * s + 512], A.max)
 
         if arrivals:
@@ -512,31 +556,44 @@ def rank_program(g, core, T, topo):
             places(["LR"], T.LR[:, 0:8], 632, 8)
             cp(["P632"], ["OF1"], T.OF1[:], T.P[:, 632:640])
             gather("s", ["OF1"] + TR, ["G1R"], T.G1[:, 0:128], TW, T.OF1[:])
-            mm(["XS", at], "KC", T.KC[:, 0:32], T.XS[:], arr, True, False)
-            quad("UX", ["PH632"], "KC", lambda x: T.KC[:, x:32:4], lambda x: T.PH[:, 632:640], False)
+            mm(["XS", at], "PC", T.PC[:, 32:36, :], T.XS[:], arr, True, False)
+            quad("UX", ["PH632"], "PC", lambda x: T.PC[:, 32:36, x:8:4], lambda x: T.PH[:, 632:640], False)
             quad("LX", ["G1R"], "LR", lambda x: T.LR[:, 16:48], lambda x: T.G1[:, x:128:4])
-            act(["KC", "SC9", "SC16"], [QTT[1]], T.QTH[:, 128 * s:128 * s + 32], T.KC[:, 0:32], ACT.Identity, col("SC", 9), col("SC", 16))
+            act(["PC", "SC9", "SC16"], [QTT[1]], T.QTH[:, 128 * s:128 * s + 32], T.PC[:, 32:36, :], ACT.Identity, col("SC", 9), col("SC", 16))
             if send:
-                act(["KC", "SC9", "SC16"], ["TBqR"], T.TB[:, 96:128], T.KC[:, 0:32], ACT.Identity, col("SC", 9), col("SC", 16))
-            offsets(CVT[3], ["LR"], ["OF2R"], T.OF2[:, 0:32], T.LR[:, 16:48])
-            gather("s", ["OF2R"] + TR, blocks("G2", 0, 32), T.G2[:, 0:512], TW, T.OF2[:, 0:32])
-            quad("LX", blocks("G2", 0, 32), "LR", lambda x: T.LR[:, 64:192], lambda x: T.G2[:, x:512:4])
-            for i in range(4):
-                offsets(CVT[4], ["LR"], ["OFV%d_0" % i], T.OFV[:, 96 * i:96 * i + 32], T.LR[:, 64 + i:192:4])
+                act(["PC", "SC9", "SC16"], ["TBqR"], T.TB[:, 96:128], T.PC[:, 32:36, :], ACT.Identity, col("SC", 9), col("SC", 16))
+            offsets(CVT[5], ["LR"], ["OF2R"], T.OF2[:, 0:32], T.LR[:, 16:48])
+            level3(0, "OF2R", mode)
             gather("v", ["OF1", "QR4R%d" % s] + XR, ["MX1R"], T.MX1[:, 0:128], XW, T.OF1[:], T.QR4[:, 512 * s:512 * s + 128], A.max)
 
         for k in range(first, 128, PIECE):
             gather("v", ["OF2R", qr] * (k < 32) + ["OF2D", qd] * (k >= 32) + XR, blocks("MX2", k, k + PIECE), T.MX2[:, 16 * k:16 * (k + PIECE)], XW,
                    T.OF2[:, k:k + PIECE], T.QR16[:, q0 + 16 * k:q0 + 16 * (k + PIECE)], A.max)
-        for j in range(32):
-            gather("s", ["OFC", "QS"] + XR, ["DFC%d" % j], T.DFC[:, 64 * j:64 * j + 64], XW, T.OFC[:, 4 * j:4 * j + 4], bias=col("QS", 96 * s + 64 + j))
-        for i in range(4):
-            for k in range(first, 96, PIECE):
-                tok = blocks("DF%d" % i, k, k + PIECE)
-                a = T.DFV[:, 1536 * i + 16 * k:1536 * i + 16 * (k + PIECE)]
-                gather("v", ["OFV%d_%d" % (i, k // 32 * 32), qr if k < 32 else qd] + XR, tok, a, XW, T.OFV[:, 96 * i + k:96 * i + k + PIECE],
-                       T.QR16[:, q0 + 16 * k:q0 + 16 * (k + PIECE)], A.subtract)
-                act(tok, tok, a, a, ACT.Abs)
+        for b in range(first // 32, 4):
+            k = 32 * b
+            if mode[b] == "c":
+                for j in range(k, k + 32):
+                    gather("s", ["OF3_%d" % b, "QS" if b else at] + XR, ["DF%d" % (j // 8)], T.DF[:, 64 * j:64 * j + 64], XW,
+                           T.OF3[:, 4 * j:4 * j + 4], bias=col("QS", 96 * s + j - 32) if b else col("ARR", a0 + j))
+                continue
+            for i in range(4):
+                o = 1536 * i + 512 * b
+                tok, a = ["DF%d" % (4 * b + i)], T.DF[:, o:o + 512]
+                if mode[b][i] == "p":
+                    raw = T.OCC[:, 512 * i:512 * i + 512]
+                    gather("s", ["OF3_%d" % b] + XR, ["OCC%d" % i], raw, XW, T.OF3[:, 4 * k + 32 * i:4 * k + 32 * i + 32])
+                    mm(["NIB", qd if b else qr], "LD", T.LD[:], T.NIB[:], T.QR16[:, q0 + 16 * k:q0 + 16 * k + 512], True, False)
+                    mm(["IB", "OCC%d" % i], "LD", T.LD[:], T.IB[:], raw, False, True)
+                    act(["LD"], tok, a, T.LD[:], ACT.Abs)
+                    continue
+                n = 16 if arrivals and tok[0] in HALVES else 32
+                for h in range(0, 32, n):
+                    gather("v", ["OF3_%d" % b, qd if b else qr] + XR, [tok[0] + "ab"[h // 16]] * (n == 16) + tok, T.DF[:, o + 16 * h:o + 16 * (h + n)], XW,
+                           T.OF3[:, 4 * k + 32 * i + h:4 * k + 32 * i + h + n], T.QR16[:, q0 + 16 * (k + h):q0 + 16 * (k + h + n)], A.subtract)
+                if mode[b][i] == "s":
+                    act(tok, tok, a, a, ACT.Abs)
+                else:
+                    ts(tok, ["RL%d" % (4 * b + i)], T.RL[:, o:o + 512], a, 0.0, 2.0, A.max, A.mult, 0.5)
 
         G1T, G2T = ["G1D", "G1R"], blocks("G2", 0, 128)
 
@@ -546,17 +603,21 @@ def rank_program(g, core, T, topo):
             return T[("KA", "KA", "KB")[i]][p0:p1, 32 * (i == 1) + j:32 * (i == 1) + 32:4, c]
 
         mm(QTT + ["RQC"], "PC", T.PC[:, 0:32, :], qth, T.RQC[:], True, False)
-        mm(QTT + ["RQK"], "KA", T.KA[:], qth, T.RQK[:, 0:64, :], True, False)
-        mm(QTT + ["RQK"], "KB", T.KB[:], qth, T.RQK[:, 64:96, :], True, False)
-        mm(QTT + ["RQK"], "KC", T.KC[:, 0:160], qth, T.RQK[:, 96:128, :], True, False)
-        mm(QTT + ["RQP"], "PA", T.PA[:], qth, T.RQP[:, 0:16, :], True, False)
-        mm(QTT + ["RQP"], "PB", T.PB[:], qth, T.RQP[:, 16:32, :], True, False)
+        mm(["ONE", "RQK"], "KA", T.KA[:], T.ONE[:], T.RQK[:, 0:64, :], True, False)
+        mm(["ONE", "RQK"], "KB", T.KB[:], T.ONE[:], T.RQK[:, 64:96, :], True, False)
+        mm(["ONE", "RQK"], "KC", T.KC[:, 0:160], T.ONE[:], T.RQK[:, 96:128, :], True, False)
+        for b, out in (("KA", T.KA[:, 0:32, 0]), ("KA", T.KA[:, 32:64, 0]), ("KB", T.KB[:, :, 0]), ("KC", T.KC[:, 0:160:5])):
+            mm(QTT + ["RQS"], b, out, qth, T.RQS[:], False, False, True)
+        mm(QTT + ["RQPa"], "PA", T.PA[:], qth, T.RQP[:, 0:16, :], True, False)
+        mm(QTT + ["RQPb"], "PB", T.PB[:], qth, T.RQP[:, 16:32, :], True, False)
         for i in range(4):
             r, c = 16 + 8 * (i // 2), 4 * (i % 2)
             mm(G1T + ["RP2"], "PC", T.PC[:, r:r + 8, c:c + 4], T.G1[:, i:512:4], T.RP2[:, 0:8, :], False, False, True)
             mm(G1T + ["RK2"], "PC", T.PC[:, 8:12, i:8:4], T.G1[:, i:512:4], T.RK2[:, :, 0], False, False, True)
+        sums = [k for k in range(marks[-1], len(calls)) if "RK2" in calls[k]["rd"]]
         for i in range(4):
             mm(["MX1D", "MX1R", "BD2"], "PC", T.PC[:, 8:12, i:8:4], T.MX1[:, i:512:4], T.BD2[:], False, i == 3, i < 3)
+            calls[-1]["behind"] = sums
         act(["PC"], ["PC12"], T.PCW[:, 32:256], T.PC[:, 4:32, :], ACT.Copy)
         for h, pb in enumerate(("PA", "PB")):
             for j in range(8):
@@ -587,14 +648,25 @@ def rank_program(g, core, T, topo):
                     mm(G2T + ["RK2"], b, rows(i, j, k), g2, T.RK2[:, :, k], False, False, True)
                 for k in range(4):
                     mm(fg, b, rows(i, j, 1 + k), T.IPEN[:], T.FG[:, 8:16, 16 + 4 * j + k], False, False, True)
-            for r in range(16):
-                mm(["DFC%d" % k for k in range(32)] + ["BD1"], b, rows(i, r // 4, 1 + r % 4, 96), T.DFC[:, 16 * i + r:2048:64], T.BD1[:],
-                   False, False, True)
-                mm(blocks("DF%d" % i, 0, 96) + ["BD1"], b, rows(i, r // 4, 1 + r % 4, 0, 96), T.DFV[:, 1536 * i + r:1536 * i + 1536:16], T.BD1[:],
-                   False, False, True)
+            sums = [k for k in range(marks[-1], len(calls)) if "RK2" in calls[k]["rd"] and b in calls[k]["rd"]]
+            for k in range(first // 32, 4):
+                for r in range(16):
+                    out, o = rows(i, r // 4, 1 + r % 4, 32 * k, 32 * k + 32), 1536 * i + 512 * k
+                    if arrivals and k < WIDE[i]:
+                        if k == 0:
+                            mm(["DF%d" % (4 * j + i) for j in range(WIDE[i])] + ["BD1"], b, rows(i, r // 4, 1 + r % 4, 0, 32 * WIDE[i]),
+                               T.DF[:, o + r:o + 512 * WIDE[i]:16], T.BD1[:], False, False, True)
+                        continue
+                    if mode[k] == "c":
+                        mm(["DF%d" % (4 * k + j) for j in range(4)] + ["BD1"], b, out, T.DF[:, 2048 * k + 16 * i + r:2048 * k + 2048:64], T.BD1[:],
+                           False, False, True)
+                        continue
+                    for n, w in (("DF", "BD1"),) if mode[k][i] != "v" else (("DF", "BDN"), ("RL", "BD1")):
+                        mm(["%s%d" % (n, 4 * k + i), w], b, out, T[n][:, o + r:o + 512:16], T[w][:], False, False, True)
             for j in range(4):
                 last = j == 3 and i != 0
                 mm(blocks("MX2", 0, 128) + ["BD2"], b, rows(i, j, 0), T.MX2[:, 4 * i + j:2048:16], T.BD2[:], False, last, not last)
+                calls[-1]["behind"] = sums
         for i in range(3):
             b, o = ("KA", "KA", "KB")[i], 32 * (i == 1)
             tt([b, "MS%d" % i], ["MS%d" % (i + 1)], T.MS[:, 160 * i + 160:160 * i + 320], T[b][:, o:o + 32, :], T.MS[:, 160 * i:160 * i + 160], A.max)
@@ -639,10 +711,11 @@ def rank_program(g, core, T, topo):
         for hi in range(1, 8):
             k, cl = 9 * (hi - 1), col("RS16", 16 * hi + 15)
             if hi in ON_PE:
-                pb = ("LR", "KC")[ON_PE.index(hi)]
+                pb = {7: "LR", 6: "PB", 5: "KC", 4: "KA"}[hi]
+                sums = T.PB[:, 0:3, :] if hi == 6 else T.KA[:, :, 0] if hi == 4 else T[pb][:, 128:128 + 16 * hi]
                 for j in range(9):
-                    mm(["IB", "EQ%d" % hi], pb, T[pb][:, 128:128 + 16 * hi], T.IB[:], T.EQ[:, 8 * j + hi, 112 - 16 * hi:112], j == 0, j == 8)
-                count([pb], ["CL%d" % hi, "JK%d" % hi], T.JK[:, k, 0:16 * hi], T[pb][:, 128:128 + 16 * hi], cl)
+                    mm(["IB", "EQ%d" % hi], pb, sums, T.IB[:], T.EQ[:, 8 * j + hi, 112 - 16 * hi:112], j == 0, j == 8)
+                count([pb], ["CL%d" % hi, "JK%d" % hi], T.JK[:, k, 0:16 * hi], sums, cl)
             else:
                 count(["EQ%d" % hi], ["CL%d" % hi, "JK%d" % hi], T.JK[:, k:k + 9, 0:16 * hi], T.EQ[:, hi:72:8, 112 - 16 * hi:112], cl)
         for h0 in (4, 0):
@@ -664,13 +737,26 @@ def rank_program(g, core, T, topo):
                 mm(["BDB", "ND"], "KC", T.KC[:, d:8], T.BDB[:], T.ND[:, 0:8 - d], False, d == 7)
             sb = "SB%d" % s
             tt(["KC", "TL"], ["D3"], sm("D3"), T.KC[:, 0:8], T.TL[:], A.min)
-            cp(["D3"], ["SLU"], T.SLU[:], sm("D3"))
+            offsets("s", ["D3"], ["SLU"], T.SLU[:], sm("D3"))
             scatter(["DLU", "NEWT"], tall, T.TB[:], T.DLU[:], T.NEWT[:])
             scatter(["SLU", "OLD"], [sb], T.SB[:, 256 * s:256 * s + 256], T.SLU[:], T.OLD[:, 0:128])
             calls.append({"q": "g", "rd": [sb], "wr": ["ARR%d" % (s + 1)], "cost": 0.5, "late": FAR, "kind": "far", "ev": ("arr%d" % (s + 1), nland, "far"),
                           "call": lambda e, k=s: e.remote_dma(T.ARR[:, 32 * k + 32:32 * k + 64], T.SB[:, 256 * k:256 * k + 32],
                                                               T.sem["arr%d" % (k + 1)], T.sem.sent, pid, rid, wire)})
         scatter(["DLU", "OLD", "OLDqD", "OLDqR"], xall, T.XB[:], T.DLU[:], T.OLD[:, 128:512])
+        marks.append(len(calls))
+    for s in range(S):
+        for q, names in (FIXED if s else FIXED0).items():
+            last = None
+            for w in names.split():
+                k = s - (w[0] == "-")
+                if k < 0:
+                    continue
+                w = w.lstrip("-").replace("#", "%d" % k)
+                found = [i for i in range(marks[k], marks[k + 1]) if calls[i]["q"] == q and calls[i]["wr"][0] == w]
+                if found and last is not None:
+                    calls[found[0]]["behind"] = [last]
+                last = found[-1] if found else last
     dma("y", XR, ["y0"], T.y[:, 0:1024], T.XB[:, 256:1280])
     dma("s", XR, ["y1"], T.y[:, 1024:2048], T.XB[:, 1280:2304])
     issue(g, T, calls)

from concourse.mybir import AluOpType, AxisListType, ActivationFunctionType

A = AluOpType
ACT = ActivationFunctionType
X = AxisListType.X
S = 5
PEN = -16777216.0
DEADKEY = 12582912.0
ON_PE = (7, 6, 5)
FIXED = {"v": "-D3 -TB0 -SB# -XB0 MX1D MX2_2 MX2_6 MX2_4 OF3_2 DF8 OF3_1 DF9a UI632 DF4a U632 DF9b Z632 Y632 DF4b P632 DF5a OF1 PH632 DF5b MX1R DF6 "
              "MX2_0 DF10 OF3_0 L1 DF1 L2 FG1 MD0 H3 FG0 DF0 DF2 MS0 DF11 DF3 MS1 MS2 MS3 POU SELM SELN OTHH EQ4 EQ7 EQ3 EQ6 EQ5 EQ2 EQ1 EQ0",
         "s": "G1D OF2D G2_6 G2_4 OF3_3 G2_2 DF14 DF12 OCC3 DF13 G1R DF7 TBqR OF2R QTR# G2_0 DF4 PC12 DF8 DF15 DF10 DF5 DF6 DF1 DF9 DF0 DF2 "
              "DF11 DF3 PC3b PC3a"}
FIXED0 = {"v": "MX1D MX2_6 MX2_4 MX2_2 DF8 DF4 DF9 DF5 DF10 DF6 DF11 DF7 POU SELM SELN OTHH EQ4 EQ7 EQ3 EQ6 EQ5 EQ2 EQ1 EQ0",
          "s": "G1D OF2D G2_6 G2_4 OF3_3 G2_2 DF12 PC12 DF15"}
MODE = ("ssss", "sssp", "ssss", "c")
MODE0 = ("", "vsss", "vsss", "c")
WIDE = (3, 3, 3, 0)
G2Q0 = "ssss"
G2Q = "ssss"
CVT = "svvvss"
PIECE = 32
CYC, PEC, GATHER, SCATTER, HOP, LOCAL, FAR = 0.00083, 0.00045, 1.56, 3.8, 0.22, 2.2, 4.6
SLACK, ROUNDS, KEEP, GAIN = 0.1, 4, 3, (-0.3, 0.0, 0.1)
RUN = 0.65
HALVES = ("DF9", "DF4", "DF5")
MARGIN = {"OF3_0": 1.0, "FG0": 1.0, "FG1": 1.0, "MS2": 1.0, "MS3": 0.5}
PLANNED = {}

SCRATCH = {}
for _t, _l in (
        ("bfloat16", "XB:2688 QS:480 WTS:1 CQ:128 CM:128 CG:128 CR:128 WX:512 XS:128 XT:128 XU:128 IB:128 IB5:128 NIB:128 OCC:2048 IPEN:128 BDB:128 LTB:128 MKB:128 BD2:8"
                     " QR4:2560 QR16:10240 MX1:512 MX2:2048 OLD:512 ND:8 NTL:8 DEAD:8 MASK:384 SB:1024 ARR:160"),
        ("float16", "LX:512 UX:512 AM:128 AT:128 AU:128 BM:128 BT:128 BU:128 IOT:512 BD1:8 BDN:8 HI:8 ST:384 G1:512 G2:2048 DF:8192 RL:8192 QTH:640 PH:640"
                    " ONE:128 RQS:32 SELM:384 SELN:128 TH:128 OLDT:256"),
        ("float32", "TB:2688 QT:480 PCW:1024 NEWT:384 MS:960 RST:160 RS16:128 CFS:128 IOF:512 KF:4 KM:4 KC1:4 PF:4 IO4:8 PX:4 BX:4 EX:4 EA:4 SC:18"
                    " LN0:8 LN:8 TRC:24 TL:8 SM:512 MD:16"),
        ("int32", "KKI:4 PIN:1 PI:6 UI:640 U:640 Z:640 Y:640 P:640 MI:8 PO:24"),
        ("uint16", "L1U:120 OF1:8 OF2:128 OF3:512 POU:24 NEU:8 XL:24 DLU:24 SLU:8")):
    for _w in _l.split():
        SCRATCH[_w.split(":")[0]] = ("sbuf", [128, int(_w.split(":")[1])], _t)
for _n, _s, _t in (("CA", [8, 16], "bfloat16"), ("MAS", [8, 16], "float16"), ("CV", [32, 16], "float16"), ("RK1", [32, 5], "float16"),
                   ("RK2", [8, 5], "float16"), ("RP2", [16, 4], "float16"), ("RQP", [32, 32], "float16"), ("RQC", [32, 8], "float16"),
                   ("RQK", [128, 5], "float16"), ("RQF", [128, 5], "float32"), ("RCF", [4, 8], "float32"), ("FG", [16, 32], "bfloat16"),
                   ("OTHH", [3, 128], "float16"), ("EQ", [72, 128], "bfloat16"), ("JK", [63, 112], "bfloat16")):
    SCRATCH[_n] = ("sbuf", [128] + _s, _t)
BANKS = ("LD", "LR", "KA", "KB", "KC", "PA", "PB", "PC")
for _n, _s in zip(BANKS, ([512], [512], [64, 5], [32, 5], [512], [16, 32], [16, 32], [64, 8])):
    SCRATCH[_n] = ("psum", [128] + _s, "float32")
SEMAPHORES = ["cv", "cs", "cp", "cg", "sent"] + ["arr%d" % (i + 1) for i in range(S - 1)] + ["d%d" % i for i in range(60)]


def plan(calls):
    runs = []
    for i, c in enumerate(calls):
        r = runs[-1] if runs else None
        if r and (r["q"], r["rd"], r["wr"], r["kind"]) == (c["q"], c["rd"], c["wr"], "op") and r["cost"] + c["cost"] < RUN and not set(c["rd"]) & set(c["wr"]):
            r["cost"] += c["cost"]
            r["ids"].append(i)
        else:
            runs.append(dict(c, ids=[i], margin=max([MARGIN.get(t, 0.0) for t in c["wr"]] + [0.0])))
    calls = runs
    run = {i: k for k, r in enumerate(runs) for i in r["ids"]}
    n = len(calls)
    preds, writer, readers = [], {}, {}
    for i, c in enumerate(calls):
        p = {}
        for t in c["rd"]:
            if t in writer:
                p[writer[t]] = HOP
        for t in c["wr"]:
            for r in readers.get(t, []):
                p[r] = 0.0 if t in BANKS and calls[r]["q"] == c["q"] else HOP
            if t in writer:
                w = writer[t]
                p[w] = max(p.get(w, 0.0), 0.0 if calls[w]["q"] == c["q"] and calls[w]["kind"] == "op" else HOP)
        if c["q"] == "p":
            for t in c["rd"]:
                if t in BANKS and t in writer and calls[writer[t]]["q"] == "p":
                    p[writer[t]] = 0.0
        for k in c.get("behind", []):
            p.setdefault(run[k], -calls[run[k]]["late"])
        p.pop(i, None)
        preds.append(p)
        for t in c["rd"]:
            readers.setdefault(t, []).append(i)
        for t in c["wr"]:
            writer[t] = i
            readers[t] = []
    succ, back = [[] for _ in calls], [[] for _ in calls]
    for i, p in enumerate(preds):
        for j, lat in p.items():
            succ[j].append((i, lat + calls[j]["late"]))
            back[i].append((j, lat + calls[j]["late"] + calls[j]["margin"]))

    def walk(after, way, gain, early):
        left = [0] * n
        for i in range(n):
            for j, _ in after[i]:
                left[j] += 1
        ready, end = [0.0] * n, [0.0] * n
        free = {q: 0.0 for q in "vspgy"}
        may = {q: [i for i in range(n) if calls[i]["q"] == q and not left[i]] for q in free}
        order = []
        while len(order) < n:
            pick = None
            goal = max([max(free[q], ready[i]) + way[i] for q in free for i in may[q]]) - gain
            for q in free:
                if not may[q]:
                    continue
                top, limit = None, 1e9
                may[q].sort(key=lambda k: -way[k] - early[k])
                for i in may[q]:
                    t = max(free[q], ready[i])
                    if top is None or t < top[0] and t + calls[i]["cost"] <= limit:
                        top = (t, i)
                        if t == free[q]:
                            break
                    limit = min(limit, max(t + SLACK, goal - way[i] - early[i]))
                if pick is None or top < pick:
                    pick = top
            t, i = pick
            q = calls[i]["q"]
            may[q].remove(i)
            free[q] = end[i] = t + calls[i]["cost"]
            order.append(i)
            for j, lat in after[i]:
                ready[j] = max(ready[j], end[i] + lat)
                left[j] -= 1
                if not left[j]:
                    may[calls[j]["q"]].append(j)
        return order, end

    way = walk(back, [0.0] * n, 0.0, [0.0] * n)[1]
    best = None
    early = [c.get("early", 0.0) for c in calls]
    for k in range(ROUNDS):
        order, end = walk(succ, way, GAIN[k % len(GAIN)], early)
        if best is None or max(end) < best[0]:
            best = (max(end), order, end)
        way = walk(back, end if k % KEEP else best[2], GAIN[(k // 2) % len(GAIN)], [-e for e in early])[1]
    PLANNED["time"] = best[0]
    return [i for k in best[1] for i in calls[k]["ids"]]


def issue(g, T, calls):
    eng = {"v": g.vector, "s": g.scalar, "p": g.tensor, "g": g, "y": g.sync}
    count = {"cv": 0, "cs": 0, "cp": 0, "cg": 0}
    known = {q: {} for q in eng}
    snap, writer, readers, touch = {}, {}, {}, {}
    dmas = 0
    if len(calls) not in PLANNED:
        PLANNED[len(calls)] = plan(calls)
    for i in PLANNED[len(calls)]:
        c = calls[i]
        q, rd, wr = c["q"], c["rd"], c["wr"]
        evs = []
        for t in rd + wr:
            if t in BANKS:
                evs += [e for e in touch.get(t, {}).values() if e[2] != q]
            elif t in rd and t in writer:
                evs.append(writer[t])
        for t in wr:
            if t in BANKS:
                continue
            if readers.get(t):
                evs += list(readers[t].values()) + ([writer[t]] if t in writer else [])
            elif t in writer and writer[t][2] != q:
                evs.append(writer[t])
        best = {}
        for sem, val, _ in evs:
            best[sem] = max(best.get(sem, 0), val)
        for sem in sorted(best):
            val = best[sem]
            if known[q].get(sem, 0) < val:
                eng[q].wait_ge(T.sem[sem], val)
                for k, m in snap.get((sem, val), {}).items():
                    known[q][k] = max(known[q].get(k, 0), m)
                known[q][sem] = val
        if c["kind"] == "op":
            sem = "c" + q
            count[sem] += 1
            c["call"](eng[q]).then_inc(T.sem[sem], 1)
            ev = (sem, count[sem], q)
        elif c["kind"] == "dma":
            sem = "d%d" % dmas
            dmas += 1
            c["call"](eng[q]).then_inc(T.sem[sem], 16)
            ev = (sem, 16, "dma")
        else:
            c["call"](g)
            ev = c["ev"]
        if c["kind"] != "far":
            snap[ev[:2]] = dict(known[q])
        for t in rd + wr:
            if t in BANKS:
                touch.setdefault(t, {})[ev[2]] = ev
            elif t in wr:
                writer[t] = ev
                readers[t] = {}
            elif c["kind"] != "far":
                readers.setdefault(t, {})[(ev[2], ev[0])] = ev
    for sem in count:
        if known["g"].get(sem, 0) < count[sem]:
            g.wait_ge(T.sem[sem], count[sem])
    for i in range(dmas):
        g.wait_ge(T.sem["d%d" % i], 16)


def rank_program(g, core, T, topo):
    rank = T.rank_of(core)
    if rank is None:
        return
    nxt = T.cores[(rank + 1) % len(T.cores)]
    rid, pid = topo.addr(nxt, core)
    wire = topo.mask(core, nxt)
    nwire = len(topo.engines(core, nxt))
    nland = len(topo.engines(T.cores[(rank - 1) % len(T.cores)], core))
    calls = []

    def size(ap):
        n = 1
        for k in ap.shape[1:]:
            n *= int(k)
        return n

    def op(q, rd, wr, cost, call):
        calls.append({"q": q, "rd": list(rd), "wr": list(wr), "cost": cost, "late": 0.0, "kind": "op", "call": call})

    def dma(q, rd, wr, out, in_, late=LOCAL):
        calls.append({"q": q, "rd": rd, "wr": wr, "cost": 0.05, "late": late, "kind": "dma", "call": lambda e: e.dma_start(out, in_)})

    def cyc(n):
        return max(64, n) * CYC

    def iota(tok, out, pattern, base, cm, small=True):
        if small:
            op("g", [], [tok], 0.13 + 2 * size(out) * CYC, lambda e: e.iota(out, pattern, base, cm, allow_small_or_imprecise_dtypes=True))
        else:
            op("g", [], [tok], 0.13 + 2 * size(out) * CYC, lambda e: e.iota(out, pattern, base, cm))

    def sel(rd, tok, out, in_, pattern, cmp, fill, base, cm):
        op("g", [rd], [tok], 0.17 + 2 * size(out) * CYC, lambda e: e.affine_select(out, in_, pattern, cmp, fill, base, cm))

    def paint(tok, ap, pattern, base, w):
        sel(tok, tok, ap, ap, pattern, A.not_equal, w, base, -1)

    def vset(toks, out, c, k=0.5):
        op("v", [], toks, cyc(k * size(out)), lambda e: e.memset(out, c))

    def ts(rd, wr, out, in0, s1, s2, op0, op1=None, k=1.0):
        if op1 is None:
            op("v", rd, wr, cyc(k * size(out)), lambda e: e.tensor_scalar(out, in0, s1, None, op0=op0))
        else:
            op("v", rd, wr, cyc(k * size(out)), lambda e: e.tensor_scalar(out, in0, s1, s2, op0=op0, op1=op1))

    def tt(rd, wr, out, a, b, o):
        k = 1 if [t for t in rd if t in BANKS] else 2
        op("v", rd, wr, cyc(k * size(out)), lambda e: e.tensor_tensor(out, a, b, o))

    def cp(rd, wr, out, a):
        op("v", rd, wr, cyc(size(out)), lambda e: e.tensor_copy(out, a))

    def offsets(q, rd, wr, out, a):
        if q == "v":
            cp(rd, wr, out, a)
        else:
            act(rd, wr, out, a, ACT.Copy)

    def runmax(rd, wr, out, reset, a):
        op("v", rd, wr, cyc(size(out)), lambda e: e.tensor_tensor_scan(out, reset, a, 0.0, A.add, A.max))

    def act(rd, wr, out, a, func, bias=0.0, scale=1.0):
        op("s", rd, wr, cyc(size(out)), lambda e: e.activation(out, a, func, bias=bias, scale=scale))

    def sset(toks, out, src, rd, c):
        act([rd], toks, out, src, ACT.Identity, c, 0.0)

    def count(rd, wr, out, a, acc):
        op("s", rd, wr, cyc(size(out)) + 0.02, lambda e: e.activation(out, a, ACT.Copy, scale=65536.0, accum_out=acc))

    def gather(q, rd, wr, out, win, lst, other=None, o=None, bias=None):
        cost = 0.06 + GATHER * size(out) * CYC
        if q == "v" and other is None:
            op(q, rd, wr, cost, lambda e: e.tensor_copy(out, win.indirect(lst)))
        elif q == "v":
            op(q, rd, wr, cost, lambda e: e.tensor_tensor(out, win.indirect(lst), other, o))
        elif bias is None:
            op(q, rd, wr, cost, lambda e: e.activation(out, win.indirect(lst), ACT.Copy))
        else:
            op(q, rd, wr, cost, lambda e: e.activation(out, win.indirect(lst), ACT.Abs, bias=bias, scale=-1.0))

    def scatter(rd, wr, win, lst, a):
        op("v", rd, wr, 0.05 + SCATTER * size(a) * CYC, lambda e: e.tensor_copy(win.indirect(lst), a))

    def mm(rd, bank, out, lhsT, rhs, start, stop, free=False):
        op("p", rd + [bank] * free, [bank] * (not free), max(min(64, size(lhsT)), size(rhs)) * PEC, lambda e: e.matmul(out, lhsT, rhs, start, stop))

    def quad(mat, rd, bank, out, rhs, start=True, stop=True):
        for x in range(4):
            mm([mat] + rd, bank, out(x), T[mat][:, 128 * x:128 * x + 128], rhs(x), start and x == 0, stop and x == 3)

    def col(name, i):
        return T[name][:, i:i + 1]

    def sm(name, a=0, b=8, st=1):
        o = 32 * "L1 L2 H1 H2 H3 W1 W2 W3 D2 D3".split().index(name)
        return T.SM[:, o + a:o + b:st]

    XR, TR = ["XB0", "XB1"], ["TB0", "TB1", "TB2", "TB3"]
    xall, tall = XR + ["XBqD", "XBqR", "XBz", "XBy"], TR + ["TBqD", "TBqR", "TBz", "TBy"]
    XW, TW = T.XB[:, 256:2304], T.TB[:, 256:2304]
    dma("s", [], ["WTS"], T.WTS[:], T.wt[:])
    dma("s", [], ["KKI"], T.KKI[:], T.kk[:])
    dma("s", [], ["XB0"], T.XB[:, 256:1280], T.x0[:, 0:1024], 4.0)
    dma("y", [], ["QS"], T.QS[:], T.qs[:])
    dma("y", [], ["XB1"], T.XB[:, 1280:2304], T.x0[:, 1024:2048], 4.0)
    dma("y", [], ["XBqD", "XBqR", "XBz"], T.XB[:, 0:256], T.qs[:, 0:256])
    dma("y", [], ["XBy"], T.XB[:, 2304:2688], T.qs[:, 0:384])
    dma("y", [], ["OLDqD", "OLDqR"], T.OLD[:, 384:512], T.qs[:, 0:128])
    dma("y", [], ["MX1R"], T.MX1[:, 0:128], T.qs[:, 0:128])
    dma("y", [], ["MX2_0"], T.MX2[:, 0:256], T.qs[:, 0:256])
    dma("y", [], ["MX2_1"], T.MX2[:, 256:512], T.qs[:, 0:256])
    for i in range(len(calls)):
        calls[i]["early"] = 1000.0
        if i % 3 or i > 3:
            calls[i]["behind"] = [i - 1]

    iota("PIN", T.PIN[:], [[0, 1]], 0, 1, False)
    iota("IO4", T.IO4[:, 0:4], [[4, 4]], 0, 0)
    iota("IO4", T.IO4[:, 4:8], [[1, 4]], 0, 0)
    iota("CQ", T.CQ[:], [[4, 32], [0, 4]], 0, 0)
    iota("CA", T.CA[:], [[16, 8], [0, 4], [1, 4]], 0, 0)
    iota("CM", T.CM[:], [[1, 128]], 0, 0)
    iota("IOF", T.IOF[0:64, :], [[1, 512]], 0, 0)
    iota("PX", T.PX[:], [[4, 4]], 0, 1)
    iota("CG", T.CG[:], [[16, 8], [0, 16]], 0, 0)
    iota("CR", T.CR[:], [[0, 8], [1, 16]], 0, 0)
    iota("LN0", T.LN0[:], [[16, 8]], 0, 0)
    vset(["G2_0", "G2_1"], T.G2[:, 0:512], 0.0)
    vset(["MAS"], T.MAS[:], 0.0)
    vset(["ONE"], T.ONE[:], 1.0)
    vset(["IOT1"], T.IOT[64:128, :], 1.0)
    for n, out in (("RQC", T.RQC[:]), ("RK1", T.RK1[:]), ("RK2", T.RK2[:]), ("RP2", T.RP2[:]), ("RQS", T.RQS[:]), ("RQPa", T.RQP[:, 0:16, :]),
                   ("RQPb", T.RQP[:, 16:32, :]), ("ST", T.ST[:]), ("G1R", T.G1[:, 0:128])):
        dma("y", ["G2_0", "G2_1"], [n], out, T.G2[:, 0:size(out)])
    for i, (sh, m) in enumerate(((0, 112), (0, 15), (0, 3), (2, 3))):
        ts(["PIN"], ["PI"], col("PI", i), T.PIN[:], sh, m, A.arith_shift_right, A.bitwise_and)
    cp(["PI"], ["PF"], T.PF[:], T.PI[:, 0:4])
    ts(["IO4", "PF"], ["BX"], T.BX[:], T.IO4[:, 0:4], col("PF", 0), None, A.add)
    ts(["IO4", "PF"], ["EA"], T.EA[:], T.IO4[:, 4:8], col("PF", 2), None, A.is_equal)
    ts(["IO4", "PF"], ["EX"], T.EX[:], T.IO4[:, 4:8], col("PF", 3), None, A.is_equal)
    parts = [(0, 0, 32, 0, 4, 0.0), (64, 0, 32, 0, 4, 0.0), (0, 0, 32, 12, 16, 0.0), (64, 0, 32, 12, 14, 0.0), (0, 0, 32, 4, 8, -16.0),
             (0, 0, 32, 8, 12, 16.0), (64, 0, 32, 14, 15, -16.0), (64, 0, 32, 15, 16, 1.0 / 64)]
    for b in range(4):
        parts += [(64, 8 * b, 8 * b + 8, 4, 8, -16.0 - 8192.0 * b), (64, 8 * b, 8 * b + 8, 8, 12, 8192.0 * b)]
    for p, r0, r1, c0, c1, c in parts:
        sset(["CV"], T.CV[p:p + 64, r0:r1, c0:c1], T.CQ[p:p + 64, 0:(r1 - r0) * (c1 - c0)], "CQ", c)
    cp(["WTS"], ["WTF"], col("KC1", 3), T.WTS[:])
    for x in range(4):
        ts(["CQ", "BX", "WTF"], ["WX"], T.WX[:, 128 * x:128 * x + 128], T.CQ[:], col("BX", x), col("KC1", 3), A.is_equal, A.mult, 0.5)
    cp(["KKI"], ["KF"], T.KF[:], T.KKI[:])
    tt(["KF", "EA"], ["KM"], T.KM[:], T.KF[:], T.EA[:], A.mult)
    op("v", ["KM"], ["K0"], cyc(4), lambda e: e.tensor_reduce(col("KC1", 0), T.KM[:], X, A.add))
    ts(["K0"], ["K1"], col("KC1", 1), col("KC1", 0), 1024.0, -2048.0, A.is_gt, A.mult)
    ts(["K0", "K1"], ["K32"], col("KC1", 2), col("KC1", 0), col("KC1", 1), 32.0, A.add, A.mult)

    def places(rd, src, o, n, q="v"):
        k = "%d" % o
        offsets(q, rd, ["UI" + k], T.UI[:, o:o + n], src)
        ts(["UI" + k], ["U" + k], T.U[:, o:o + n], T.UI[:, o:o + n], 2047, None, A.bitwise_and)
        ts(["U" + k, "K32"], ["Z" + k], T.Z[:, o:o + n], T.U[:, o:o + n], col("KC1", 2), None, A.add)
        tt(["Z" + k, "U" + k], ["Y" + k], T.Y[:, o:o + n], T.Z[:, o:o + n], T.U[:, o:o + n], A.mult)
        ts(["Y" + k], ["P" + k], T.P[:, o:o + n], T.Y[:, o:o + n], 5, 2047, A.arith_shift_right, A.bitwise_and)
        offsets(q, ["P" + k], ["PH" + k], T.PH[:, o:o + n], T.P[:, o:o + n])

    ts(["PF"], ["SC0"], col("SC", 0), col("PF", 0), col("PF", 2), None, A.add)
    ts(["PF"], ["SC10"], col("SC", 10), col("PF", 1), 8.0, 12.0, A.is_ge, A.add)
    ts(["PF"], ["SC2"], col("SC", 2), col("PF", 0), 14.0, None, A.add)
    ts(["PF"], ["SC3"], col("SC", 3), col("PF", 1), 0.0, 4.0, A.is_equal, A.mult)
    ts(["PF", "SC10"], ["SC1"], col("SC", 1), col("SC", 10), col("PF", 0), None, A.add)
    for lo, hi, w in ((0, 4, 1.0), (4, 8, 1024.0), (8, 12, -1024.0)):
        ts(["CA", "SC0", "MAS"], ["MAS%d" % lo], T.MAS[:, :, lo:hi], T.CA[:, :, lo:hi], col("SC", 0), w, A.is_equal, A.mult)
    ts(["CM", "SC1"], ["XT"], T.XT[:], T.CM[:], col("SC", 1), None, A.is_equal, None, 0.5)
    ts(["CM", "SC2", "SC3"], ["XU"], T.XU[:], T.CM[:], col("SC", 2), col("SC", 3), A.is_equal, A.mult, 0.5)
    act(["IOF"], ["IOT0"], T.IOT[0:64, :], T.IOF[0:64, :], ACT.Copy)
    tt(["XT", "XU"], ["XS"], T.XS[:], T.XT[:], T.XU[:], A.add)
    for x in range(4):
        act(["MAS0", "MAS4", "MAS8", "EX"], ["UX"], T.UX[:, 128 * x:128 * x + 128], T.MAS[:], ACT.Identity, 0.0, col("EX", x))
    ts(["PF"], ["SC11"], col("SC", 11), col("PF", 1), 14.0, None, A.is_equal)
    ts(["PF"], ["SC6"], col("SC", 6), col("PF", 1), 15.0, -1024.0, A.is_equal, A.mult)
    ts(["PF"], ["SC13"], col("SC", 13), col("PF", 1), 15.0, None, A.is_equal)
    ts(["EX"], ["SC7"], col("SC", 7), col("EX", 1), -1024.0, None, A.mult)
    ts(["EX"], ["SC12"], col("SC", 12), col("EX", 1), -8192.0, 8192.0, A.mult, A.add)
    ts(["SC11", "EX"], ["SC14"], col("SC", 14), col("SC", 11), col("EX", 2), -7168.0, A.add, A.mult)
    ts(["SC11", "SC13"], ["SC9"], col("SC", 9), col("SC", 11), -1024.0, col("SC", 13), A.mult, A.add)
    ts(["SC14", "SC12"], ["SC8"], col("SC", 8), col("SC", 14), col("SC", 12), None, A.add)
    ts(["EX"], ["SC16"], col("SC", 16), col("EX", 0), col("EX", 3), None, A.add)
    ts(["PF"], ["SC4"], col("SC", 4), col("PF", 1), 4.0, None, A.is_lt)
    ts(["PF"], ["SC5"], col("SC", 5), col("PF", 1), 12.0, None, A.is_ge)
    for x in range(4):
        ts(["CM", "PX", "SC4"], ["LX"], T.LX[:, 128 * x:128 * x + 128], T.CM[:], col("PX", x), col("SC", 4), A.is_equal, A.mult, 0.5)

    for i in range(4):
        iota("RQF", T.RQF[:, 32 * i:32 * i + 32, 0], [[8, 8], [1, 4]], 128 + 64 * (i // 2) + 4 * (i % 2), 0)
        iota("RQF", T.RQF[:, 32 * i:32 * i + 32, 1:5], [[32, 8], [4, 4], [1, 4]], 512 + 256 * (i // 2) + 16 * (i % 2), 0)
    sel("RQF", "RQK", T.RQK[:], T.RQF[:], [[0, 4], [16, 8], [0, 20]], A.is_equal, 0.0, 15, -1)
    iota("RCF", T.RCF[:], [[2, 8], [16, 2], [1, 2]], 32, 0)
    sel("RCF", "RQC", T.RQC[:, 8:12, :], T.RCF[:], [[16, 8], [0, 4]], A.is_equal, 0.0, 15, -1)
    for r in (12, 13):
        paint("RQS", T.RQS[:], [[16, 8], [0, 4]], r, -1024.0)
        paint("RQC", T.RQC[:, 8:12, :], [[16, 8], [0, 4]], r, -1024.0)
        paint("RQC", T.RQC[:, 12, :], [[16, 8]], r, 1.0)
        paint("RK2", T.RK2[:, :, 0], [[16, 8]], r, -1024.0)
    paint("RQC", T.RQC[:, 4:8, :], [[2, 2], [16, 8], [1, 2]], 0, 1.0)
    for h in range(2):
        paint("RQP" + "ab"[h], T.RQP[:, 16 * h + 8:16 * h + 16, :], [[16, 8], [1, 2], [0, 16]], 2 * h, -1.0)
    for r in (4, 8):
        paint("RK1", T.RK1[:], [[16, 8], [1, 4], [0, 5]], r, 16384.0)
        paint("RK2", T.RK2[:, :, 1:5], [[16, 8], [1, 4]], r, 16384.0)
    paint("RK1", T.RK1[:], [[16, 8], [0, 20]], 14, -16384.0)
    paint("RK2", T.RK2[:, :, 1:5], [[16, 8], [0, 4]], 14, -16384.0)
    paint("RP2", T.RP2[:], [[0, 2], [16, 8], [1, 4]], 0, 1.0)
    paint("ST", T.ST[:], [[8, 3], [1, 8], [0, 16]], 0, 1.0)

    quad("WX", ["QS"], "KC", lambda x: T.KC[:, 256:376], lambda x: T.QS[:, x:480:4])
    places(["KC"], T.KC[:, 256:376], 512, 120)
    cp(["P512"], ["L1U"], T.L1U[:], T.P[:, 512:632])
    for j in range(4):
        act(["QS"], ["QR4D0"], T.QR4[:, 128 + j:512:4], T.QS[:, 0:96], ACT.Copy)
    for j in range(4):
        act(["QR4D0"], ["QRD0"], T.QR16[:, 512 + j:2048:4], T.QR4[:, 128:512], ACT.Copy)
    mm(["XS", "QS"], "PC", T.PC[:, 0:60, :], T.XS[:], T.QS[:], True, False)
    quad("UX", ["PH512"], "PC", lambda x: T.PC[:, 0:60, x:8:4], lambda x: T.PH[:, 512:632], False)
    act(["PC", "SC9", "SC16"], ["QT"], T.QT[:], T.PC[:, 0:60, :], ACT.Identity, col("SC", 9), col("SC", 16))
    for s in range(S):
        act(["QT"], ["QTD%d" % s], T.QTH[:, 128 * s + 32:128 * s + 128], T.QT[:, 96 * s:96 * s + 96], ACT.Copy)
    dma("y", ["QT"], ["TBqD", "TBqR", "TBz"], T.TB[:, 0:256], T.QT[:, 0:256])
    dma("y", ["QT"], ["TBy"], T.TB[:, 2304:2688], T.QT[:, 0:384])

    TBANK = ("PA", "PB", "LR", "LD")
    table = len(calls)
    for h in range(2):
        hb = ("LD", "KC")[h]
        quad("WX", [XR[h]], hb, lambda x: T[hb][:, 0:256], lambda x: T.XB[:, 256 + 1024 * h + x:1280 + 1024 * h:4])
        places([hb], T[hb][:, 0:256], 256 * h, 256, "s")
    for c in calls[table:]:
        c["early"] = 5.0
    for c in calls:
        if c["wr"][0] in ("QRD0", "PCz", "PCy", "MS0", "RST", "RS16"):
            c["behind"] = [i for i in range(table, len(calls)) if calls[i]["wr"][0][0:2] == "UI"]
    for b in range(4):
        tb = TBANK[b]
        mm(["CV", "IOT0", "IOT1"], tb, T[tb][:], T.CV[:, 8 * b:8 * b + 8, :], T.IOT[:], True, False)
        mm(["XS", XR[b // 2]], tb, T[tb][:], T.XS[:], T.XB[:, 256 + 512 * b:768 + 512 * b], False, False)
        quad("UX", ["PH%d" % (256 * (b // 2))], tb, lambda x: T[tb][..., x::4], lambda x: T.PH[:, 128 * b:128 * b + 128], False)
        ts([tb, "SC7", "SC8"], [TR[b]], T.TB[:, 256 + 512 * b:768 + 512 * b], T[tb][:], col("SC", 7), col("SC", 8), A.max, A.min)

    ts(["CG", "PF"], ["BD1"], T.BD1[:], T.CG[:, 0:128:16], col("PF", 0), 1024.0, A.is_equal, A.mult)
    ts(["CG", "PF"], ["BDN"], T.BDN[:], T.CG[:, 0:128:16], col("PF", 0), -1024.0, A.is_equal, A.mult)
    ts(["CG", "PF"], ["BD2"], T.BD2[:], T.CG[:, 0:128:16], col("PF", 0), 2048.0, A.is_equal, A.mult)
    sset(["QTR0"], T.QTH[:, 0:32], T.QS[:, 0:32], "QS", 4096.0)
    sset(["PCz", "PC12"], T.PCW[:, 0:256], T.QS[:, 0:256], "QS", -256.0)
    sset(["PCy"], T.PCW[:, 256:512], T.QS[:, 0:256], "QS", -256.0)
    sset(["RST"], T.RST[:], T.QS[:, 0:160], "QS", 0.0)
    sset(["RS16"] + ["CL%d" % h for h in range(1, 8)], T.RS16[:], T.QS[:, 0:128], "QS", 0.0)
    sset(["MS0"], T.MS[:, 0:160], T.QS[:, 0:160], "QS", 0.0)
    sset(["RST"], T.RST[:, 0:160:20], T.RST[:, 0:160:20], "RST", -1e9)
    sset(["RS16"], T.RS16[:, 0:128:16], T.RS16[:, 0:128:16], "RS16", -1e9)
    for i in range(S - 1):
        sset(["SB%d" % i], T.SB[:, 256 * i:256 * i + 32], T.QS[:, 0:32], "QS", 512.0)
    ts(["PIN"], ["PI4"], col("PI", 4), T.PIN[:], 96.0, None, A.add)
    ts(["CM", "PX"], ["IB"], T.IB[:], T.CM[:], col("PX", 0), None, A.is_equal, None, 0.5)
    ts(["CM", "PX"], ["IPEN"], T.IPEN[:], T.CM[:], col("PX", 0), PEN, A.is_equal, A.mult, 0.5)
    ts(["PI4"], ["PI5"], col("PI", 5), col("PI", 4), 127, None, A.bitwise_and)
    ts(["PI5"], ["SC15"], col("SC", 15), col("PI", 5), -256.0, None, A.add)
    for t in range(3):
        ts(["CR", "PF"], ["MASK"], T.MASK[:, 128 * t:128 * t + 128], T.CR[:], col("PF", 1), None, A.is_equal, None, 0.5)
    ts(["PCz", "LN0", "SC15"], ["PCz"], T.PCW[:, 8:16], T.LN0[:], 0.0, col("SC", 15), A.mult, A.add)
    ts(["PCz"], ["PCz"], T.PCW[:, 2:4], T.PCW[:, 8:10], 128.0, None, A.add)
    ts(["PCz", "IO4"], ["PCz"], T.PCW[:, 4:6], T.IO4[:, 4:6], -60000.0, None, A.mult)
    ts(["CG", "PF"], ["BDB"], T.BDB[:], T.CG[:], col("PF", 0), None, A.is_equal, None, 0.5)
    ts(["CG", "PF"], ["HI"], T.HI[:, 0:6], T.CG[:, 32:128:16], col("PF", 0), None, A.is_equal)
    ts(["CG", "PF"], ["HI"], T.HI[:, 6:8], T.CG[:, 0:32:16], col("PF", 0), None, A.is_equal)
    ts(["LN0", "PF"], ["LN"], T.LN[:], T.LN0[:], col("PF", 1), None, A.add)
    sel("BDB", "LTB", T.LTB[:], T.BDB[:], [[1, 128]], A.is_gt, 0.0, 0, -1)
    ts(["CQ", "BX", "SC6"], ["AU"], T.AU[:], T.CQ[:], col("BX", 1), col("SC", 6), A.is_equal, A.mult, 0.5)
    ts(["CM", "PX", "SC5"], ["AT"], T.AT[:], T.CM[:], col("PX", 0), col("SC", 5), A.is_equal, A.mult, 0.5)
    tt(["AU", "UX"], ["AU"], T.AU[:], T.AU[:], T.UX[:, 0:128], A.add)
    tt(["AU", "AT"], ["AM"], T.AM[:], T.AU[:], T.AT[:], A.add)
    ts(["CQ", "BX"], ["BU"], T.BU[:], T.CQ[:], col("BX", 1), -64.0, A.is_equal, A.mult, 0.5)
    ts(["CQ", "BX"], ["BT"], T.BT[:], T.CQ[:], col("BX", 2), 64.0, A.is_equal, A.mult, 0.5)
    tt(["BU", "BT"], ["BM"], T.BM[:], T.BU[:], T.BT[:], A.add)
    for t in range(3):
        act(["LN"], ["TRC"], T.TRC[:, 8 * t:8 * t + 8], T.LN[:], ACT.Identity, 2048.0 + 128 * t)
    act(["LN"], ["TL"], T.TL[:], T.LN[:], ACT.Identity, 128.0)
    sset(["NTL"], T.NTL[:], T.LN[:], "LN", 256.0)
    ts(["CR", "PF", "XS"], ["MKA"], T.XT[:], T.CR[:], col("PF", 1), -48640.0, A.is_ge, A.mult, 0.5)
    act(["MKA"], ["MKB"], T.MKB[:], T.XT[:], ACT.Identity, -2560.0)
    act(["IB"], ["IB5"], T.IB5[:], T.IB[:], ACT.Identity, 0.0, 5120.0)
    act(["IB"], ["NIB"], T.NIB[:], T.IB[:], ACT.Identity, 0.0, -1.0)
    paint("LTB", T.LTB[:], [[1, 128]], 0, -256.0)

    def repeat(rd, t4, t16, src, o4, n):
        for j in range(4):
            sel(rd, t4, T.QR4[:, o4 + j:o4 + 4 * n:4], src, [[0, n]], A.is_equal, 0.0, 0, 0)
        for j in range(4):
            sel(t4, t16, T.QR16[:, 4 * o4 + j:4 * o4 + 16 * n:4], T.QR4[:, o4:o4 + 4 * n], [[0, 4 * n]], A.is_equal, 0.0, 0, 0)

    def blocks(name, lo, hi):
        return ["%s_%d" % (name, k) for k in range(lo // 16, (hi + 15) // 16)]

    def level3(k, tok, mode):
        b, g2 = k // 32, blocks("G2", k, k + 32)
        pb = ("LR", "PB", "PA", "LD")[b]
        gather((G2Q if mode[0] else G2Q0)[b], [tok] + TR, g2, T.G2[:, 16 * k:16 * k + 512], TW, T.OF2[:, k:k + 32])
        out = T[pb][:, 0:4, :] if pb[0] == "P" else T[pb][:, 96:224]
        if mode[b] == "c":
            quad("LX", g2, pb, lambda x: out, lambda x: T.G2[:, 16 * k + x:16 * k + 512:4])
        else:
            for i in range(4):
                quad("LX", g2, pb, lambda x: T[pb][:, i, :] if pb[0] == "P" else T[pb][:, 96 + 32 * i:128 + 32 * i],
                     lambda x: T.G2[:, 16 * k + 4 * i + x:16 * k + 512:16])
        offsets(CVT[1 + b], [pb], ["OF3_%d" % b], T.OF3[:, 4 * k:4 * k + 128], out)

    marks = [len(calls)]
    for s in range(S):
        arrivals = s > 0
        send = s + 1 < S
        at, qd, qr, q0 = "ARR%d" % s, "QRD%d" % s, "QRR%d" % s, 2048 * s
        a0 = 32 * s
        arr = T.ARR[:, a0:a0 + 32]
        QTT = ["QTD%d" % s, "QTR%d" % s]
        qth = T.QTH[:, 128 * s:128 * s + 128]
        first = 0 if arrivals else 32
        mode = MODE if arrivals else MODE0
        if arrivals:
            dma("y", ["QT"], ["TBqD"], T.TB[:, 0:96], T.QT[:, 96 * s:96 * s + 96])
            dma("y", [], ["XBqD"], T.XB[:, 0:96], T.qs[:, 96 * s:96 * s + 96])
            dma("y", [], ["OLDqD"], T.OLD[:, 384:480], T.qs[:, 96 * s:96 * s + 96])
            repeat(at, "QR4R%d" % s, qr, arr, 512 * s, 32)
            dma("y", [at], ["XBqR"], T.XB[:, 96:128], arr)
            dma("y", [at], ["OLDqR"], T.OLD[:, 480:512], arr)
            repeat("QS", "QR4D%d" % s, qd, T.QS[:, 96 * s:96 * s + 96], 512 * s + 128, 96)

        l1 = T.L1U[:, 24 * s:24 * s + 24]
        gather("s", ["L1U"] + TR, ["G1D"], T.G1[:, 128:512], TW, l1)
        quad("LX", ["G1D"], "LD", lambda x: T.LD[:, 0:96], lambda x: T.G1[:, 128 + x:512:4])
        offsets(CVT[0], ["LD"], ["OF2D"], T.OF2[:, 32:128], T.LD[:, 0:96])
        for k in (96, 64, 32):
            level3(k, "OF2D", mode)
        gather("v", ["L1U", "QR4D%d" % s] + XR, ["MX1D"], T.MX1[:, 128:512], XW, l1, T.QR4[:, 512 * s + 128:512 * s + 512], A.max)

        if arrivals:
            quad("WX", [at], "LR", lambda x: T.LR[:, 0:8], lambda x: T.ARR[:, a0 + x:a0 + 32:4])
            places(["LR"], T.LR[:, 0:8], 632, 8)
            cp(["P632"], ["OF1"], T.OF1[:], T.P[:, 632:640])
            gather("s", ["OF1"] + TR, ["G1R"], T.G1[:, 0:128], TW, T.OF1[:])
            mm(["XS", at], "PC", T.PC[:, 32:36, :], T.XS[:], arr, True, False)
            quad("UX", ["PH632"], "PC", lambda x: T.PC[:, 32:36, x:8:4], lambda x: T.PH[:, 632:640], False)
            quad("LX", ["G1R"], "LR", lambda x: T.LR[:, 16:48], lambda x: T.G1[:, x:128:4])
            act(["PC", "SC9", "SC16"], [QTT[1]], T.QTH[:, 128 * s:128 * s + 32], T.PC[:, 32:36, :], ACT.Identity, col("SC", 9), col("SC", 16))
            if send:
                act(["PC", "SC9", "SC16"], ["TBqR"], T.TB[:, 96:128], T.PC[:, 32:36, :], ACT.Identity, col("SC", 9), col("SC", 16))
            offsets(CVT[5], ["LR"], ["OF2R"], T.OF2[:, 0:32], T.LR[:, 16:48])
            level3(0, "OF2R", mode)
            gather("v", ["OF1", "QR4R%d" % s] + XR, ["MX1R"], T.MX1[:, 0:128], XW, T.OF1[:], T.QR4[:, 512 * s:512 * s + 128], A.max)

        for k in range(first, 128, PIECE):
            gather("v", ["OF2R", qr] * (k < 32) + ["OF2D", qd] * (k >= 32) + XR, blocks("MX2", k, k + PIECE), T.MX2[:, 16 * k:16 * (k + PIECE)], XW,
                   T.OF2[:, k:k + PIECE], T.QR16[:, q0 + 16 * k:q0 + 16 * (k + PIECE)], A.max)
        for b in range(first // 32, 4):
            k = 32 * b
            if mode[b] == "c":
                for j in range(k, k + 32):
                    gather("s", ["OF3_%d" % b, "QS" if b else at] + XR, ["DF%d" % (j // 8)], T.DF[:, 64 * j:64 * j + 64], XW,
                           T.OF3[:, 4 * j:4 * j + 4], bias=col("QS", 96 * s + j - 32) if b else col("ARR", a0 + j))
                continue
            for i in range(4):
                o = 1536 * i + 512 * b
                tok, a = ["DF%d" % (4 * b + i)], T.DF[:, o:o + 512]
                if mode[b][i] == "p":
                    raw = T.OCC[:, 512 * i:512 * i + 512]
                    gather("s", ["OF3_%d" % b] + XR, ["OCC%d" % i], raw, XW, T.OF3[:, 4 * k + 32 * i:4 * k + 32 * i + 32])
                    mm(["NIB", qd if b else qr], "LD", T.LD[:], T.NIB[:], T.QR16[:, q0 + 16 * k:q0 + 16 * k + 512], True, False)
                    mm(["IB", "OCC%d" % i], "LD", T.LD[:], T.IB[:], raw, False, True)
                    act(["LD"], tok, a, T.LD[:], ACT.Abs)
                    continue
                n = 16 if arrivals and tok[0] in HALVES else 32
                for h in range(0, 32, n):
                    gather("v", ["OF3_%d" % b, qd if b else qr] + XR, [tok[0] + "ab"[h // 16]] * (n == 16) + tok, T.DF[:, o + 16 * h:o + 16 * (h + n)], XW,
                           T.OF3[:, 4 * k + 32 * i + h:4 * k + 32 * i + h + n], T.QR16[:, q0 + 16 * (k + h):q0 + 16 * (k + h + n)], A.subtract)
                if mode[b][i] == "s":
                    act(tok, tok, a, a, ACT.Abs)
                else:
                    ts(tok, ["RL%d" % (4 * b + i)], T.RL[:, o:o + 512], a, 0.0, 2.0, A.max, A.mult, 0.5)

        G1T, G2T = ["G1D", "G1R"], blocks("G2", 0, 128)

        def rows(i, j, c, p0=0, p1=128):
            if i == 3:
                return T.KC[p0:p1, 5 * j + c:160:20]
            return T[("KA", "KA", "KB")[i]][p0:p1, 32 * (i == 1) + j:32 * (i == 1) + 32:4, c]

        mm(QTT + ["RQC"], "PC", T.PC[:, 0:32, :], qth, T.RQC[:], True, False)
        mm(["ONE", "RQK"], "KA", T.KA[:], T.ONE[:], T.RQK[:, 0:64, :], True, False)
        mm(["ONE", "RQK"], "KB", T.KB[:], T.ONE[:], T.RQK[:, 64:96, :], True, False)
        mm(["ONE", "RQK"], "KC", T.KC[:, 0:160], T.ONE[:], T.RQK[:, 96:128, :], True, False)
        for b, out in (("KA", T.KA[:, 0:32, 0]), ("KA", T.KA[:, 32:64, 0]), ("KB", T.KB[:, :, 0]), ("KC", T.KC[:, 0:160:5])):
            mm(QTT + ["RQS"], b, out, qth, T.RQS[:], False, False, True)
        mm(QTT + ["RQPa"], "PA", T.PA[:], qth, T.RQP[:, 0:16, :], True, False)
        mm(QTT + ["RQPb"], "PB", T.PB[:], qth, T.RQP[:, 16:32, :], True, False)
        for i in range(4):
            r, c = 16 + 8 * (i // 2), 4 * (i % 2)
            mm(G1T + ["RP2"], "PC", T.PC[:, r:r + 8, c:c + 4], T.G1[:, i:512:4], T.RP2[:, 0:8, :], False, False, True)
            mm(G1T + ["RK2"], "PC", T.PC[:, 8:12, i:8:4], T.G1[:, i:512:4], T.RK2[:, :, 0], False, False, True)
        sums = [k for k in range(marks[-1], len(calls)) if "RK2" in calls[k]["rd"]]
        for i in range(4):
            mm(["MX1D", "MX1R", "BD2"], "PC", T.PC[:, 8:12, i:8:4], T.MX1[:, i:512:4], T.BD2[:], False, i == 3, i < 3)
            calls[-1]["behind"] = sums
        act(["PC"], ["PC12"], T.PCW[:, 32:256], T.PC[:, 4:32, :], ACT.Copy)
        for h, pb in enumerate(("PA", "PB")):
            for j in range(8):
                mm(G2T + ["RP2"], pb, T[pb][:, :, 4 * j:4 * j + 4], T.G2[:, 8 * h + j:2048:16], T.RP2[:], False, j == 7, j < 7)
            ts([pb], ["FG%d" % h], T.FG[:, 8 * h:8 * h + 8, :], T[pb][:, 8:16, :], 0.0, None, A.is_equal)
            act([pb], ["PC3" + "ab"[h]], T.PCW[:, 512 + 256 * h:768 + 256 * h], T[pb][:, 0:8, :], ACT.Copy)
        tt(["PC12"], ["L1"], sm("L1", 0, 16), T.PCW[:, 64:96:2], T.PCW[:, 65:96:2], A.min)
        tt(["PC12"], ["H1"], sm("H1", 0, 16), T.PCW[:, 64:96:2], T.PCW[:, 65:96:2], A.max)
        ts(["PC12"], ["MD1"], T.MD[:, 8:16], T.PCW[:, 96:104], 8192.0, DEADKEY, A.is_ge, A.mult)
        tt(["L1"], ["L2"], sm("L2"), sm("L1", 0, 16, 2), sm("L1", 1, 16, 2), A.min)
        tt(["H1"], ["H2"], sm("H2"), sm("H1", 0, 16, 2), sm("H1", 1, 16, 2), A.max)
        ts(["L2"], ["MD0"], T.MD[:, 0:8], sm("L2"), 1024.0, DEADKEY, A.is_lt, A.mult)
        tt(["H2", "MD1"], ["H3"], sm("H3"), sm("H2"), T.MD[:, 8:16], A.max)
        tt(["H3", "MD0"], ["MS0"], T.MS[:, 0:160:20], sm("H3"), T.MD[:, 0:8], A.max)
        for i in range(4):
            b, o = ("KA", "KA", "KB", "KC")[i], 32 * (i == 1)
            h, c = i // 2, 16 * (i % 2)
            fg = ["FG%d" % h, "IPEN"]
            mm(G1T + ["RK1"], b, T.KC[:, 0:160] if i == 3 else T[b][:, o:o + 32, :], T.G1[:, i:512:4], T.RK1[:], False, False, True)
            if i < 3:
                mm(fg, b, T[b][:, o:o + 32, 1:5], T.IPEN[:], T.FG[:, 8 * h:8 * h + 8, c:c + 16], False, False, True)
            for j in range(4):
                g2 = T.G2[:, 4 * i + j:2048:16]
                if i < 3:
                    mm(G2T + ["RK2"], b, T[b][:, o + j:o + 32:4, :], g2, T.RK2[:], False, False, True)
                    continue
                for k in range(5):
                    mm(G2T + ["RK2"], b, rows(i, j, k), g2, T.RK2[:, :, k], False, False, True)
                for k in range(4):
                    mm(fg, b, rows(i, j, 1 + k), T.IPEN[:], T.FG[:, 8:16, 16 + 4 * j + k], False, False, True)
            sums = [k for k in range(marks[-1], len(calls)) if "RK2" in calls[k]["rd"] and b in calls[k]["rd"]]
            for k in range(first // 32, 4):
                for r in range(16):
                    out, o = rows(i, r // 4, 1 + r % 4, 32 * k, 32 * k + 32), 1536 * i + 512 * k
                    if arrivals and k < WIDE[i]:
                        if k == 0:
                            mm(["DF%d" % (4 * j + i) for j in range(WIDE[i])] + ["BD1"], b, rows(i, r // 4, 1 + r % 4, 0, 32 * WIDE[i]),
                               T.DF[:, o + r:o + 512 * WIDE[i]:16], T.BD1[:], False, False, True)
                        continue
                    if mode[k] == "c":
                        mm(["DF%d" % (4 * k + j) for j in range(4)] + ["BD1"], b, out, T.DF[:, 2048 * k + 16 * i + r:2048 * k + 2048:64], T.BD1[:],
                           False, False, True)
                        continue
                    for n, w in (("DF", "BD1"),) if mode[k][i] != "v" else (("DF", "BDN"), ("RL", "BD1")):
                        mm(["%s%d" % (n, 4 * k + i), w], b, out, T[n][:, o + r:o + 512:16], T[w][:], False, False, True)
            for j in range(4):
                last = j == 3 and i != 0
                mm(blocks("MX2", 0, 128) + ["BD2"], b, rows(i, j, 0), T.MX2[:, 4 * i + j:2048:16], T.BD2[:], False, last, not last)
                calls[-1]["behind"] = sums
        for i in range(3):
            b, o = ("KA", "KA", "KB")[i], 32 * (i == 1)
            tt([b, "MS%d" % i], ["MS%d" % (i + 1)], T.MS[:, 160 * i + 160:160 * i + 320], T[b][:, o:o + 32, :], T.MS[:, 160 * i:160 * i + 160], A.max)
        runmax(["MS3", "RST"], ["MS4"], T.MS[:, 640:800], T.RST[:], T.MS[:, 480:640])
        runmax(["KC", "RST"], ["MS5"], T.MS[:, 800:960], T.RST[:], T.KC[:, 0:160])

        tt(["MS4", "MS5"], ["MI"], T.MI[:], T.MS[:, 659:800:20], T.MS[:, 819:960:20], A.max)
        for t in range(3):
            ts(["MI"], ["PO"], T.PO[:, 8 * t:8 * t + 8], T.MI[:], 2 * t, 1023 >> 2 * t, A.arith_shift_right, A.bitwise_and)
        cp(["PO"], ["POU"], T.POU[:], T.PO[:])
        PCT = ["MASK", "PCz", "PCy", "PC12", "PC3a", "PC3b"]
        gather("v", ["POU"] + PCT, ["SELM"], T.SELM[:], T.PCW[:], T.POU[:], T.MASK[:], A.mult)
        for r in range(16):
            mm(["HI", "SELM"], "LR", T.LR[0:24, r:128:16], T.SELM[:, r:384:16], T.HI[:], True, True)
        for t in range(3):
            mm(["HI", "SELM"], "PC", T.PC[:, t, :], T.SELM[:, 128 * t:128 * t + 128], T.HI[:], True, True)
        cp(["LR"], ["TH"], T.TH[0:24, :], T.LR[0:24, 0:128])
        for t in range(3):
            mm(["ST", "TH"], "LD", T.LD[:, 128 * t:128 * t + 128], T.ST[0:24, 128 * t:128 * t + 128], T.TH[0:24, :], True, True)
        ts(["PC"], ["XL"], T.XL[:], T.PC[:, 0:3, :], 256.0, None, A.add)
        ts(["PC"], ["DEAD"], T.DEAD[:], T.PC[:, 0, :], 0.0, 16.0, A.is_lt, A.mult)
        cp(["LD"], ["OTHH"], T.OTHH[:], T.LD[:, 0:384])
        if send:
            ts(["MI"], ["NEU"], T.NEU[:], T.MI[:], 4194304.0, 4.0, A.is_ge, A.add)
            gather("v", ["NEU"] + PCT, ["SELN"], T.SELN[:], T.PCW[:], T.NEU[:], T.MASK[:, 0:128], A.mult)
            mm(["HI", "SELN"], "KB", T.KB[:, 0:8, 0], T.SELN[:], T.HI[:], True, True)
            gather("s", ["XL"] + tall, ["OLDT"], T.OLDT[:], T.TB[:], T.XL[:, 8:24])
            mm(["BM", "OTHH"], "PA", T.PA[:, 0:12, :], T.BM[:], T.OTHH[:], True, False)
            mm(["AM"] + QTT, "PA", T.PA[:, 8:11, :], T.AM[:], T.QTH[:, 128 * s + 32:128 * s + 128], False, False)
            mm(["AM"] + QTT, "PA", T.PA[:, 11, :], T.AM[:], T.QTH[:, 128 * s:128 * s + 32], False, False)
            mm(["AM", "OLDT"], "PA", T.PA[:, 0:8, :], T.AM[:], T.OLDT[:], False, True)
            ts(["PA", "SC7", "SC8"], ["NEWT"], T.NEWT[:], T.PA[:, 0:12, :], col("SC", 7), col("SC", 8), A.max, A.min)
        gather("s", ["XL"] + xall, ["OLD"], T.OLD[:, 0:384], T.XB[:], T.XL[:])

        mm(["IB", "MKB"], "LD", T.LD[:, 384:512], T.IB[:], T.MKB[:], True, False)
        mm(["IB5", "DEAD"], "LD", T.LD[:, 384:512:16], T.IB5[:], T.DEAD[:], False, False)
        for hi in range(8):
            n = 16 * (hi + 1)
            for t in range(3):
                ts(["OTHH", "PC"], ["EQ%d" % hi], T.EQ[:, 24 * t + hi:24 * t + hi + 17:8, 128 - n:128], T.OTHH[:, :, 0:n],
                   T.PC[:, t, hi:hi + 1], None, A.is_equal, None, 0.5)
        for hi in range(1, 8):
            k, cl = 9 * (hi - 1), col("RS16", 16 * hi + 15)
            if hi in ON_PE:
                pb = {7: "LR", 6: "PB", 5: "KC", 4: "KA"}[hi]
                sums = T.PB[:, 0:3, :] if hi == 6 else T.KA[:, :, 0] if hi == 4 else T[pb][:, 128:128 + 16 * hi]
                for j in range(9):
                    mm(["IB", "EQ%d" % hi], pb, sums, T.IB[:], T.EQ[:, 8 * j + hi, 112 - 16 * hi:112], j == 0, j == 8)
                count([pb], ["CL%d" % hi, "JK%d" % hi], T.JK[:, k, 0:16 * hi], sums, cl)
            else:
                count(["EQ%d" % hi], ["CL%d" % hi, "JK%d" % hi], T.JK[:, k:k + 9, 0:16 * hi], T.EQ[:, hi:72:8, 112 - 16 * hi:112], cl)
        for h0 in (4, 0):
            for k in range(9):
                last = h0 == 0 and k == 8
                mm(["IB5"] + ["EQ%d" % h for h in range(h0, h0 + 4)], "LD", T.LD[:, 384 + 16 * h0:448 + 16 * h0], T.IB5[:],
                   T.EQ[:, 8 * k + h0:8 * k + h0 + 4, 112:128], False, last, not last)
        runmax(["LD", "RS16"] + ["CL%d" % h for h in range(1, 8)], ["CFS"], T.CFS[:], T.RS16[:], T.LD[:, 384:512])
        met = T.CFS[:, 15:128:16]
        for t in range(3):
            tt(["CFS", "PC"], ["W2"], sm("W2", 8 * t, 8 * t + 8), T.PC[:, t, :], met, A.max)
        tt(["W2", "TRC"], ["W3"], sm("W3", 0, 24), sm("W2", 0, 24), T.TRC[:], A.min)
        ts(["W3"], ["DLU"], T.DLU[:], sm("W3", 0, 24), 256.0, None, A.add)
        if send:
            tt(["CFS", "KB"], ["ND"], T.ND[:], met, T.KB[:, 0:8, 0], A.is_lt)
            mm(["IB", "NTL"], "KC", T.KC[:, 0:8], T.IB[:], T.NTL[:], True, False)
            mm(["LTB", "ND"], "KC", T.KC[:, 0:8], T.LTB[:], T.ND[:], False, False)
            for d in range(1, 8):
                mm(["BDB", "ND"], "KC", T.KC[:, d:8], T.BDB[:], T.ND[:, 0:8 - d], False, d == 7)
            sb = "SB%d" % s
            tt(["KC", "TL"], ["D3"], sm("D3"), T.KC[:, 0:8], T.TL[:], A.min)
            offsets("s", ["D3"], ["SLU"], T.SLU[:], sm("D3"))
            scatter(["DLU", "NEWT"], tall, T.TB[:], T.DLU[:], T.NEWT[:])
            scatter(["SLU", "OLD"], [sb], T.SB[:, 256 * s:256 * s + 256], T.SLU[:], T.OLD[:, 0:128])
            calls.append({"q": "g", "rd": [sb], "wr": ["ARR%d" % (s + 1)], "cost": 0.5, "late": FAR, "kind": "far", "ev": ("arr%d" % (s + 1), nland, "far"),
                          "call": lambda e, k=s: e.remote_dma(T.ARR[:, 32 * k + 32:32 * k + 64], T.SB[:, 256 * k:256 * k + 32],
                                                              T.sem["arr%d" % (k + 1)], T.sem.sent, pid, rid, wire)})
        scatter(["DLU", "OLD", "OLDqD", "OLDqR"], xall, T.XB[:], T.DLU[:], T.OLD[:, 128:512])
        marks.append(len(calls))
    for s in range(S):
        for q, names in (FIXED if s else FIXED0).items():
            last = None
            for w in names.split():
                k = s - (w[0] == "-")
                if k < 0:
                    continue
                w = w.lstrip("-").replace("#", "%d" % k)
                found = [i for i in range(marks[k], marks[k + 1]) if calls[i]["q"] == q and calls[i]["wr"][0] == w]
                if found and last is not None:
                    calls[found[0]]["behind"] = [last]
                last = found[-1] if found else last
    dma("y", XR, ["y0"], T.y[:, 0:1024], T.XB[:, 256:1280])
    dma("s", XR, ["y1"], T.y[:, 1024:2048], T.XB[:, 1280:2304])
    issue(g, T, calls)
    g.wait_ge(T.sem.sent, nwire * (S - 1))
